import numpy as np, ml_dtypes
CORES = [6,15,38,47]
N = 4
import mx_ref
BF = ml_dtypes.bfloat16
def entries(a):
    return np.ascontiguousarray(a.T).reshape(-1)
def table(e):
    return np.ascontiguousarray(np.reshape(e, (-1, 16)).T).astype(np.int32)
def gentries(a):
    return np.ascontiguousarray(a.reshape(8, 16, -1).transpose(0, 2, 1)).reshape(8, -1)
def gtable(e):
    e = np.asarray(e); return np.ascontiguousarray(e.reshape(8, -1, 16).transpose(0, 2, 1)).reshape(128, -1).astype(np.int32)
def gcols(t, e):
    v = np.concatenate([t.reshape(8, 16, -1, 4), np.zeros((8, 16, 1, 4), BF)], axis=2)
    return np.ascontiguousarray(np.stack([v[g][:, e[g]] for g in range(8)])).reshape(128, -1)
def tile(rs):
    return np.stack(rs, axis=2).reshape(128, -1).astype(BF)
def pick(q, e):
    c = np.concatenate([q[0].reshape(128, -1, 4), np.zeros((128, 1, 4), np.uint8)], axis=1); s = np.concatenate([q[1], np.ones((16, 1), np.uint8)], axis=1)
    return (np.ascontiguousarray(c[:, e].reshape(128, -1)), np.ascontiguousarray(s[:, e]))
def join(*qs):
    return (np.concatenate([q[0] for q in qs], axis=1), np.concatenate([q[1] for q in qs], axis=1))
def put(q, e, v):
    c, s = q[0].reshape(128, -1, 4).copy(), q[1].copy(); c[:, e] = v[0].reshape(128, -1, 4); s[:, e] = v[1]
    return (c.reshape(128, -1), s)
def pk(c, s):
    return (np.ascontiguousarray(c), mx_ref.live(s))
def emit(q):
    return q[0], q[1]
def packed(v, rng):
    q = [mx_ref.quantize(np.ascontiguousarray(v[r])) for r in range(N)]
    return np.stack([a for a, b in q]), np.stack([mx_ref.plane(b, rng) for a, b in q])
def values_of_codes():
    e, c = np.zeros((128, 128, 4), np.float32), np.zeros((128, 2, 4), np.uint8)
    e[np.arange(128), np.arange(128), 0] = 1
    c[:127, :, 0] = np.arange(256).reshape(2, 128).T[:127]
    return mx_ref.matmul(mx_ref.quantize(e.reshape(128, 512).astype(BF)), (c.reshape(128, 8), np.full((16, 2), 127, np.uint8))).T.reshape(-1).astype(np.float64)
CODE_VALUE, SCALE_VALUE = values_of_codes(), 2.0 ** (np.arange(256) - 127.0)
def decode(q):
    return (CODE_VALUE[q[0]].reshape(16, 8, -1, 4) * SCALE_VALUE[q[1]][:, None, :, None] + 0.0).reshape(128, -1).astype(np.float32)
def f(rng, *shape):
    return mx_ref.flush((rng.standard_normal(shape, dtype=np.float32) * np.exp2(rng.integers(-2, 3, shape[:-1] + (1,)))).astype(BF))
def wide(rng, *shape, cols=0):
    v = rng.standard_normal(shape, dtype=np.float32) * np.exp2(rng.integers(-12, 13, shape)).astype(np.float32)
    if cols: v *= np.repeat(np.exp2(rng.integers(-cols, cols + 1, shape[:-2] + (1, shape[-1] // 4))) * (rng.random(shape[:-2] + (1, shape[-1] // 4)) > 0.0625), 4, axis=-1).astype(np.float32)
    return mx_ref.flush(v.astype(BF))
C, L, M, CAP, E = 480, 3, 160, 64, 480
def pairs_of(e, lev):
    r, s = np.arange(N * C) // C, e // C
    return np.where((e < 0) | (s == r), -1, ((np.arange(8)[:, None] * L + lev) * N + r) * N + s)
def big(v):
    v = v.astype(np.float32)
    v[np.abs(v) < np.float32(2.0 ** -16)] = 0
    return v.astype(BF)
def levels(rng):
    return np.concatenate([rng.permutation(np.arange(C) // M) for r in range(N)])
def drawn(rng, lev, far=()):
    e = np.full((2, 8, N * C), -1)
    for k in range(2):
        for g in range(8):
            free = np.ones(N * C, bool)
            deep = g in far
            for l in range(L - 1 if deep else 1, L):
                a = rng.permutation(np.flatnonzero((lev < (1 if deep else l)) & free))[:E]
                e[k, g, rng.permutation(np.flatnonzero(lev == l))[:E]] = a
                free[a] = False
    return e
def fit(rng, e, lev):
    k = pairs_of(e, lev).reshape(-1)
    o = rng.permutation(k.size)
    o = o[np.argsort(k[o], kind="stable")]
    k = k[o]
    v = e.reshape(-1).copy()
    v[o[(k >= 0) & (np.arange(k.size) - np.searchsorted(k, k) >= CAP)]] = -1
    return v.reshape(e.shape)
def inputs(rng, x, e, lev, w, v):
    wc, ws = packed(w, rng)
    vc, vs = packed(v, rng)
    d = {"x": x, "lv": np.stack([table(a) for a in lev.reshape(N, C)])}
    for k in range(2): d["pr%d" % k] = np.stack([gtable(e[k][:, C * r:C * r + C]) for r in range(N)])
    return {**d, "u": np.array(f(rng, N, 128, 512)), "wc": wc, "ws": ws, "vc": vc, "vs": vs}
def still(k=32):
    w = np.zeros((N, 128, 4, 128, 4), np.float32)
    i = np.arange(128)
    for b in range(4): w[:, i, b, i, b] = k
    return w.reshape(N, 128, 2048).astype(BF)
def setup_inputs(rng):
    lev = levels(rng)
    return inputs(rng, big(f(rng, N, 128, 4 * C)), fit(rng, drawn(rng, lev), lev), lev, f(rng, N, 128, 2048), f(rng, N, 128, 2048))
def setup_inputs_same(rng):
    lev = levels(rng)
    o, p = rng.permutation(8), rng.permutation(N)
    e = drawn(rng, lev, o[[3, 7]])
    e[1, o[:4]] = e[0, o[:4]]
    e[0, o[4]] = -1
    e[1, o[5]] = -1
    e[:, o[6]] = -1
    e[:, :, C * p[0]:C * p[0] + C] = -1
    e[e // C == p[1]] = -1
    return inputs(rng, big(f(rng, N, 128, 4 * C)), fit(rng, e, lev), lev, f(rng, N, 128, 2048), f(rng, N, 128, 2048))
def setup_inputs_full(rng):
    lev = levels(rng)
    v, e = lev.reshape(N, C), np.full((2, 8, N * C), -1)
    o, n = rng.permutation(N), N - 1
    m = min(n - 1, 2 * (M // CAP))
    some = rng.permutation(8)
    far, near = some[:2], some[2:4]
    for g in range(8):
        flip, deep = int(rng.integers(2)), g in far
        for k in range(2):
            free = np.ones((N, C), bool)
            for l in range(L - 1 if deep else 1, L):
                may = v == 1 if g in near and l == L - 1 else v < (1 if deep else l)
                pool = [rng.permutation(np.flatnonzero(may[s] & free[s])) for s in range(N)]
                for i in range(N):
                    r, p = o[i], 0
                    to = C * r + rng.permutation(np.flatnonzero(v[r] == l))
                    want = [(o[(i + 1 + a) % n], CAP) for a in range(m) if (a + k + flip) % 2 == 0] if i < n else []
                    rest = M - CAP * len(want)
                    want.append((r, rest if l == L - 1 else rest // 2))
                    for s, c in want:
                        a, pool[s] = pool[s][:c], pool[s][c:]
                        e[k, g, to[p:p + c]] = C * s + a
                        free[s, a] = False
                        p += c
    return inputs(rng, big(f(rng, N, 128, 4 * C)), e, lev, f(rng, N, 128, 2048), f(rng, N, 128, 2048))
def setup_inputs_cancel(rng):
    lev = levels(rng)
    e, x = np.full((2, 8, N * C), -1), np.zeros((8, 16, N * C, 4))
    large = rng.permutation(8) % 2
    for g in range(8):
        v = rng.integers(4, 8, (16, N * C, 4)) * rng.choice([-1.0, 1.0], (16, N * C, 4)) * 2.0 ** -16
        half = []
        for l in range(L):
            p = rng.permutation(np.flatnonzero(lev == l)).reshape(2, -1)
            v[:, p[1]] = -v[:, p[0]]
            if l % 2 == large[g]: v[:, p] = v[:, p] * 2.0 ** 28
            half.append(p[:, :E // 2])
        for l in range(1, L):
            e[0, g, half[l]] = half[l - 1]
            e[1, g, half[l]] = half[l - 1][::-1]
        x[g] = v
    x = np.ascontiguousarray(x.reshape(128, N, 4 * C).transpose(1, 0, 2)).astype(np.float32).astype(BF)
    return inputs(rng, x, fit(rng, e, lev), lev, still(), still())
def setup_inputs_crowd(rng):
    lev = levels(rng)
    e, x = np.full((2, 8, N * C), -1), np.zeros((8, 16, N * C, 4))
    by, h, some = lev.reshape(N, C), CAP // 2, rng.permutation(8)
    for g in range(8):
        v = rng.integers(1, 32, (16, N * C, 4)) * rng.choice([-1.0, 1.0], (16, N * C, 4)) * 2.0 ** -13
        half = [rng.permutation(np.flatnonzero(lev == l)).reshape(2, -1) for l in range(L)]
        v[::8, half[0][0], 0] = 28
        v[::8, half[0][1], 0] = -28
        x[g] = v
        if g in some[L:]:
            for l in range(1, L):
                e[0, g, half[l][:, :E // 2]] = half[l - 1][:, :E // 2]
                e[1, g, half[l][:, :E // 2]] = half[l - 1][::-1, :E // 2]
            continue
        p = rng.permutation(N)
        for k in range(2):
            free = np.ones((N, C), bool)
            for l in range(1, L):
                if g == some[0]:
                    to = C * p[0] + rng.permutation(np.flatnonzero(by[p[0]] == l))
                    for j in range(N - 1):
                        s, t = p[j + 1], to[h * j:h * j + h]
                        a = rng.permutation(np.flatnonzero((by[s] < l) & free[s]))[:t.size]
                        e[k, g, t] = C * s + a
                        free[s, a] = False
                elif g == some[l]:
                    a = C * p[0] + rng.permutation(np.flatnonzero(by[p[0]] < l))
                    for j in range(N - 1):
                        r, t = p[j + 1], a[h * j:h * j + h]
                        e[k, g, C * r + rng.permutation(np.flatnonzero(by[r] == l))[:t.size]] = t
    x = np.ascontiguousarray(x.reshape(128, N, 4 * C).transpose(1, 0, 2)).astype(np.float32).astype(BF)
    return inputs(rng, x, fit(rng, e, lev), lev, still(36), still())
def setup_inputs_spread(rng):
    d = setup_inputs(rng)
    d["x"] = big(wide(rng, N, 128, 4 * C, cols=6))
    return d
def check_inputs(d):
    b = []
    for k in ("x", "u"):
        a = np.abs(d[k].astype(np.float32))
        if not (np.isfinite(a).all() and ((a == 0) | (a >= 2.0 ** -30) & (a <= 2.0 ** 30)).all()): b.append("a value of " + k)
    lev = np.concatenate([entries(a) for a in d["lv"]])
    if not all((np.sum(lev.reshape(N, C) == l, axis=1) == M).all() for l in range(L)): b.append("a number of columns of a level")
    e = np.stack([np.concatenate([gentries(a) for a in d[k]], axis=1) for k in ("pr0", "pr1")]).astype(np.int64)
    ok = (e >= -1) & (e < N * C)
    if not ok.all(): b.append("an entry out of range")
    e = np.where(ok, e, -1)
    if ((e >= 0) & (lev[np.maximum(e, 0)] >= lev)).any(): b.append("a predecessor that isn't of a lower level")
    s = np.sort(e, axis=2)
    if ((s[:, :, 1:] == s[:, :, :-1]) & (s[:, :, 1:] >= 0)).any(): b.append("a number twice in a list of a group")
    if np.bincount(pairs_of(e, np.clip(lev, 0, L - 1)).reshape(-1) + 1)[1:].max(initial=0) > CAP: b.append("too many entries of two ranks in a group and a level")
    return b
def sweep(base, links, lev, steps, layer):
    got = np.zeros((128, 4 * N * C), BF)
    kept, order = [], []
    for l in steps:
        at = np.flatnonzero(lev == l)
        a, b = [gcols(got, e[:, at]).astype(np.float32) for e in links]
        t = (base.reshape(128, -1, 4)[:, at].reshape(128, -1) - (a + b) * np.float32(0.5)).astype(BF)
        q = mx_ref.quantize(np.ascontiguousarray(t))
        made = []
        for r in range(N):
            mine = pick(q, np.arange(M * r, M * r + M))
            made.append(tile([mx_ref.matmul(pick(layer[r], np.arange(128 * i, 128 * i + 128)), mine) * np.float32(0.03125) for i in range(4)]))
        z = mx_ref.quantize(np.ascontiguousarray(np.concatenate(made, axis=1)))
        got.reshape(128, -1, 4)[:, at] = decode(z).astype(BF).reshape(128, -1, 4)
        kept.append(z)
        order.append(at)
    return pick(join(*kept), np.argsort(np.concatenate(order))), got
def reference(x, lv, pr0, pr1, u, wc, ws, vc, vs):
    lev = np.concatenate([entries(lv[r]) for r in range(N)])
    pr = [np.concatenate([gentries(a[r]) for r in range(N)], axis=1) for a in (pr0, pr1)]
    su = []
    for e in pr:
        i = np.full((8, N * C + 1), -1)
        i[np.arange(8)[:, None], e] = np.arange(N * C)
        su.append(i[:, :N * C])
    first = decode(mx_ref.quantize(np.ascontiguousarray(np.concatenate([x[r] for r in range(N)], axis=1))))
    qy, dy = sweep(first, pr, lev, range(L), [pk(wc[r], ws[r]) for r in range(N)])
    qz, dz = sweep(dy.astype(np.float32), su, lev, range(L - 1, -1, -1), [pk(vc[r], vs[r]) for r in range(N)])
    y = np.zeros((N, 128, C), np.float32)
    oc, osc = np.zeros((N, 128, 4 * C), np.uint8), np.zeros((N, 16, C), np.uint8)
    for r in range(N):
        mine = pick(qz, np.arange(C * r, C * r + C))
        y[r] = mx_ref.matmul(mx_ref.quantize(u[r]), mine)
        oc[r], osc[r] = emit(mine)
    return {"y": y, "oc": oc, "osc": osc}

@@ -1,0 +1,634 @@
+from concourse.bass import DstId, RemoteDMATransfer
+from concourse.mybir import dt, AluOpType, ActivationFunctionType
+
+C, M, CAP = 480, 160, 64
+NS = 3 * CAP
+PF, PB_ = 1024, 768
+TABW = 32 + 4 * 512
+Q4, U8, BF, F32, I32, U16 = "float8_e4m3fn_x4", "uint8", "bfloat16", "float32", "int32", "uint16"
+
+
+def _sb(n, d):
+    return ("sbuf", [128, n], d)
+
+
+SCRATCH = {
+    "ps": ("psum", [128, 4096], F32),
+    "xs": _sb(4 * C, BF), "sq": _sb(C, Q4), "ss": _sb(C, U8), "pq": _sb(C, Q4), "pss": _sb(C, U8),
+    "et": _sb(2048, BF), "eq": _sb(512, Q4), "es": _sb(512, U8), "one": _sb(128, F32), "ident": _sb(128, F32),
+    "wq": _sb(512, Q4), "wp": _sb(512, U8), "vq": _sb(512, Q4), "vp": _sb(512, U8),
+    "us": _sb(512, BF), "uq": _sb(128, Q4), "up": _sb(128, U8),
+    "xt": _sb(4 * M, BF), "xq": _sb(M, Q4), "xp": _sb(M, U8), "tl": _sb(4 * M, BF),
+    "yq": _sb(C, Q4), "yp": _sb(C, U8), "zq": _sb(C, Q4), "zp": _sb(C, U8), "oq": _sb(C, Q4), "op": _sb(C, U8),
+    "wf": _sb(4 * PF, BF), "wb": _sb(4 * PB_, BF), "ab": _sb(4 * M, F32), "sm": _sb(4 * M, F32),
+    "st": _sb(4 * NS, BF), "yo": _sb(C, F32),
+    "laq": _sb(3 * M, Q4), "lap": _sb(3 * M, U8),
+    "sbq": _sb(NS, Q4), "sbp": _sb(NS, U8), "lbq": _sb(NS, Q4), "lbp": _sb(NS, U8),
+    "scq": _sb(NS, Q4), "scp": _sb(NS, U8), "lcq": _sb(NS, Q4), "lcp": _sb(NS, U8),
+    "sdq": _sb(NS, Q4), "sdp": _sb(NS, U8), "ldq": _sb(NS, Q4), "ldp": _sb(NS, U8),
+    "pid": _sb(2, I32), "pt": _sb(4, I32), "pf": _sb(4, F32), "io32": _sb(192, F32), "keep": _sb(192, F32),
+    "m32": _sb(96, F32), "m16": _sb(192, F32), "oti": _sb(12, I32), "ot": _sb(12, U16),
+    "io3": _sb(8, F32), "sel": _sb(8, F32), "io16": _sb(64, F32), "dmp": _sb(128, F32), "col": _sb(16, F32),
+    "io1": _sb(NS, F32), "kp": _sb(2 * M, BF), "pb1": _sb(512, BF), "pb2": _sb(512, BF), "k160": _sb(64, F32),
+    "lvl": _sb(16, I32), "rw": _sb(C, I32), "sw": _sb(2 * C, F32), "swt": _sb(2 * C, F32),
+    "ind": _sb(192, F32), "cum": _sb(192, F32), "cuc": _sb(192, F32), "bc": _sb(192, F32), "tr": _sb(192, F32), "sc": _sb(192, F32),
+    "pp": _sb(192, F32), "pd": _sb(192, F32), "tr2": _sb(192, F32), "t5": _sb(64, F32), "t6": _sb(64, F32),
+    "t1": _sb(64, F32), "t2": _sb(64, F32), "t3": _sb(64, F32), "t4": _sb(64, F32),
+    "i1": _sb(64, I32), "i2": _sb(64, I32), "ofs": _sb(32, U16),
+    "tc30": _sb(16, BF), "vu": _sb(16, U16), "pij": _sb(32, U16), "sig": _sb(32, U16),
+    "pri": _sb(64, I32), "si": _sb(64, I32), "s160": _sb(64, F32), "idx": _sb(64, F32),
+    "idc": _sb(64, U16), "id2": _sb(128, U16), "tab": _sb(TABW, BF),
+    "g2a": _sb(4 * M, BF), "g2b": _sb(4 * M, BF), "g2t": _sb(4 * M, BF), "gc": _sb(2 * M, BF),
+    "tca": _sb(64, F32), "ko": _sb(64, F32), "qq": _sb(64, F32),
+    "iw1": _sb(704, BF), "iw2": _sb(704, BF), "iwt": _sb(384, BF), "iof": _sb(64, U16),
+    "rq1": _sb(24, F32), "rq2": _sb(24, F32), "rl1": _sb(24, F32), "rl2": _sb(24, F32),
+    "fr1": _sb(20, U16), "fr2": _sb(20, U16), "br1": _sb(20, U16), "br0": _sb(20, U16),
+    "fs": _sb(48, U16), "bs1": _sb(48, U16), "bs2": _sb(48, U16),
+    "bw": _sb(1792, BF), "bof": _sb(64, U16),
+    "td0": ("dram", [128, 16], BF), "td1": ("dram", [128, 16], BF), "td2": ("dram", [128, 16], BF),
+    "pdr": ("dram", [128, 16], U16),
+}
+SEMAPHORES = ["cv", "cs", "ct", "cg", "dlv", "dx", "drw", "dw", "dv", "du", "dtab", "dpd", "dpij", "dout",
+              "sent", "atab", "aa0", "aa1", "aa2", "ar1", "ar2", "ab_", "ac_", "ad_"]
+
+
+def rank_program(g, core, T, topo):
+    rank = T.rank_of(core)
+    if rank is None:
+        return
+    cores = list(T.cores)
+    add, sub, mul, mx_ = AluOpType.add, AluOpType.subtract, AluOpType.mult, AluOpType.max
+    COPY, IDENT = ActivationFunctionType.Copy, ActivationFunctionType.Identity
+
+    def peers_of(r):
+        def near(s):
+            a, b = topo.chip(cores[r]), topo.chip(cores[s])
+            return 2 if topo.mates(a, b) else (1 if topo.same_plane(a, b) else 0)
+        return sorted([s for s in range(len(cores)) if s != r], key=lambda s: (near(s), s))
+
+    peers = peers_of(rank)
+    slot_at = [peers_of(s).index(rank) for s in peers]
+
+    queues = {"v": g.vector, "s": g.scalar, "t": g.tensor, "g": g, "y": g.sync}
+    csem = {"v": "cv", "s": "cs", "t": "ct", "g": "cg"}
+    total = {}
+    known = {q: {} for q in queues}
+    hist = {}
+
+    def bits(a, b, st):
+        if st == 1:
+            return ((1 << (b - a)) - 1) << a
+        m = 0
+        for i in range(a, b, st):
+            m |= 1 << i
+        return m
+
+    def V(name, a=0, b=None, st=1, p=(0, 128, 1)):
+        if b is None:
+            b = SCRATCH[name][1][1]
+        t = T[name]
+        ap = t[p[0]:p[1]:p[2], a:b:st] if (st != 1 or p[2] != 1) else t[p[0]:p[1], a:b]
+        cm = bits(a, b, st)
+        if name == "ps":
+            cm = bits(512 * (a // 512), 512 * ((b - 1) // 512 + 1), 1)
+        return (ap, name, bits(p[0], p[1], p[2]), cm)
+
+    def need(q, tok):
+        sem, cnt, snap = tok
+        if cnt is None:
+            cnt = total[sem]
+        k = known[q]
+        if k.get(sem, 0) >= cnt:
+            return
+        queues[q].wait_ge(T.sem[sem], cnt)
+        k[sem] = cnt
+        for s_, c_ in snap.items():
+            if k.get(s_, 0) < c_:
+                k[s_] = c_
+
+    def order(q, reads, writes):
+        toks = {}
+        for views, w in ((reads, False), (writes, True)):
+            for (_, name, pm, cm) in views:
+                for (tok, pm2, cm2, w2) in hist.get(name, []):
+                    if (w or w2 or name == "ps") and (pm & pm2) and (cm & cm2):
+                        old = toks.get(tok[0])
+                        if old is None or tok[1] is None or (old[1] is not None and old[1] < tok[1]):
+                            toks[tok[0]] = tok
+        for tok in toks.values():
+            need(q, tok)
+
+    def note(tok, reads, writes):
+        for views, w in ((reads, False), (writes, True)):
+            for (_, name, pm, cm) in views:
+                hist.setdefault(name, []).append((tok, pm, cm, w))
+
+    def op(q, fn, reads, writes):
+        order(q, reads, writes)
+        sem = csem[q]
+        fn().then_inc(T.sem[sem], 1)
+        total[sem] = total.get(sem, 0) + 1
+        note((sem, total[sem], dict(known[q])), reads, writes)
+
+    def dma(q, sem, out, in_, reads, writes):
+        order(q, reads, writes)
+        queues[q].dma_start(out, in_).then_inc(T.sem[sem], 16)
+        total[sem] = total.get(sem, 0) + 16
+        note((sem, None, dict(known[q])), reads, writes)
+
+    def landed(sem, n, views):
+        total[sem] = total.get(sem, 0) + n
+        note((sem, None, {}), [], views)
+
+    def cp(o, i):
+        op("v", lambda: g.vector.tensor_copy(o[0], i[0]), [i], [o])
+
+    def fill(o, c):
+        op("v", lambda: g.vector.memset(o[0], c), [], [o])
+
+    def tt(o, a, b, f):
+        op("v", lambda: g.vector.tensor_tensor(o[0], a[0], b[0], f), [a, b], [o])
+
+    def ts(o, a, s1, f1, s2=None, f2=None):
+        rd = [a] + [s for s in (s1, s2) if isinstance(s, tuple)]
+        x1 = s1[0] if isinstance(s1, tuple) else s1
+        x2 = s2[0] if isinstance(s2, tuple) else s2
+        if f2 is None:
+            op("v", lambda: g.vector.tensor_scalar(o[0], a[0], x1, None, f1), rd, [o])
+        else:
+            op("v", lambda: g.vector.tensor_scalar(o[0], a[0], x1, x2, f1, f2), rd, [o])
+
+    def ttg(o, w, off, b, f):
+        op("v", lambda: g.vector.tensor_tensor(o[0], w[0].indirect(off[0]), b[0], f), [w, off, b], [o])
+
+    def gat(q, o, w, off):
+        if q == "v":
+            op("v", lambda: g.vector.tensor_copy(o[0], w[0].indirect(off[0])), [w, off], [o])
+        else:
+            op("s", lambda: g.scalar.activation(o[0], w[0].indirect(off[0]), COPY), [w, off], [o])
+
+    def sca(w, off, i):
+        op("v", lambda: g.vector.tensor_copy(w[0].indirect(off[0]), i[0]), [i, off], [w])
+
+    def scan(o, d, n):
+        k = V("keep", 0, n)
+        op("v", lambda: g.vector.tensor_tensor_scan(o[0], k[0], d[0], 0.0, mul, add), [k, d], [o])
+
+    def trn(o, i):
+        op("v", lambda: g.vector.transpose(o[0], i[0]), [i], [o])
+
+    def act(o, i, scale=1.0, bias=None, f=None):
+        rd = [i] + [s for s in (scale, bias) if isinstance(s, tuple)]
+        sc_ = scale[0] if isinstance(scale, tuple) else scale
+        if bias is None:
+            f = f or (IDENT if isinstance(scale, tuple) else COPY)
+            op("s", lambda: g.scalar.activation(o[0], i[0], f, scale=sc_), rd, [o])
+        else:
+            b_ = bias[0] if isinstance(bias, tuple) else bias
+            op("s", lambda: g.scalar.activation(o[0], i[0], f or IDENT, bias=b_, scale=sc_), rd, [o])
+
+    def scaled(q, o, i, c):
+        if q == "s":
+            act(o, i, c)
+        elif c == 1.0:
+            cp(o, i)
+        else:
+            ts(o, i, c, mul)
+
+    def iota(o, pat, base, cm, fl=True):
+        if fl:
+            op("g", lambda: g.iota(o[0], pat, base, cm, allow_small_or_imprecise_dtypes=True), [], [o])
+        else:
+            op("g", lambda: g.iota(o[0], pat, base, cm), [], [o])
+
+    def quant(qn, pn, a, n, i):
+        o, s_ = V(qn, a, a + n), V(pn, a, a + n)
+        op("v", lambda: g.vector.quantize_mx(o[0], s_[0], i[0]), [i], [o, s_])
+
+    def mm(bank, lq, lp, b, rq, rp, a, n):
+        o, l1, l2 = V("ps", 512 * bank, 512 * bank + n), V(lq, 128 * b, 128 * b + 128), V(lp, 128 * b, 128 * b + 128)
+        r1, r2 = V(rq, a, a + n), V(rp, a, a + n)
+        op("t", lambda: g.tensor.matmul_mx(o[0], l1[0], l2[0], r1[0], r2[0], True, True), [l1, l2, r1, r2], [o])
+
+    def four(bank0, lq, lp, rq, rp, a, n):
+        for b in range(4):
+            mm(bank0 + b, lq, lp, b, rq, rp, a, n)
+
+    def pick(oq, op_, sq_, sp_, n, off, a, k):
+        o, w, f = V(oq, a, a + k), V(sq_, 0, n), V(off, a // 16, (a + k) // 16)
+        op("v", lambda: g.vector.tensor_copy(o[0].bitcast(dt.uint32), w[0].bitcast(dt.uint32).indirect(f[0])), [w, f], [o])
+        gat("s", V(op_, a, a + k), V(sp_, 0, n), f)
+
+    eng = topo.engines(core, cores[peers[0]])
+    for s in peers:
+        eng = [e for e in eng if e in topo.engines(core, cores[s])]
+    h = len(eng) // 4
+
+    def emask(es):
+        m = 0
+        for e in es:
+            m |= 1 << e
+        return m
+
+    def fused(sem, pairs, masks):
+        order("g", [p[0] for p in pairs], [])
+        trs = []
+        for e in range(3):
+            rid, pid, _ = topo.addr(cores[peers[e]])
+            trs.append(RemoteDMATransfer(dst_ids=[DstId(rid=rid, pnc=pid)], dma_engine_mask=emask(masks[e]),
+                                         remote_sem=T.sem[sem], src=pairs[e][1], dst=pairs[e][2]))
+        g.remote_dma_fused(trs, local_sem=T.sem.sent)
+        total["sent"] = total.get("sent", 0) + len(eng)
+
+    first = [eng[0:2 * h], eng[2 * h:3 * h], eng[3 * h:4 * h]]
+    second = [eng[2 * h:4 * h], eng[0:h], eng[h:2 * h]]
+
+    def send_packed(sem, sq_, sp_, lq, lp):
+        pc, pz = [], []
+        for e in range(3):
+            a, b = CAP * e, CAP * slot_at[e]
+            v = V(sq_, a, a + CAP)
+            pc.append((v, v[0].bitcast(dt.uint8), T[lq][:, b:b + CAP].bitcast(dt.uint8)))
+            v = V(sp_, a, a + CAP)
+            pz.append((v, v[0], T[lp][:, b:b + CAP]))
+        fused(sem, pc, first)
+        fused(sem, pz, second)
+        landed(sem, 2 * len(eng), [V(lq), V(lp)])
+
+    fill(V("lvl"), 2)
+    fill(V("one"), 1.0)
+    for a in range(4):
+        o = V("lvl", p=(32 * a, 32 * a + 30, 1))
+        dma("y" if a % 2 == 0 else "s", "dlv", o[0], T.lv[:], [], [o])
+    dma("y", "dx", T.xs[:], T.x[:], [], [V("xs")])
+    fill(V("et"), 0.0)
+    iota(V("pid"), [[0, 2]], 0, 1, False)
+    op("g", lambda: g.affine_select(T.ident[:], T.one[:], [[-1, 128]], AluOpType.is_equal, 0.0, 0, 1), [V("one")], [V("ident")])
+    iota(V("io32"), [[0, 6], [1, 32]], 0, 0)
+    iota(V("oti"), [[32, 6], [0, 2]], 31, 0, False)
+    iota(V("io3"), [[16, 2], [1, 4]], 0, 0)
+    iota(V("rw"), [[1, 16], [16, 30]], 0, 0, False)
+    for k, src in ((1, T.pr0), (2, T.pr1)):
+        o = V("rw", p=(k, 128, 16))
+        dma("y", "drw", o[0], src[:], [], [o])
+    dma("y", "dw", T.wq[:].bitcast(dt.uint8), T.wc[:], [], [V("wq")])
+    dma("y", "dw", T.wp[:], T.ws[:], [], [V("wp")])
+    dma("y", "dv", T.vq[:].bitcast(dt.uint8), T.vc[:], [], [V("vq")])
+    dma("y", "dv", T.vp[:], T.vs[:], [], [V("vp")])
+    for b in range(4):
+        act(V("et", 513 * b, 512 * b + 512, 4), V("ident"))
+    act(V("keep"), V("io32"), f=ActivationFunctionType.Sign)
+    fill(V("ind", 0, 96), 0.0)
+    ts(V("pt", 0, 1), V("pid", 0, 1), 31, AluOpType.bitwise_and)
+    ts(V("pt", 1, 2), V("pid", 0, 1), 15, AluOpType.bitwise_and)
+    ts(V("pt", 2, 3), V("pid", 0, 1), 16, AluOpType.bitwise_and)
+    cp(V("ot"), V("oti"))
+    cp(V("pf", 0, 3), V("pt", 0, 3))
+    ts(V("m32"), V("io32", 0, 96), V("pf", 0, 1), AluOpType.is_gt)
+    ts(V("sel", 0, 4), V("io3", 0, 4), V("pf", 1, 2), AluOpType.is_equal)
+    ts(V("sel", 4, 6), V("io3", 0, 8, 4), V("pf", 2, 3), AluOpType.is_equal)
+    quant("eq", "es", 0, 512, V("et"))
+    act(V("sw"), V("et", 0, 960), 0.0)
+    act(V("tab", 0, 2048), V("et"), 0.0)
+    act(V("tab", 2048, TABW), V("et", 0, TABW - 2048), 0.0)
+    iota(V("io16"), [[0, 2], [16, 32]], 0, 0)
+    iota(V("io1"), [[1, NS]], 1, 0)
+    for a in (0, 32):
+        iota(V("k160", a, a + 20), [[M, 2], [0, 10]], -1001, 0)
+    act(V("col", 0, 1), V("pf", 2, 3), -0.5, -8.0)
+    act(V("col", 1, 2), V("pf", 2, 3), 0.5, 7.5)
+    act(V("col", 2, 3), V("pf", 0, 1), -0.5, V("col", 0, 1))
+    act(V("col", 3, 4), V("pf", 0, 1), -0.5, V("col", 1, 2))
+    act(V("col", 8, 9), V("pf", 1, 2), 1.0, 384.0)
+    act(V("col", 9, 10), V("pf", 1, 2), 1.0, 1280.0)
+    act(V("cuc"), V("io32"), 1.0, V("col", 2, 3), ActivationFunctionType.Abs)
+    act(V("dmp", 0, 64), V("io16"), 1.0, V("col", 8, 9))
+    act(V("tr2"), V("cuc"), -1.0, V("col", 3, 4), ActivationFunctionType.Sign)
+    act(V("dmp", 64, 128), V("io16"), 1.0, V("col", 9, 10))
+    act(V("m16"), V("tr2"), f=ActivationFunctionType.Relu)
+    act(V("iw2", 0, 384), V("et", 0, 384), 0.0)
+    act(V("kp", 0, M), V("io1", 0, M), V("sel", 1, 2))
+    act(V("kp", M, 2 * M), V("io1", 0, M), V("sel", 1, 2), V("sel", 2, 3))
+
+    def ranks_in_class(mask, n):
+        def W(name):
+            return V(name, 0, n)
+        scan(W("cum"), W("ind"), n)
+        ttg(W("bc"), W("cum"), V("ot", 0, n // 16), W(mask), mul)
+        if n > 96:
+            for e in range(3):
+                act(V("cuc", 64 * e, 64 * e + 64), V("cum", 64 * e, 64 * e + 64), 1.0, float(CAP * e))
+        trn(W("tr"), W("bc"))
+        scan(W("sc"), W("tr"), n)
+        ttg(W("pp"), W("sc"), V("ot", 0, n // 16), W("cuc" if n > 96 else "cum"), add)
+        tt(W("pd"), W("pp"), W("ind"), mul)
+
+    for l in range(3):
+        ts(V("ind", 32 * l, 32 * l + 16), V("lvl"), l, AluOpType.is_equal)
+    ts(V("t3", 0, 16), V("lvl"), M, mul, -1, add)
+    ranks_in_class("m32", 96)
+    tt(V("t1", 0, 16), V("pd", 0, 16), V("pd", 32, 48), add)
+    tt(V("t2", 0, 16), V("pd", 64, 80), V("t3", 0, 16), add)
+    tt(V("tc30"), V("pd", 0, 16), V("pd", 32, 48), sub)
+    tt(V("i1", 0, 16), V("t1", 0, 16), V("t2", 0, 16), add)
+    v = V("tc30")
+    fused("atab", [(v, v[0], T["td%d" % slot_at[e]][:]) for e in range(3)], first)
+    for p0 in (0, 16):
+        o = V("tab", 32 + 512 * rank, 32 + 512 * rank + 512, p=(p0, 128, 32))
+        dma("y", "dtab", o[0], v[0], [v], [o])
+    ts(V("i2", 0, 16), V("i1", 0, 16), 496, AluOpType.bitwise_and)
+    ts(V("i1", 16, 32), V("i1", 0, 16), 16, add)
+    tt(V("t4", 0, 16), V("i1", 0, 16), V("i2", 0, 16), add)
+    tt(V("t4", 16, 32), V("i1", 16, 32), V("i2", 0, 16), add)
+    trn(V("t4", 32, 64), V("t4", 0, 32))
+    cp(V("vu"), V("i1", 0, 16))
+    cp(V("ofs"), V("t4", 32, 64))
+    quant("sq", "ss", 0, C, V("xs"))
+    sca(V("sw"), V("ofs", 0, 30), V("rw"))
+    dma("y", "dpd", T.pdr[:], T.vu[:], [V("vu")], [V("pdr")])
+    landed("atab", len(eng), [V("td0"), V("td1"), V("td2")])
+    for e in range(3):
+        for p0 in (0, 16):
+            a = 32 + 512 * peers[e]
+            o = V("tab", a, a + 512, p=(p0, 128, 32))
+            dma("y", "dtab", o[0], T["td%d" % e][:], [V("td%d" % e)], [o])
+    trn(V("swt", 0, 320), V("sw", 0, 320))
+    tt(V("t1", 0, 10), V("swt", 0, 320, 32), V("swt", 16, 320, 32), add)
+    cp(V("sig", 0, 10), V("t1", 0, 10))
+    pick("pq", "pss", "sq", "ss", C, "sig", 0, M)
+
+    def evac(bank0, tile, c, who="vsvs"):
+        for b in range(4):
+            scaled(who[b], V(tile, b, 4 * M, 4), V("ps", 512 * (bank0 + b), 512 * (bank0 + b) + M), c)
+
+    def to_window(win, pitch, a, n, who):
+        for b in range(4):
+            if who[b] != "-":
+                scaled(who[b], V(win, pitch * b + a, pitch * b + a + n), V("ps", 512 * b, 512 * b + n), -0.5)
+
+    def places():
+        for l in (1, 2):
+            for k in (0, 1):
+                a = 32 * (l - 1) + 10 * k
+                tt(V("pri", a, a + 10), V("swt", 320 * l + 1 + k, 320 * l + 320, 32), V("swt", 320 * l + 17 + k, 320 * l + 320, 32), add)
+        tt(V("t2", 0, 20), V("swt", 320, 960, 32), V("swt", 336, 960, 32), add)
+        ts(V("idx"), V("pri"), -(C - 1) / 2.0, add, 1.0 / C, mul)
+        ts(V("i1"), V("pri"), 15, AluOpType.bitwise_and)
+        ts(V("i2"), V("pri"), 4, AluOpType.arith_shift_right)
+        cp(V("si"), V("idx"))
+        ts(V("t1"), V("i1"), 30, mul, 32, add)
+        cp(V("sig", 10, 30), V("t2", 0, 20))
+        ts(V("t3"), V("si"), 512 - 30, mul)
+        tt(V("t4"), V("t1"), V("i2"), add)
+        for e in range(3):
+            ts(V("ind", 64 * e, 64 * e + 64), V("si"), peers[e], AluOpType.is_equal)
+        tt(V("idx"), V("t3"), V("t4"), add)
+        pick("pq", "pss", "sq", "ss", C, "sig", M, M)
+        ts(V("id2", 0, 128, 2), V("idx"), 0.0, mx_, V("sel", 4, 5), mul)
+        ts(V("id2", 1, 128, 2), V("idx"), 0.0, mx_, V("sel", 5, 6), mul)
+        cp(V("idc"), V("idx"))
+
+    four(4, "eq", "es", "pq", "pss", 0, M)
+    trn(V("swt", 320, 640), V("sw", 320, 640))
+    evac(4, "xt", 1.0, "svsv")
+    fill(V("pri"), -1)
+    quant("xq", "xp", 0, M, V("xt"))
+    four(0, "wq", "wp", "xq", "xp", 0, M)
+    trn(V("swt", 640, 960), V("sw", 640, 960))
+    evac(0, "tl", 0.03125, "svsv")
+    fill(V("wf", 0, 4 * PF, PF), 0.0)
+    quant("yq", "yp", 0, M, V("tl"))
+    for e in range(3):
+        rid, pid, _ = topo.addr(cores[peers[e]])
+        b = M * slot_at[e]
+        sem = "aa%d" % slot_at[e]
+        order("g", [V("yq", 0, M), V("yp", 0, M)], [])
+        g.remote_dma(T.laq[:, b:b + M].bitcast(dt.uint8), T.yq[:, 0:M].bitcast(dt.uint8), T.sem[sem], T.sem.sent, pid, rid, emask(eng))
+        g.remote_dma(T.lap[:, b:b + M], T.yp[:, 0:M], T.sem[sem], T.sem.sent, pid, rid, emask(eng))
+        total["sent"] += 2 * len(eng)
+        landed("aa%d" % e, 2 * len(eng), [V("laq", M * e, M * e + M), V("lap", M * e, M * e + M)])
+    four(0, "eq", "es", "yq", "yp", 0, M)
+    to_window("wf", PF, 1 + M * rank, M, "ssss")
+    places()
+    four(4, "eq", "es", "pq", "pss", M, M)
+
+    def scatter_places(out, high, dump):
+        ts(V("i2"), V("i1"), high, AluOpType.bitwise_and)
+        ts(V("t1"), V("i1"), V("pf", 2, 3), add)
+        tt(V("t2"), V("t1"), V("i2"), add)
+        tt(V("t1"), V("t2"), dump, AluOpType.min)
+        cp(V(out), V("t1"))
+
+    def slots():
+        ranks_in_class("m16", 192)
+        gat("s", V("g2a"), V("tab"), V("id2", 0, 40))
+        tt(V("t1"), V("pd", 0, 64), V("pd", 64, 128), add)
+        ts(V("s160"), V("si"), M, mul)
+        tt(V("qq"), V("t1"), V("pd", 128, 192), add)
+        ts(V("i1"), V("qq"), -1.0, add)
+        scatter_places("iof", 1008, V("dmp", 0, 64))
+
+    def four_lists(name, src, c1, c2):
+        ts(V("t4", 0, 12), src, c1, mul, c2, add)
+        for b in range(4):
+            ts(V(name, 12 * b, 12 * b + 12), V("t4", 0, 12), 0.0, mx_, float(b), add)
+
+    def codes_of(l):
+        trn(V("g2t"), V("g2a" if l == 1 else "g2b"))
+        yield
+        tt(V("tca", 32 * l - 32, 32 * l - 12), V("g2t", 0, 640, 32), V("g2t", 16, 640, 32), add)
+        yield
+
+    def requests(l):
+        iw, rq, rl, a = "iw%d" % l, "rq%d" % l, "rl%d" % l, 32 * (l - 1)
+        ttg(V("gc"), V("tab"), V("idc", a, a + 20), V("kp"), add)
+        yield
+        sca(V(iw), V("iof", a, a + 20), V("gc"))
+        yield
+        trn(V("iwt"), V(iw, 0, 384))
+        yield
+        tt(V(rq, 0, 24, 2), V("iwt", 0, 384, 32), V("iwt", 16, 384, 32), add)
+        tt(V(rq, 1, 24, 2), V("iwt", 2, 384, 32), V("iwt", 18, 384, 32), add)
+        tt(V("t5", a, a + 12), V("iwt", 1, 384, 32), V("iwt", 17, 384, 32), add)
+        prs = []
+        for e in range(3):
+            v_ = V(rq, 8 * e, 8 * e + 8)
+            prs.append((v_, v_[0], T[rl][:, 8 * slot_at[e]:8 * slot_at[e] + 8]))
+        fused("ar%d" % l, prs, first)
+        landed("ar%d" % l, len(eng), [V(rl)])
+        yield
+
+    def front2():
+        ts(V("t6", 0, 20), V("qq", 32, 52), 0.0, AluOpType.is_gt, float(5 * M), mul)
+        for _ in codes_of(2):
+            yield
+        tc = V("tca", 32, 52)
+        tt(V("t6", 32, 52), V("t6", 0, 20), V("qq", 32, 52), add)
+        ts(V("t3", 0, 20), tc, -1.0, mul, float(4 * M), add)
+        ts(V("t3", 32, 52), tc, 0.0, AluOpType.is_lt)
+        tt(V("t2", 0, 20), tc, V("s160", 32, 52), add)
+        yield
+        tt(V("t6", 0, 20), V("t3", 0, 20), V("t6", 32, 52), mx_)
+        yield
+        tt(V("t3", 0, 20), V("t6", 0, 20), V("t3", 32, 52), mul)
+        yield
+        tt(V("t6", 0, 20), V("t3", 0, 20), V("t2", 0, 20), mx_)
+        yield
+        cp(V("fr2"), V("t6", 0, 20))
+        yield
+
+    def weave(*gens):
+        gens = list(gens)
+        while gens:
+            for x in list(gens):
+                if next(x, 1) == 1:
+                    gens.remove(x)
+
+    def successor_places():
+        for l in (1, 2):
+            a, rl = 32 * l - 12, "rl%d" % l
+            cp(V("tca", a, a + 12), V(rl, 0, 24, 2))
+            ts(V("k160", a, a + 12), V(rl, 1, 24, 2), M, mul, -1.0, add)
+        ts(V("ko"), V("si"), rank, AluOpType.is_equal, 1000.0, mul)
+        ts(V("t1"), V("tca"), -2.0, mul, 2.0 * M, add)
+        ts(V("t2"), V("tca"), 0.0, AluOpType.is_lt)
+        tt(V("t4"), V("tca"), V("k160"), add)
+        tt(V("t3"), V("t1"), V("t2"), mul)
+        tt(V("t6"), V("t4"), V("ko"), add)
+        tt(V("i1"), V("t3"), V("t6"), add)
+        scatter_places("bof", 4080, V("dmp", 64, 128))
+
+    def successors(l, out):
+        sca(V("bw"), V("bof", 32 * l - 32, 32 * l), V("pb%d" % l))
+        a = 640 * (l - 1)
+        trn(V("g2t"), V("bw", a, a + 640))
+        tt(V("t1", 0, 20), V("g2t", 0, 640, 32), V("g2t", 16, 640, 32), add)
+        tt(V("t2", 0, 20), V("g2t", 1, 640, 32), V("g2t", 17, 640, 32), add)
+        tt(V("t3", 0, 20), V("t1", 0, 20), V("t2", 0, 20), add)
+        cp(V(out), V("t3", 0, 20))
+
+    def payload(name, own, far):
+        for a, n, c in ((0, M, own), (M, M, own), (2 * M, NS, far)):
+            if c is None:
+                act(V(name, a, a + n), V("io1", 0, n), V("sel", 0, 1))
+            else:
+                act(V(name, a, a + n), V("io1", 0, n), V("sel", 0, 1), c)
+
+    def make(win, pitch, wn, a, n, lst, lq, lp, between=None):
+        def w(b):
+            return V(win, pitch * b, pitch * b + wn)
+
+        def ga(b, q):
+            gat(q, V("ab", M * b, M * b + M), w(b), V(lst, 0, 10))
+
+        def gb(b):
+            ttg(V("sm", M * b, M * b + M), w(b), V(lst, 10, 20), V("ab", M * b, M * b + M), add)
+
+        def fin(b):
+            tt(V("xt", b, 4 * M, 4), V("ps", 512 * (4 + b), 512 * (4 + b) + M), V("sm", M * b, M * b + M), add)
+        to_window(win, pitch, a, n, "vs--")
+        ga(0, "v")
+        ga(1, "s")
+        to_window(win, pitch, a, n, "--s-")
+        ga(2, "s")
+        to_window(win, pitch, a, n, "---s")
+        ga(3, "s")
+        gb(0)
+        gb(1)
+        fin(0)
+        gb(2)
+        fin(1)
+        fin(2)
+        gb(3)
+        fin(3)
+        layer(lq, lp, between)
+
+    def layer(lq, lp, between=None):
+        quant("xq", "xp", 0, M, V("xt"))
+        four(0, lq, lp, "xq", "xp", 0, M)
+        if between:
+            between()
+        evac(0, "tl", 0.03125, "vsvs")
+
+    def pack(lst, sem, sq_, sp_, lq, lp):
+        for b in range(4):
+            gat("vsvs"[b], V("st", b, 4 * NS, 4), V("tl"), V(lst, 12 * b, 12 * b + 12))
+        quant(sq_, sp_, 0, NS, V("st"))
+        send_packed(sem, sq_, sp_, lq, lp)
+
+    slots()
+    weave(requests(2), codes_of(1))
+    tt(V("t1", 0, 20), V("tca", 0, 20), V("s160", 0, 20), add)
+    cp(V("fr1"), V("t1", 0, 20))
+    for e in range(2):
+        four(0, "eq", "es", "laq", "lap", M * e, M)
+        to_window("wf", PF, 1 + M * peers[e], M, "ssss")
+        if e == 0:
+            gat("s", V("g2b"), V("tab"), V("id2", 64, 104))
+    four(0, "eq", "es", "laq", "lap", 2 * M, M)
+    make("wf", PF, 1 + 4 * M, 1 + M * peers[2], M, "fr1", "wq", "wp",
+         lambda: four_lists("fs", V("rl2", 0, 24, 2), -4.0, -4.0))
+    pack("fs", "ab_", "sbq", "sbp", "lbq", "lbp")
+
+    quant("yq", "yp", M, M, V("tl"))
+    act(V("iw1", 0, 384), V("et", 0, 384), 0.0)
+    pick("pq", "pss", "sq", "ss", C, "sig", 2 * M, M)
+    four(0, "eq", "es", "yq", "yp", M, M)
+    four(4, "eq", "es", "pq", "pss", 2 * M, M)
+    to_window("wf", PF, 1 + 4 * M, M, "ssss")
+    act(V("bw", 0, 1280), V("et", 0, 1280), 0.0)
+    for i, c in enumerate((M, M + NS, 2 * M + NS)):
+        act(V("col", 5 + i, 6 + i), V("sel", 1, 2), float(c))
+    payload("pb2", None, V("col", 5, 6))
+    payload("pb1", V("col", 6, 7), V("col", 7, 8))
+    weave(front2(), requests(1))
+    four_lists("bs2", V("t5", 32, 44), 4.0, -4.0)
+    fill(V("wb", 0, 4 * PB_, PB_), 0.0)
+    four(0, "eq", "es", "lbq", "lbp", 0, NS)
+    order("y", [V("lbq")], [])
+    dma("y", "du", T.us[:], T.u[:], [], [V("us")])
+    for gr in range(8):
+        o = V("pij", 0, 30, p=(16 * gr, 16 * gr + 16, 1))
+        dma("y", "dpij", o[0], T.pdr[0:30, :], [V("pdr")], [o])
+    make("wf", PF, 1 + 5 * M + NS, 1 + 5 * M, NS, "fr2", "wq", "wp")
+
+    quant("yq", "yp", 2 * M, M, V("tl"))
+    four(4, "eq", "es", "yq", "yp", 2 * M, M)
+    evac(4, "xt", 1.0, "vsvs")
+    layer("vq", "vp")
+    pack("bs2", "ac_", "scq", "scp", "lcq", "lcp")
+
+    quant("zq", "zp", 2 * M, M, V("tl"))
+    four(4, "eq", "es", "yq", "yp", M, M)
+    four(0, "eq", "es", "zq", "zp", 2 * M, M)
+    to_window("wb", PB_, 1, M, "ssss")
+    successor_places()
+    successors(2, "br1")
+    four(0, "eq", "es", "lcq", "lcp", 0, NS)
+    make("wb", PB_, 1 + M + NS, 1 + M, NS, "br1", "vq", "vp",
+         lambda: four_lists("bs1", V("t5", 0, 12), 4.0, -4.0))
+    pack("bs1", "ad_", "sdq", "sdp", "ldq", "ldp")
+
+    quant("zq", "zp", M, M, V("tl"))
+    four(4, "eq", "es", "yq", "yp", 0, M)
+    four(0, "eq", "es", "zq", "zp", M, M)
+    to_window("wb", PB_, 1 + M + NS, M, "ssss")
+    successors(1, "br0")
+    quant("uq", "up", 0, 128, V("us"))
+    four(0, "eq", "es", "ldq", "ldp", 0, NS)
+    make("wb", PB_, 1 + 2 * M + 2 * NS, 1 + 2 * M + NS, NS, "br0", "vq", "vp")
+
+    quant("zq", "zp", 0, M, V("tl"))
+    halves = ((0, 256), (256, 224))
+    for a, n in halves:
+        pick("oq", "op", "zq", "zp", C, "pij", a, n)
+    for i, (a, n) in enumerate(halves):
+        mm(4 + i, "uq", "up", 0, "oq", "op", a, n)
+    dma("y", "dout", T.oc[:], T.oq[:].bitcast(dt.uint8), [V("oq")], [])
+    for i, (a, n) in enumerate(halves):
+        scaled("vs"[i], V("yo", a, a + n), V("ps", 512 * (4 + i), 512 * (4 + i) + n), 1.0)
+    for k in range(4):
+        dma("y", "dout", T.osc[4 * k:4 * k + 4, :], T.op[32 * k:32 * k + 4, :], [V("op")], [])
+    dma("s", "dout", T.y[:], T.yo[:], [V("yo")], [])
+    for sem in total:
+        need("g", (sem, None, {}))

@@ -21,17 +21,17 @@ SCRATCH = {
     "xt": _sb(4 * M, BF), "xq": _sb(M, Q4), "xp": _sb(M, U8), "tl": _sb(4 * M, BF),
     "yq": _sb(C, Q4), "yp": _sb(C, U8), "zq": _sb(C, Q4), "zp": _sb(C, U8), "oq": _sb(C, Q4), "op": _sb(C, U8),
     "wf": _sb(4 * PF, BF), "wb": _sb(4 * PB_, BF), "ab": _sb(4 * M, F32), "sm": _sb(4 * M, F32),
-    "st": _sb(4 * NS, BF), "yo": _sb(C, F32),
+    "tp": _sb(4 * M, BF), "st": _sb(4 * NS, BF), "yo": _sb(C, F32),
     "laq": _sb(3 * M, Q4), "lap": _sb(3 * M, U8),
-    "sbq": _sb(NS, Q4), "sbp": _sb(NS, U8), "lbq": _sb(NS, Q4), "lbp": _sb(NS, U8),
-    "scq": _sb(NS, Q4), "scp": _sb(NS, U8), "lcq": _sb(NS, Q4), "lcp": _sb(NS, U8),
-    "sdq": _sb(NS, Q4), "sdp": _sb(NS, U8), "ldq": _sb(NS, Q4), "ldp": _sb(NS, U8),
-    "pid": _sb(2, I32), "pt": _sb(4, I32), "pf": _sb(4, F32), "io32": _sb(192, F32), "keep": _sb(192, F32),
+    "sbq": _sb(256, Q4), "sbp": _sb(256, U8), "lbq": _sb(NS, Q4), "lbp": _sb(NS, U8),
+    "scq": _sb(256, Q4), "scp": _sb(256, U8), "lcq": _sb(NS, Q4), "lcp": _sb(NS, U8),
+    "sdq": _sb(256, Q4), "sdp": _sb(256, U8), "ldq": _sb(NS, Q4), "ldp": _sb(NS, U8),
+    "pid": _sb(2, I32), "pt": _sb(4, I32), "pf": _sb(4, F32), "io32": _sb(192, F32), "keep": _sb(192, BF),
     "m32": _sb(96, F32), "m16": _sb(192, F32), "oti": _sb(12, I32), "ot": _sb(12, U16),
     "io3": _sb(8, F32), "sel": _sb(8, F32), "io16": _sb(64, F32), "dmp": _sb(128, F32), "col": _sb(16, F32),
     "io1": _sb(NS, F32), "kp": _sb(2 * M, BF), "pb1": _sb(512, BF), "pb2": _sb(512, BF), "k160": _sb(64, F32),
     "lvl": _sb(16, I32), "rw": _sb(C, I32), "sw": _sb(2 * C, F32), "swt": _sb(2 * C, F32),
-    "ind": _sb(192, F32), "cum": _sb(192, F32), "cuc": _sb(192, F32), "bc": _sb(192, F32), "tr": _sb(192, F32), "sc": _sb(192, F32),
+    "ind": _sb(192, BF), "cum": _sb(192, BF), "cuc": _sb(192, F32), "bc": _sb(192, BF), "tr": _sb(192, BF), "sc": _sb(192, BF),
     "pp": _sb(192, F32), "pd": _sb(192, F32), "tr2": _sb(192, F32), "t5": _sb(64, F32), "t6": _sb(64, F32),
     "t1": _sb(64, F32), "t2": _sb(64, F32), "t3": _sb(64, F32), "t4": _sb(64, F32),
     "i1": _sb(64, I32), "i2": _sb(64, I32), "ofs": _sb(32, U16),
@@ -43,13 +43,13 @@ SCRATCH = {
     "iw1": _sb(704, BF), "iw2": _sb(704, BF), "iwt": _sb(384, BF), "iof": _sb(64, U16),
     "rq1": _sb(24, F32), "rq2": _sb(24, F32), "rl1": _sb(24, F32), "rl2": _sb(24, F32),
     "fr1": _sb(20, U16), "fr2": _sb(20, U16), "br1": _sb(20, U16), "br0": _sb(20, U16),
-    "fs": _sb(48, U16), "bs1": _sb(48, U16), "bs2": _sb(48, U16),
+    "fs": _sb(12, U16), "bs": _sb(24, U16),
     "bw": _sb(1792, BF), "bof": _sb(64, U16),
     "td0": ("dram", [128, 16], BF), "td1": ("dram", [128, 16], BF), "td2": ("dram", [128, 16], BF),
     "pdr": ("dram", [128, 16], U16),
 }
 SEMAPHORES = ["cv", "cs", "ct", "cg", "dlv", "dx", "drw", "dw", "dv", "du", "dtab", "dpd", "dpij", "dout",
-              "sent", "atab", "aa0", "aa1", "aa2", "ar1", "ar2", "ab_", "ac_", "ad_"]
+              "sent", "atab", "aa0", "aa1", "aa2", "ar1", "ar2", "ab_", "ac_", "ad_", "ab_2", "ac_2", "ad_2"]
 
 
 def rank_program(g, core, T, topo):
@@ -214,10 +214,12 @@ def rank_program(g, core, T, topo):
         for b in range(4):
             mm(bank0 + b, lq, lp, b, rq, rp, a, n)
 
-    def pick(oq, op_, sq_, sp_, n, off, a, k):
+    def pick(oq, op_, sq_, sp_, n, off, a, k, who="vs"):
         o, w, f = V(oq, a, a + k), V(sq_, 0, n), V(off, a // 16, (a + k) // 16)
-        op("v", lambda: g.vector.tensor_copy(o[0].bitcast(dt.uint32), w[0].bitcast(dt.uint32).indirect(f[0])), [w, f], [o])
-        gat("s", V(op_, a, a + k), V(sp_, 0, n), f)
+        if "v" in who:
+            op("v", lambda: g.vector.tensor_copy(o[0].bitcast(dt.uint32), w[0].bitcast(dt.uint32).indirect(f[0])), [w, f], [o])
+        if "s" in who:
+            gat("s", V(op_, a, a + k), V(sp_, 0, n), f)
 
     eng = topo.engines(core, cores[peers[0]])
     for s in peers:
@@ -241,19 +243,24 @@ def rank_program(g, core, T, topo):
         total["sent"] = total.get("sent", 0) + len(eng)
 
     first = [eng[0:2 * h], eng[2 * h:3 * h], eng[3 * h:4 * h]]
-    second = [eng[2 * h:4 * h], eng[0:h], eng[h:2 * h]]
 
-    def send_packed(sem, sq_, sp_, lq, lp):
-        pc, pz = [], []
-        for e in range(3):
-            a, b = CAP * e, CAP * slot_at[e]
-            v = V(sq_, a, a + CAP)
-            pc.append((v, v[0].bitcast(dt.uint8), T[lq][:, b:b + CAP].bitcast(dt.uint8)))
-            v = V(sp_, a, a + CAP)
-            pz.append((v, v[0], T[lp][:, b:b + CAP]))
-        fused(sem, pc, first)
-        fused(sem, pz, second)
-        landed(sem, 2 * len(eng), [V(lq), V(lp)])
+    def send_part(sem, sq_, sp_, lq, lp, es):
+        k = len(eng) // len(es)
+        for src, dst, codes in ((sq_, lq, True), (sp_, lp, False)):
+            trs = []
+            for i, e in enumerate(es):
+                a, b = (CAP * e if e < 2 else 3 * CAP), CAP * slot_at[e]
+                v = V(src, a, a + CAP)
+                order("g", [v], [])
+                rid, pid, _ = topo.addr(cores[peers[e]])
+                o = T[dst][:, b:b + CAP]
+                trs.append(RemoteDMATransfer(dst_ids=[DstId(rid=rid, pnc=pid)], dma_engine_mask=emask(eng[k * i:k * i + k]),
+                                             remote_sem=T.sem[sem], src=v[0].bitcast(dt.uint8) if codes else v[0],
+                                             dst=o.bitcast(dt.uint8) if codes else o))
+            g.remote_dma_fused(trs, local_sem=T.sem.sent)
+            total["sent"] += len(eng)
+        a, b = CAP * es[0], CAP * es[-1] + CAP
+        landed(sem, 2 * len(eng), [V(lq, a, b), V(lp, a, b)])
 
     fill(V("lvl"), 2)
     fill(V("one"), 1.0)
@@ -341,9 +348,9 @@ def rank_program(g, core, T, topo):
     tt(V("t4", 0, 16), V("i1", 0, 16), V("i2", 0, 16), add)
     tt(V("t4", 16, 32), V("i1", 16, 32), V("i2", 0, 16), add)
     trn(V("t4", 32, 64), V("t4", 0, 32))
-    cp(V("vu"), V("i1", 0, 16))
-    cp(V("ofs"), V("t4", 32, 64))
     quant("sq", "ss", 0, C, V("xs"))
+    cp(V("ofs"), V("t4", 32, 64))
+    cp(V("vu"), V("i1", 0, 16))
     sca(V("sw"), V("ofs", 0, 30), V("rw"))
     dma("y", "dpd", T.pdr[:], T.vu[:], [V("vu")], [V("pdr")])
     landed("atab", len(eng), [V("td0"), V("td1"), V("td2")])
@@ -357,14 +364,14 @@ def rank_program(g, core, T, topo):
     cp(V("sig", 0, 10), V("t1", 0, 10))
     pick("pq", "pss", "sq", "ss", C, "sig", 0, M)
 
-    def evac(bank0, tile, c, who="vsvs"):
+    def evac(bank0, tile, c, who="svsv"):
         for b in range(4):
             scaled(who[b], V(tile, b, 4 * M, 4), V("ps", 512 * (bank0 + b), 512 * (bank0 + b) + M), c)
 
-    def to_window(win, pitch, a, n, who):
+    def to_window(win, pitch, a, n, who, skip=0):
         for b in range(4):
             if who[b] != "-":
-                scaled(who[b], V(win, pitch * b + a, pitch * b + a + n), V("ps", 512 * b, 512 * b + n), -0.5)
+                scaled(who[b], V(win, pitch * b + a, pitch * b + a + n), V("ps", 512 * b + skip, 512 * b + skip + n), -0.5)
 
     def places():
         for l in (1, 2):
@@ -383,19 +390,19 @@ def rank_program(g, core, T, topo):
         for e in range(3):
             ts(V("ind", 64 * e, 64 * e + 64), V("si"), peers[e], AluOpType.is_equal)
         tt(V("idx"), V("t3"), V("t4"), add)
-        pick("pq", "pss", "sq", "ss", C, "sig", M, M)
+        pick("pq", "pss", "sq", "ss", C, "sig", M, M, "s")
+        scan(V("cum"), V("ind"), 192)
         ts(V("id2", 0, 128, 2), V("idx"), 0.0, mx_, V("sel", 4, 5), mul)
         ts(V("id2", 1, 128, 2), V("idx"), 0.0, mx_, V("sel", 5, 6), mul)
-        cp(V("idc"), V("idx"))
 
     four(4, "eq", "es", "pq", "pss", 0, M)
     trn(V("swt", 320, 640), V("sw", 320, 640))
-    evac(4, "xt", 1.0, "svsv")
+    evac(4, "xt", 1.0)
     fill(V("pri"), -1)
     quant("xq", "xp", 0, M, V("xt"))
     four(0, "wq", "wp", "xq", "xp", 0, M)
     trn(V("swt", 640, 960), V("sw", 640, 960))
-    evac(0, "tl", 0.03125, "svsv")
+    evac(0, "tl", 0.03125)
     fill(V("wf", 0, 4 * PF, PF), 0.0)
     quant("yq", "yp", 0, M, V("tl"))
     for e in range(3):
@@ -410,7 +417,6 @@ def rank_program(g, core, T, topo):
     four(0, "eq", "es", "yq", "yp", 0, M)
     to_window("wf", PF, 1 + M * rank, M, "ssss")
     places()
-    four(4, "eq", "es", "pq", "pss", M, M)
 
     def scatter_places(out, high, dump):
         ts(V("i2"), V("i1"), high, AluOpType.bitwise_and)
@@ -420,18 +426,25 @@ def rank_program(g, core, T, topo):
         cp(V(out), V("t1"))
 
     def slots():
-        ranks_in_class("m16", 192)
+        ttg(V("bc"), V("cum"), V("ot"), V("m16"), mul)
+        for e in range(3):
+            act(V("cuc", 64 * e, 64 * e + 64), V("cum", 64 * e, 64 * e + 64), 1.0, float(CAP * e))
         gat("s", V("g2a"), V("tab"), V("id2", 0, 40))
-        tt(V("t1"), V("pd", 0, 64), V("pd", 64, 128), add)
+        cp(V("idc"), V("idx"))
+        trn(V("tr"), V("bc"))
         ts(V("s160"), V("si"), M, mul)
+        scan(V("sc"), V("tr"), 192)
+        ts(V("ko"), V("si"), rank, AluOpType.is_equal, 1000.0, mul)
+        ttg(V("pp"), V("sc"), V("ot"), V("cuc"), add)
+        tt(V("pd"), V("pp"), V("ind"), mul)
+        tt(V("t1"), V("pd", 0, 64), V("pd", 64, 128), add)
         tt(V("qq"), V("t1"), V("pd", 128, 192), add)
         ts(V("i1"), V("qq"), -1.0, add)
         scatter_places("iof", 1008, V("dmp", 0, 64))
 
-    def four_lists(name, src, c1, c2):
-        ts(V("t4", 0, 12), src, c1, mul, c2, add)
-        for b in range(4):
-            ts(V(name, 12 * b, 12 * b + 12), V("t4", 0, 12), 0.0, mx_, float(b), add)
+    def one_list(out, src, c1):
+        ts(V("t4", 0, 12), src, c1, mul, -1.0, add)
+        cp(out, V("t4", 0, 12))
 
     def codes_of(l):
         trn(V("g2t"), V("g2a" if l == 1 else "g2b"))
@@ -489,22 +502,31 @@ def rank_program(g, core, T, topo):
             a, rl = 32 * l - 12, "rl%d" % l
             cp(V("tca", a, a + 12), V(rl, 0, 24, 2))
             ts(V("k160", a, a + 12), V(rl, 1, 24, 2), M, mul, -1.0, add)
-        ts(V("ko"), V("si"), rank, AluOpType.is_equal, 1000.0, mul)
+        yield
         ts(V("t1"), V("tca"), -2.0, mul, 2.0 * M, add)
         ts(V("t2"), V("tca"), 0.0, AluOpType.is_lt)
+        ts(V("bs", 12, 24), V("t5", 32, 44), -1.0, add, 0.0, mx_)
+        yield
         tt(V("t4"), V("tca"), V("k160"), add)
         tt(V("t3"), V("t1"), V("t2"), mul)
+        yield
         tt(V("t6"), V("t4"), V("ko"), add)
         tt(V("i1"), V("t3"), V("t6"), add)
         scatter_places("bof", 4080, V("dmp", 64, 128))
+        yield
 
-    def successors(l, out):
-        sca(V("bw"), V("bof", 32 * l - 32, 32 * l), V("pb%d" % l))
+    def successors(l, out, between=None):
+        a = 32 * l - 32
+        if between:
+            sca(V("bw"), V("bof", a + 20, a + 32), V("pb%d" % l, 2 * M, 512))
+            between()
+            sca(V("bw"), V("bof", a, a + 20), V("pb%d" % l, 0, 2 * M))
+        else:
+            sca(V("bw"), V("bof", a, a + 32), V("pb%d" % l))
         a = 640 * (l - 1)
         trn(V("g2t"), V("bw", a, a + 640))
-        tt(V("t1", 0, 20), V("g2t", 0, 640, 32), V("g2t", 16, 640, 32), add)
-        tt(V("t2", 0, 20), V("g2t", 1, 640, 32), V("g2t", 17, 640, 32), add)
-        tt(V("t3", 0, 20), V("t1", 0, 20), V("t2", 0, 20), add)
+        tt(V("t1", 0, 40), V("g2t", 0, 640, 16), V("g2t", 1, 640, 16), add)
+        tt(V("t3", 0, 20), V("t1", 0, 40, 2), V("t1", 1, 40, 2), add)
         cp(V(out), V("t3", 0, 20))
 
     def payload(name, own, far):
@@ -514,7 +536,7 @@ def rank_program(g, core, T, topo):
             else:
                 act(V(name, a, a + n), V("io1", 0, n), V("sel", 0, 1), c)
 
-    def make(win, pitch, wn, a, n, lst, lq, lp, between=None):
+    def make(win, pitch, wn, a, n, lst, lq, lp, between=None, early=False):
         def w(b):
             return V(win, pitch * b, pitch * b + wn)
 
@@ -526,97 +548,122 @@ def rank_program(g, core, T, topo):
 
         def fin(b):
             tt(V("xt", b, 4 * M, 4), V("ps", 512 * (4 + b), 512 * (4 + b) + M), V("sm", M * b, M * b + M), add)
-        to_window(win, pitch, a, n, "vs--")
-        ga(0, "v")
-        ga(1, "s")
-        to_window(win, pitch, a, n, "--s-")
-        ga(2, "s")
-        to_window(win, pitch, a, n, "---s")
-        ga(3, "s")
+        if early:
+            for b in range(4):
+                to_window(win, pitch, a, n, "-" * b + "s" + "-" * (3 - b))
+                ga(b, "s")
+            gat("s", V("g2b"), V("tab"), V("id2", 64, 104))
+        else:
+            to_window(win, pitch, a, n, "vs--", CAP)
+            ga(0, "v")
+            ga(1, "s")
+            to_window(win, pitch, a, n, "--s-", CAP)
+            ga(2, "s")
+            to_window(win, pitch, a, n, "---s", CAP)
+            ga(3, "s")
         gb(0)
         gb(1)
         fin(0)
         gb(2)
         fin(1)
-        fin(2)
         gb(3)
+        fin(2)
         fin(3)
         layer(lq, lp, between)
+
+    def arrive(lq, lp, win, pitch, a):
+        four(0, "eq", "es", lq, lp, 0, 2 * CAP)
+        to_window(win, pitch, a, 2 * CAP, "ssss")
+        four(0, "eq", "es", lq, lp, CAP, 2 * CAP)
 
     def layer(lq, lp, between=None):
         quant("xq", "xp", 0, M, V("xt"))
         four(0, lq, lp, "xq", "xp", 0, M)
         if between:
             between()
-        evac(0, "tl", 0.03125, "vsvs")
 
     def pack(lst, sem, sq_, sp_, lq, lp):
         for b in range(4):
-            gat("vsvs"[b], V("st", b, 4 * NS, 4), V("tl"), V(lst, 12 * b, 12 * b + 12))
-        quant(sq_, sp_, 0, NS, V("st"))
-        send_packed(sem, sq_, sp_, lq, lp)
+            scaled("svsv"[b], V("tp", M * b, M * b + M), V("ps", 512 * b, 512 * b + M), 0.03125)
+        for b in range(4):
+            gat("svsv"[b], V("st", b, 8 * CAP, 4), V("tp", M * b, M * b + M), V(lst[0], lst[1], lst[1] + 8))
+        quant(sq_, sp_, 0, 2 * CAP, V("st", 0, 8 * CAP))
+        send_part(sem, sq_, sp_, lq, lp, [0, 1])
+        for b in range(4):
+            gat("svss"[b], V("st", 8 * CAP + b, 4 * NS, 4), V("tp", M * b, M * b + M), V(lst[0], lst[1] + 8, lst[1] + 12))
+        quant(sq_, sp_, 2 * CAP, 2 * CAP, V("st", 4 * CAP, 4 * NS))
+        send_part(sem + "2", sq_, sp_, lq, lp, [2])
+        evac(0, "tl", 0.03125, "ssss")
 
     slots()
-    weave(requests(2), codes_of(1))
-    tt(V("t1", 0, 20), V("tca", 0, 20), V("s160", 0, 20), add)
-    cp(V("fr1"), V("t1", 0, 20))
-    for e in range(2):
-        four(0, "eq", "es", "laq", "lap", M * e, M)
-        to_window("wf", PF, 1 + M * peers[e], M, "ssss")
-        if e == 0:
-            gat("s", V("g2b"), V("tab"), V("id2", 64, 104))
-    four(0, "eq", "es", "laq", "lap", 2 * M, M)
-    make("wf", PF, 1 + 4 * M, 1 + M * peers[2], M, "fr1", "wq", "wp",
-         lambda: four_lists("fs", V("rl2", 0, 24, 2), -4.0, -4.0))
-    pack("fs", "ab_", "sbq", "sbp", "lbq", "lbp")
-
-    quant("yq", "yp", M, M, V("tl"))
-    act(V("iw1", 0, 384), V("et", 0, 384), 0.0)
-    pick("pq", "pss", "sq", "ss", C, "sig", 2 * M, M)
-    four(0, "eq", "es", "yq", "yp", M, M)
-    four(4, "eq", "es", "pq", "pss", 2 * M, M)
-    to_window("wf", PF, 1 + 4 * M, M, "ssss")
-    act(V("bw", 0, 1280), V("et", 0, 1280), 0.0)
+    act(V("wb", 0, 4 * PB_, PB_), V("et", 0, 4), 0.0)
     for i, c in enumerate((M, M + NS, 2 * M + NS)):
         act(V("col", 5 + i, 6 + i), V("sel", 1, 2), float(c))
+    for e in range(3):
+        four(0, "eq", "es", "laq", "lap", M * e, M)
+        if e < 2:
+            to_window("wf", PF, 1 + M * peers[e], M, "ssss")
+    act(V("bw", 0, 1280), V("et", 0, 1280), 0.0)
+    r2, c1 = requests(2), codes_of(1)
+    next(c1)
+    next(r2)
+    weave(c1)
+    tt(V("t3", 0, 20), V("tca", 0, 20), V("s160", 0, 20), add)
+    cp(V("fr1"), V("t3", 0, 20))
+    weave(r2)
+    pick("pq", "pss", "sq", "ss", C, "sig", M, M, "v")
+    four(4, "eq", "es", "pq", "pss", M, M)
+    make("wf", PF, 1 + 4 * M, 1 + M * peers[2], M, "fr1", "wq", "wp",
+         lambda: one_list(V("fs"), V("rl2", 0, 24, 2), -1.0), True)
+    pack(("fs", 0), "ab_", "sbq", "sbp", "lbq", "lbp")
+
+    act(V("iw1", 0, 384), V("et", 0, 384), 0.0)
+    pick("pq", "pss", "sq", "ss", C, "sig", 2 * M, M)
+    four(4, "eq", "es", "pq", "pss", 2 * M, M)
+    w1, w2 = front2(), requests(1)
+    next(w1)
+    next(w2)
+    quant("yq", "yp", M, M, V("tl"))
+    four(0, "eq", "es", "yq", "yp", M, M)
+    to_window("wf", PF, 1 + 4 * M, M, "ssss")
     payload("pb2", None, V("col", 5, 6))
-    payload("pb1", V("col", 6, 7), V("col", 7, 8))
-    weave(front2(), requests(1))
-    four_lists("bs2", V("t5", 32, 44), 4.0, -4.0)
-    fill(V("wb", 0, 4 * PB_, PB_), 0.0)
-    four(0, "eq", "es", "lbq", "lbp", 0, NS)
+    weave(w1, w2)
+    arrive("lbq", "lbp", "wf", PF, 1 + 5 * M)
     order("y", [V("lbq")], [])
     dma("y", "du", T.us[:], T.u[:], [], [V("us")])
     for gr in range(8):
         o = V("pij", 0, 30, p=(16 * gr, 16 * gr + 16, 1))
         dma("y", "dpij", o[0], T.pdr[0:30, :], [V("pdr")], [o])
-    make("wf", PF, 1 + 5 * M + NS, 1 + 5 * M, NS, "fr2", "wq", "wp")
+    sp = successor_places()
+    make("wf", PF, 1 + 5 * M + NS, 1 + 5 * M + 2 * CAP, CAP, "fr2", "wq", "wp", lambda: next(sp))
 
+    evac(0, "tl", 0.03125)
     quant("yq", "yp", 2 * M, M, V("tl"))
     four(4, "eq", "es", "yq", "yp", 2 * M, M)
-    evac(4, "xt", 1.0, "vsvs")
-    layer("vq", "vp")
-    pack("bs2", "ac_", "scq", "scp", "lcq", "lcp")
+    next(sp)
+    evac(4, "xt", 1.0)
+    layer("vq", "vp", lambda: next(sp))
+    pack(("bs", 12), "ac_", "scq", "scp", "lcq", "lcp")
 
-    quant("zq", "zp", 2 * M, M, V("tl"))
+    weave(sp)
     four(4, "eq", "es", "yq", "yp", M, M)
+    quant("zq", "zp", 2 * M, M, V("tl"))
     four(0, "eq", "es", "zq", "zp", 2 * M, M)
     to_window("wb", PB_, 1, M, "ssss")
-    successor_places()
     successors(2, "br1")
-    four(0, "eq", "es", "lcq", "lcp", 0, NS)
-    make("wb", PB_, 1 + M + NS, 1 + M, NS, "br1", "vq", "vp",
-         lambda: four_lists("bs1", V("t5", 0, 12), 4.0, -4.0))
-    pack("bs1", "ad_", "sdq", "sdp", "ldq", "ldp")
+    payload("pb1", V("col", 6, 7), V("col", 7, 8))
+    arrive("lcq", "lcp", "wb", PB_, 1 + M)
+    make("wb", PB_, 1 + M + NS, 1 + M + 2 * CAP, CAP, "br1", "vq", "vp",
+         lambda: ts(V("bs", 0, 12), V("t5", 0, 12), -1.0, add, 0.0, mx_))
+    pack(("bs", 0), "ad_", "sdq", "sdp", "ldq", "ldp")
 
-    quant("zq", "zp", M, M, V("tl"))
     four(4, "eq", "es", "yq", "yp", 0, M)
-    four(0, "eq", "es", "zq", "zp", M, M)
-    to_window("wb", PB_, 1 + M + NS, M, "ssss")
-    successors(1, "br0")
-    quant("uq", "up", 0, 128, V("us"))
-    four(0, "eq", "es", "ldq", "ldp", 0, NS)
-    make("wb", PB_, 1 + 2 * M + 2 * NS, 1 + 2 * M + NS, NS, "br0", "vq", "vp")
+    successors(1, "br0", lambda: (quant("zq", "zp", M, M, V("tl")), four(0, "eq", "es", "zq", "zp", M, M),
+                                  to_window("wb", PB_, 1 + M + NS, M, "ssss")))
+    arrive("ldq", "ldp", "wb", PB_, 1 + 2 * M + NS)
+    make("wb", PB_, 1 + 2 * M + 2 * NS, 1 + 2 * M + NS + 2 * CAP, CAP, "br0", "vq", "vp",
+         lambda: quant("uq", "up", 0, 128, V("us")))
+    evac(0, "tl", 0.03125)
 
     quant("zq", "zp", 0, M, V("tl"))
     halves = ((0, 256), (256, 224))

@@ -3,7 +3,7 @@ from concourse.mybir import dt, AluOpType, ActivationFunctionType
 
 C, M, CAP = 480, 160, 64
 NS = 3 * CAP
-PF, PB_ = 1024, 768
+PF, PB_ = 1296, 768
 TABW = 32 + 4 * 512
 Q4, U8, BF, F32, I32, U16 = "float8_e4m3fn_x4", "uint8", "bfloat16", "float32", "int32", "uint16"
 
@@ -14,42 +14,42 @@ def _sb(n, d):
 
 SCRATCH = {
     "ps": ("psum", [128, 4096], F32),
-    "xs": _sb(4 * C, BF), "sq": _sb(C, Q4), "ss": _sb(C, U8), "pq": _sb(C, Q4), "pss": _sb(C, U8),
-    "et": _sb(2048, BF), "eq": _sb(512, Q4), "es": _sb(512, U8), "one": _sb(128, F32), "ident": _sb(128, F32),
+    "xs": _sb(4 * C, BF), "sq": _sb(C, Q4), "ss": _sb(C, U8), "pq": _sb(2 * M, Q4), "pss": _sb(2 * M, U8),
+    "xa": _sb(4 * C, BF), "xaq": _sb(C, Q4), "xap": _sb(C, U8), "x0q": _sb(M, Q4), "x0p": _sb(M, U8),
+    "et": _sb(520, BF), "eq": _sb(512, Q4), "es": _sb(512, U8), "one": _sb(128, BF),
     "wq": _sb(512, Q4), "wp": _sb(512, U8), "vq": _sb(512, Q4), "vp": _sb(512, U8),
     "us": _sb(512, BF), "uq": _sb(128, Q4), "up": _sb(128, U8),
     "xt": _sb(4 * M, BF), "xq": _sb(M, Q4), "xp": _sb(M, U8), "tl": _sb(4 * M, BF),
     "yq": _sb(C, Q4), "yp": _sb(C, U8), "zq": _sb(C, Q4), "zp": _sb(C, U8), "oq": _sb(C, Q4), "op": _sb(C, U8),
     "wf": _sb(4 * PF, BF), "wb": _sb(4 * PB_, BF), "ab": _sb(4 * M, F32), "sm": _sb(4 * M, F32),
     "tp": _sb(4 * M, BF), "st": _sb(4 * NS, BF), "yo": _sb(C, F32),
-    "laq": _sb(3 * M, Q4), "lap": _sb(3 * M, U8),
-    "sbq": _sb(256, Q4), "sbp": _sb(256, U8), "lbq": _sb(NS, Q4), "lbp": _sb(NS, U8),
+    "laq": _sb(3 * M, Q4), "lap": _sb(3 * M, U8), "lbq": _sb(3 * M, Q4), "lbp": _sb(3 * M, U8),
     "scq": _sb(256, Q4), "scp": _sb(256, U8), "lcq": _sb(NS, Q4), "lcp": _sb(NS, U8),
     "sdq": _sb(256, Q4), "sdp": _sb(256, U8), "ldq": _sb(NS, Q4), "ldp": _sb(NS, U8),
     "pid": _sb(2, I32), "pt": _sb(4, I32), "pf": _sb(4, F32), "io32": _sb(192, F32), "keep": _sb(192, BF),
     "m32": _sb(96, F32), "m16": _sb(192, F32), "oti": _sb(12, I32), "ot": _sb(12, U16),
     "io3": _sb(8, F32), "sel": _sb(8, F32), "io16": _sb(64, F32), "dmp": _sb(128, F32), "col": _sb(16, F32),
-    "io1": _sb(NS, F32), "kp": _sb(2 * M, BF), "pb1": _sb(512, BF), "pb2": _sb(512, BF), "k160": _sb(64, F32),
-    "lvl": _sb(16, I32), "rw": _sb(C, I32), "sw": _sb(2 * C, F32), "swt": _sb(2 * C, F32),
-    "ind": _sb(192, BF), "cum": _sb(192, BF), "cuc": _sb(192, F32), "bc": _sb(192, BF), "tr": _sb(192, BF), "sc": _sb(192, BF),
-    "pp": _sb(192, F32), "pd": _sb(192, F32), "tr2": _sb(192, F32), "t5": _sb(64, F32), "t6": _sb(64, F32),
-    "t1": _sb(64, F32), "t2": _sb(64, F32), "t3": _sb(64, F32), "t4": _sb(64, F32),
-    "i1": _sb(64, I32), "i2": _sb(64, I32), "ofs": _sb(32, U16),
+    "io1": _sb(NS, F32), "kp": _sb(2 * M, BF), "pb1": _sb(512, BF), "pb2": _sb(512, BF), "kc": _sb(64, F32),
+    "lvl": _sb(32, I32), "rw": _sb(C, I32), "sw": _sb(2 * C, F32), "swt": _sb(2 * C, F32),
+    "ind": _sb(192, BF), "cum": _sb(192, BF), "bc": _sb(192, BF), "tr": _sb(192, BF), "sc": _sb(192, BF),
+    "ind0": _sb(96, BF), "cum0": _sb(96, BF), "bc0": _sb(96, BF), "tr0": _sb(96, BF), "sc0": _sb(96, BF),
+    "cuc": _sb(192, F32), "pp": _sb(192, F32), "pd": _sb(192, F32),
+    "tf": _sb(3072, F32), "ti": _sb(1024, I32), "ofs": _sb(32, U16),
     "tc30": _sb(16, BF), "vu": _sb(16, U16), "pij": _sb(32, U16), "sig": _sb(32, U16),
-    "pri": _sb(64, I32), "si": _sb(64, I32), "s160": _sb(64, F32), "idx": _sb(64, F32),
     "idc": _sb(64, U16), "id2": _sb(128, U16), "tab": _sb(TABW, BF),
-    "g2a": _sb(4 * M, BF), "g2b": _sb(4 * M, BF), "g2t": _sb(4 * M, BF), "gc": _sb(2 * M, BF),
-    "tca": _sb(64, F32), "ko": _sb(64, F32), "qq": _sb(64, F32),
-    "iw1": _sb(704, BF), "iw2": _sb(704, BF), "iwt": _sb(384, BF), "iof": _sb(64, U16),
-    "rq1": _sb(24, F32), "rq2": _sb(24, F32), "rl1": _sb(24, F32), "rl2": _sb(24, F32),
+    "g2a": _sb(4 * M, BF), "g2b": _sb(4 * M, BF), "g2t": _sb(16 * M, BF), "gc": _sb(4 * M, BF),
+    "iw1": _sb(704, BF), "iw2": _sb(704, BF), "iwt": _sb(768, BF), "iof": _sb(64, U16),
+    "rq1": _sb(12, U16), "rq2": _sb(12, U16), "rl1": _sb(16, U16), "rl2": _sb(16, U16),
     "fr1": _sb(20, U16), "fr2": _sb(20, U16), "br1": _sb(20, U16), "br0": _sb(20, U16),
-    "fs": _sb(12, U16), "bs": _sb(24, U16),
-    "bw": _sb(1792, BF), "bof": _sb(64, U16),
-    "td0": ("dram", [128, 16], BF), "td1": ("dram", [128, 16], BF), "td2": ("dram", [128, 16], BF),
-    "pdr": ("dram", [128, 16], U16),
+    "bs": _sb(24, U16), "bw": _sb(1792, BF), "bof": _sb(64, U16),
+    "td": ("dram", [4, 128, 4], BF), "pdr": ("dram", [128, 16], U16),
 }
-SEMAPHORES = ["cv", "cs", "ct", "cg", "dlv", "dx", "drw", "dw", "dv", "du", "dtab", "dpd", "dpij", "dout",
-              "sent", "atab", "aa0", "aa1", "aa2", "ar1", "ar2", "ab_", "ac_", "ad_", "ab_2", "ac_2", "ad_2"]
+SEMAPHORES = ["cv", "cs", "ct", "cg", "dlv", "dx", "drw", "dw", "dv", "du", "dtd", "dtab", "dpd", "dpij", "dout",
+              "sent", "atab", "aa0", "aa1", "aa2", "ab0", "ab1", "ab2", "ar1", "ar2", "ac_", "ad_", "ac_2", "ad_2"]
+SIZE = {Q4: 4, U8: 1, BF: 2, F32: 4, I32: 4, U16: 2}
+ORDER = [
+    0, 8, 7, 6, 4, 2, 14, 1, 3, 5, 23, 24, 9, 27, 21, 29, 22, 15, 16, 42, 18, 12, 10, 79, 81, 80, 26, 83, 84, 34, 33, 32, 58, 35, 54, 36, 37, 40, 17, 20, 19, 85, 86, 25, 87, 82, 88, 28, 90, 89, 13, 91, 11, 106, 92, 107, 108, 69, 109, 93, 94, 95, 70, 74, 73, 72, 71, 41, 96, 77, 76, 75, 110, 147, 112, 31, 114, 115, 44, 56, 116, 78, 118, 117, 145, 48, 119, 120, 121, 43, 123, 122, 124, 125, 126, 47, 45, 63, 127, 146, 128, 137, 138, 46, 49, 97, 139, 140, 105, 99, 100, 102, 98, 103, 104, 101, 129, 148, 149, 151, 150, 30, 155, 156, 154, 158, 157, 160, 159, 131, 132, 134, 65, 161, 135, 39, 111, 163, 162, 142, 51, 143, 59, 144, 64, 141, 38, 60, 53, 190, 180, 182, 165, 499, 166, 130, 181, 183, 152, 153, 179, 202, 201, 203, 185, 207, 206, 204, 133, 210, 186, 136, 205, 208, 209, 214, 187, 213, 212, 211, 215, 216, 62, 411, 178, 289, 167, 184, 188, 164, 189, 168, 500, 221, 222, 169, 191, 170, 225, 217, 218, 219, 229, 231, 224, 220, 223, 227, 230, 228, 235, 232, 233, 67, 234, 290, 171, 236, 237, 239, 238, 241, 240, 242, 243, 192, 247, 246, 244, 245, 250, 248, 251, 249, 252, 295, 194, 193, 253, 195, 172, 254, 197, 196, 256, 257, 66, 68, 498, 408, 61, 55, 297, 301, 50, 173, 198, 262, 259, 199, 175, 200, 174, 260, 296, 298, 302, 57, 299, 263, 176, 264, 273, 255, 292, 300, 410, 497, 496, 261, 304, 308, 306, 305, 303, 307, 309, 265, 266, 268, 267, 269, 177, 270, 271, 274, 272, 258, 312, 313, 409, 316, 311, 310, 315, 317, 314, 318, 319, 320, 321, 334, 322, 293, 294, 291, 323, 226, 113, 327, 325, 330, 324, 326, 329, 331, 328, 332, 412, 333, 335, 336, 338, 337, 340, 342, 339, 341, 343, 344, 346, 345, 347, 348, 413, 414, 415, 349, 350, 353, 352, 351, 354, 355, 52, 356, 416, 357, 358, 359, 362, 417, 552, 360, 361, 363, 364, 365, 366, 275, 398, 367, 371, 368, 372, 369, 370, 374, 373, 375, 376, 377, 378, 386, 276, 379, 277, 384, 279, 418, 385, 383, 380, 392, 393, 394, 391, 381, 387, 388, 389, 419, 278, 399, 397, 401, 400, 402, 395, 405, 403, 406, 404, 407, 281, 420, 282, 421, 422, 283, 285, 280, 423, 284, 424, 425, 286, 287, 288, 382, 390, 426, 427, 429, 396, 428, 430, 431, 435, 433, 432, 440, 434, 437, 436, 441, 442, 438, 439, 443, 444, 448, 445, 446, 450, 449, 452, 447, 453, 451, 454, 501, 484, 455, 456, 457, 459, 458, 460, 461, 462, 463, 464, 465, 466, 504, 467, 503, 502, 468, 505, 506, 472, 469, 508, 507, 474, 481, 479, 480, 471, 473, 509, 482, 510, 475, 476, 477, 511, 487, 512, 513, 488, 491, 470, 489, 485, 490, 493, 495, 494, 492, 515, 514, 516, 517, 478, 518, 522, 519, 521, 520, 483, 486, 523, 526, 524, 527, 528, 525, 530, 529, 533, 534, 537, 535, 536, 531, 532, 539, 538, 541, 540, 542, 543, 545, 544, 546, 547, 548, 549, 550, 551, 553, 554, 555, 556, 557, 559, 558, 561, 562, 560, 564, 566, 563, 570, 568, 571, 569, 565, 567,
+]
 
 
 def rank_program(g, core, T, topo):
@@ -58,6 +58,7 @@ def rank_program(g, core, T, topo):
         return
     cores = list(T.cores)
     add, sub, mul, mx_ = AluOpType.add, AluOpType.subtract, AluOpType.mult, AluOpType.max
+    AND, SHR = AluOpType.bitwise_and, AluOpType.arith_shift_right
     COPY, IDENT = ActivationFunctionType.Copy, ActivationFunctionType.Identity
 
     def peers_of(r):
@@ -71,9 +72,9 @@ def rank_program(g, core, T, topo):
 
     queues = {"v": g.vector, "s": g.scalar, "t": g.tensor, "g": g, "y": g.sync}
     csem = {"v": "cv", "s": "cs", "t": "ct", "g": "cg"}
-    total = {}
-    known = {q: {} for q in queues}
+    ops = []
     hist = {}
+    used = {"tf": 0, "ti": 0}
 
     def bits(a, b, st):
         if st == 1:
@@ -84,108 +85,101 @@ def rank_program(g, core, T, topo):
         return m
 
     def V(name, a=0, b=None, st=1, p=(0, 128, 1)):
+        if isinstance(name, tuple):
+            name, base, n = name
+            a, b = base + a, base + (n if b is None else b)
         if b is None:
-            b = SCRATCH[name][1][1]
+            b = SCRATCH[name][1][-1]
         t = T[name]
         ap = t[p[0]:p[1]:p[2], a:b:st] if (st != 1 or p[2] != 1) else t[p[0]:p[1], a:b]
         cm = bits(a, b, st)
         if name == "ps":
             cm = bits(512 * (a // 512), 512 * ((b - 1) // 512 + 1), 1)
-        return (ap, name, bits(p[0], p[1], p[2]), cm)
+        return (ap, name, bits(p[0], p[1], p[2]), cm, len(range(a, b, st)))
 
-    def need(q, tok):
-        sem, cnt, snap = tok
-        if cnt is None:
-            cnt = total[sem]
-        k = known[q]
-        if k.get(sem, 0) >= cnt:
-            return
-        queues[q].wait_ge(T.sem[sem], cnt)
-        k[sem] = cnt
-        for s_, c_ in snap.items():
-            if k.get(s_, 0) < c_:
-                k[s_] = c_
+    def new(n, pool="tf"):
+        a = used[pool]
+        used[pool] += n
+        assert used[pool] <= SCRATCH[pool][1][1]
+        return (pool, a, n)
 
-    def order(q, reads, writes):
-        toks = {}
+    def note(q, kind, fn, reads, writes, size, sem=None, n=0, after=()):
+        deps = set(after)
         for views, w in ((reads, False), (writes, True)):
-            for (_, name, pm, cm) in views:
-                for (tok, pm2, cm2, w2) in hist.get(name, []):
-                    if (w or w2 or name == "ps") and (pm & pm2) and (cm & cm2):
-                        old = toks.get(tok[0])
-                        if old is None or tok[1] is None or (old[1] is not None and old[1] < tok[1]):
-                            toks[tok[0]] = tok
-        for tok in toks.values():
-            need(q, tok)
-
-    def note(tok, reads, writes):
+            for v_ in views:
+                for (j, pm2, cm2, w2) in hist.get(v_[1], []):
+                    if (w or w2 or v_[1] == "ps") and (v_[2] & pm2) and (v_[3] & cm2):
+                        deps.add(j)
+        i = len(ops)
+        ops.append({"q": q, "kind": kind, "fn": fn, "size": size, "sem": sem, "n": n, "deps": deps, "soft": list(after)})
         for views, w in ((reads, False), (writes, True)):
-            for (_, name, pm, cm) in views:
-                hist.setdefault(name, []).append((tok, pm, cm, w))
+            for v_ in views:
+                hist.setdefault(v_[1], []).append((i, v_[2], v_[3], w))
+        return i
 
-    def op(q, fn, reads, writes):
-        order(q, reads, writes)
-        sem = csem[q]
-        fn().then_inc(T.sem[sem], 1)
-        total[sem] = total.get(sem, 0) + 1
-        note((sem, total[sem], dict(known[q])), reads, writes)
+    def op(q, fn, reads, writes, size):
+        return note(q, "c", fn, reads, writes, size)
 
-    def dma(q, sem, out, in_, reads, writes):
-        order(q, reads, writes)
-        queues[q].dma_start(out, in_).then_inc(T.sem[sem], 16)
-        total[sem] = total.get(sem, 0) + 16
-        note((sem, None, dict(known[q])), reads, writes)
+    def dma(q, sem, out, in_, reads, writes, kb=0, after=()):
+        return note(q, "d", lambda: queues[q].dma_start(out, in_), reads, writes, ("dma", kb), sem, 16, after)
 
-    def landed(sem, n, views):
-        total[sem] = total.get(sem, 0) + n
-        note((sem, None, {}), [], views)
+    def landed(sem, n, views, after):
+        return note(None, "l", None, [], views, ("land", 0), sem, n, after)
+
+    def plain(n, *vs):
+        return ("half" if all(SIZE[SCRATCH[v_[1]][2]] == 2 for v_ in vs) else "one", n)
 
     def cp(o, i):
-        op("v", lambda: g.vector.tensor_copy(o[0], i[0]), [i], [o])
+        op("v", lambda: g.vector.tensor_copy(o[0], i[0]), [i], [o], plain(o[4], o, i))
 
     def fill(o, c):
-        op("v", lambda: g.vector.memset(o[0], c), [], [o])
+        op("v", lambda: g.vector.memset(o[0], c), [], [o], plain(o[4], o))
 
     def tt(o, a, b, f):
-        op("v", lambda: g.vector.tensor_tensor(o[0], a[0], b[0], f), [a, b], [o])
+        op("v", lambda: g.vector.tensor_tensor(o[0], a[0], b[0], f), [a, b], [o], ("one" if "ps" in (a[1], b[1]) else "two", o[4]))
 
     def ts(o, a, s1, f1, s2=None, f2=None):
         rd = [a] + [s for s in (s1, s2) if isinstance(s, tuple)]
         x1 = s1[0] if isinstance(s1, tuple) else s1
         x2 = s2[0] if isinstance(s2, tuple) else s2
         if f2 is None:
-            op("v", lambda: g.vector.tensor_scalar(o[0], a[0], x1, None, f1), rd, [o])
+            op("v", lambda: g.vector.tensor_scalar(o[0], a[0], x1, None, f1), rd, [o], plain(o[4], o, a))
         else:
-            op("v", lambda: g.vector.tensor_scalar(o[0], a[0], x1, x2, f1, f2), rd, [o])
+            op("v", lambda: g.vector.tensor_scalar(o[0], a[0], x1, x2, f1, f2), rd, [o], plain(o[4], o, a))
 
     def ttg(o, w, off, b, f):
-        op("v", lambda: g.vector.tensor_tensor(o[0], w[0].indirect(off[0]), b[0], f), [w, off, b], [o])
+        op("v", lambda: g.vector.tensor_tensor(o[0], w[0].indirect(off[0]), b[0], f), [w, off, b], [o], ("gather", o[4]))
 
     def gat(q, o, w, off):
         if q == "v":
-            op("v", lambda: g.vector.tensor_copy(o[0], w[0].indirect(off[0])), [w, off], [o])
+            op("v", lambda: g.vector.tensor_copy(o[0], w[0].indirect(off[0])), [w, off], [o], ("gather", o[4]))
         else:
-            op("s", lambda: g.scalar.activation(o[0], w[0].indirect(off[0]), COPY), [w, off], [o])
+            op("s", lambda: g.scalar.activation(o[0], w[0].indirect(off[0]), COPY), [w, off], [o], ("gather", o[4]))
 
     def sca(w, off, i):
-        op("v", lambda: g.vector.tensor_copy(w[0].indirect(off[0]), i[0]), [i, off], [w])
+        op("v", lambda: g.vector.tensor_copy(w[0].indirect(off[0]), i[0]), [i, off], [w], ("scatter", i[4]))
 
     def scan(o, d, n):
         k = V("keep", 0, n)
-        op("v", lambda: g.vector.tensor_tensor_scan(o[0], k[0], d[0], 0.0, mul, add), [k, d], [o])
+        op("v", lambda: g.vector.tensor_tensor_scan(o[0], k[0], d[0], 0.0, mul, add), [k, d], [o], plain(n, o, d))
 
     def trn(o, i):
-        op("v", lambda: g.vector.transpose(o[0], i[0]), [i], [o])
+        op("v", lambda: g.vector.transpose(o[0], i[0]), [i], [o], plain(o[4], o, i))
 
     def act(o, i, scale=1.0, bias=None, f=None):
         rd = [i] + [s for s in (scale, bias) if isinstance(s, tuple)]
         sc_ = scale[0] if isinstance(scale, tuple) else scale
         if bias is None:
             f = f or (IDENT if isinstance(scale, tuple) else COPY)
-            op("s", lambda: g.scalar.activation(o[0], i[0], f, scale=sc_), rd, [o])
+            op("s", lambda: g.scalar.activation(o[0], i[0], f, scale=sc_), rd, [o], ("act", o[4]))
         else:
             b_ = bias[0] if isinstance(bias, tuple) else bias
-            op("s", lambda: g.scalar.activation(o[0], i[0], f or IDENT, bias=b_, scale=sc_), rd, [o])
+            op("s", lambda: g.scalar.activation(o[0], i[0], f or IDENT, bias=b_, scale=sc_), rd, [o], ("act", o[4]))
+
+    def zero(name, n):
+        for a in range(0, n, 520):
+            k = min(520, n - a)
+            act(V(name, a, a + k), V("et", 0, k), 0.0)
 
     def scaled(q, o, i, c):
         if q == "s":
@@ -197,29 +191,27 @@ def rank_program(g, core, T, topo):
 
     def iota(o, pat, base, cm, fl=True):
         if fl:
-            op("g", lambda: g.iota(o[0], pat, base, cm, allow_small_or_imprecise_dtypes=True), [], [o])
+            op("g", lambda: g.iota(o[0], pat, base, cm, allow_small_or_imprecise_dtypes=True), [], [o], ("iota", o[4]))
         else:
-            op("g", lambda: g.iota(o[0], pat, base, cm), [], [o])
+            op("g", lambda: g.iota(o[0], pat, base, cm), [], [o], ("iota", o[4]))
 
     def quant(qn, pn, a, n, i):
         o, s_ = V(qn, a, a + n), V(pn, a, a + n)
-        op("v", lambda: g.vector.quantize_mx(o[0], s_[0], i[0]), [i], [o, s_])
+        op("v", lambda: g.vector.quantize_mx(o[0], s_[0], i[0]), [i], [o, s_], ("quant", n))
 
     def mm(bank, lq, lp, b, rq, rp, a, n):
         o, l1, l2 = V("ps", 512 * bank, 512 * bank + n), V(lq, 128 * b, 128 * b + 128), V(lp, 128 * b, 128 * b + 128)
         r1, r2 = V(rq, a, a + n), V(rp, a, a + n)
-        op("t", lambda: g.tensor.matmul_mx(o[0], l1[0], l2[0], r1[0], r2[0], True, True), [l1, l2, r1, r2], [o])
+        op("t", lambda: g.tensor.matmul_mx(o[0], l1[0], l2[0], r1[0], r2[0], True, True), [l1, l2, r1, r2], [o], ("mm", n))
 
     def four(bank0, lq, lp, rq, rp, a, n):
         for b in range(4):
             mm(bank0 + b, lq, lp, b, rq, rp, a, n)
 
-    def pick(oq, op_, sq_, sp_, n, off, a, k, who="vs"):
-        o, w, f = V(oq, a, a + k), V(sq_, 0, n), V(off, a // 16, (a + k) // 16)
-        if "v" in who:
-            op("v", lambda: g.vector.tensor_copy(o[0].bitcast(dt.uint32), w[0].bitcast(dt.uint32).indirect(f[0])), [w, f], [o])
-        if "s" in who:
-            gat("s", V(op_, a, a + k), V(sp_, 0, n), f)
+    def pick(oq, op_, a, sq_, sp_, n, off, c, k):
+        o, w, f = V(oq, a, a + k), V(sq_, 0, n), V(off, c, c + k // 16)
+        op("v", lambda: g.vector.tensor_copy(o[0].bitcast(dt.uint32), w[0].bitcast(dt.uint32).indirect(f[0])), [w, f], [o], ("gather", k))
+        gat("s", V(op_, a, a + k), V(sp_, 0, n), f)
 
     eng = topo.engines(core, cores[peers[0]])
     for s in peers:
@@ -232,302 +224,281 @@ def rank_program(g, core, T, topo):
             m |= 1 << e
         return m
 
-    def fused(sem, pairs, masks):
-        order("g", [p[0] for p in pairs], [])
-        trs = []
-        for e in range(3):
-            rid, pid, _ = topo.addr(cores[peers[e]])
-            trs.append(RemoteDMATransfer(dst_ids=[DstId(rid=rid, pnc=pid)], dma_engine_mask=emask(masks[e]),
-                                         remote_sem=T.sem[sem], src=pairs[e][1], dst=pairs[e][2]))
-        g.remote_dma_fused(trs, local_sem=T.sem.sent)
-        total["sent"] = total.get("sent", 0) + len(eng)
+    def remote(trs, reads, size, after=()):
+        def fn():
+            out = []
+            for e, es, sem, src, dst in trs:
+                rid, pid, _ = topo.addr(cores[peers[e]])
+                out.append(RemoteDMATransfer(dst_ids=[DstId(rid=rid, pnc=pid)], dma_engine_mask=emask(es), remote_sem=T.sem[sem], src=src, dst=dst))
+            g.remote_dma_fused(out, local_sem=T.sem.sent)
+        return note("g", "r", fn, reads, [], size, "sent", sum(len(t_[1]) for t_ in trs), after)
 
     first = [eng[0:2 * h], eng[2 * h:3 * h], eng[3 * h:4 * h]]
 
-    def send_part(sem, sq_, sp_, lq, lp, es):
+    def send_part(sem, sq_, sp_, lq, lp, es, prev):
         k = len(eng) // len(es)
         for src, dst, codes in ((sq_, lq, True), (sp_, lp, False)):
-            trs = []
+            trs, rd = [], []
             for i, e in enumerate(es):
                 a, b = (CAP * e if e < 2 else 3 * CAP), CAP * slot_at[e]
                 v = V(src, a, a + CAP)
-                order("g", [v], [])
-                rid, pid, _ = topo.addr(cores[peers[e]])
                 o = T[dst][:, b:b + CAP]
-                trs.append(RemoteDMATransfer(dst_ids=[DstId(rid=rid, pnc=pid)], dma_engine_mask=emask(eng[k * i:k * i + k]),
-                                             remote_sem=T.sem[sem], src=v[0].bitcast(dt.uint8) if codes else v[0],
-                                             dst=o.bitcast(dt.uint8) if codes else o))
-            g.remote_dma_fused(trs, local_sem=T.sem.sent)
-            total["sent"] += len(eng)
+                rd.append(v)
+                trs.append((e, eng[k * i:k * i + k], sem, v[0].bitcast(dt.uint8) if codes else v[0], o.bitcast(dt.uint8) if codes else o))
+            prev = [remote(trs, rd, ("rows", 16 * len(es), CAP * (4 if codes else 1)), prev)]
         a, b = CAP * es[0], CAP * es[-1] + CAP
-        landed(sem, 2 * len(eng), [V(lq, a, b), V(lp, a, b)])
+        landed(sem, 2 * len(eng), [V(lq, a, b), V(lp, a, b)], prev)
+        return prev
 
-    fill(V("lvl"), 2)
-    fill(V("one"), 1.0)
+    def send_whole(a, lq, lp, sem):
+        prev = []
+        for e in range(3):
+            b, vq_, vp_ = M * slot_at[e], V("yq", a, a + M), V("yp", a, a + M)
+            prev = [remote([(e, eng, sem + str(slot_at[e]), vq_[0].bitcast(dt.uint8), T[lq][:, b:b + M].bitcast(dt.uint8))], [vq_], ("rows", 16, 4 * M), prev)]
+            prev = [remote([(e, eng, sem + str(slot_at[e]), vp_[0], T[lp][:, b:b + M])], [vp_], ("rows", 16, M), prev)]
+            landed(sem + str(e), 2 * len(eng), [V(lq, M * e, M * e + M), V(lp, M * e, M * e + M)], prev)
+        return prev
+
+    fill(V("lvl"), 7)
     for a in range(4):
-        o = V("lvl", p=(32 * a, 32 * a + 30, 1))
-        dma("y" if a % 2 == 0 else "s", "dlv", o[0], T.lv[:], [], [o])
-    dma("y", "dx", T.xs[:], T.x[:], [], [V("xs")])
+        o = V("lvl", 0, 16, p=(32 * a, 32 * a + 30, 1))
+        last = dma("y" if a % 2 == 0 else "s", "dlv", o[0], T.lv[:], [], [o])
+    last = dma("y", "dx", T.xs[:], T.x[:], [], [V("xs")], 480, [last])
+    fill(V("one"), 1.0)
     fill(V("et"), 0.0)
     iota(V("pid"), [[0, 2]], 0, 1, False)
-    op("g", lambda: g.affine_select(T.ident[:], T.one[:], [[-1, 128]], AluOpType.is_equal, 0.0, 0, 1), [V("one")], [V("ident")])
-    iota(V("io32"), [[0, 6], [1, 32]], 0, 0)
+    o = V("et", 3, 515, 4)
+    op("g", lambda: g.affine_select(o[0], T.one[:], [[-1, 128]], AluOpType.is_equal, 0.0, 0, 1), [V("one")], [o], ("iota", 150))
+    for b in range(4):
+        quant("eq", "es", 128 * b, 128, V("et", 3 - b, 515 - b))
+    iota(V("io32", 0, 96), [[0, 3], [1, 32]], 0, 0)
+    iota(V("io32", 96, 192), [[0, 3], [1, 32]], 0, 0)
     iota(V("oti"), [[32, 6], [0, 2]], 31, 0, False)
     iota(V("io3"), [[16, 2], [1, 4]], 0, 0)
     iota(V("rw"), [[1, 16], [16, 30]], 0, 0, False)
     for k, src in ((1, T.pr0), (2, T.pr1)):
-        o = V("rw", p=(k, 128, 16))
-        dma("y", "drw", o[0], src[:], [], [o])
-    dma("y", "dw", T.wq[:].bitcast(dt.uint8), T.wc[:], [], [V("wq")])
-    dma("y", "dw", T.wp[:], T.ws[:], [], [V("wp")])
-    dma("y", "dv", T.vq[:].bitcast(dt.uint8), T.vc[:], [], [V("vq")])
-    dma("y", "dv", T.vp[:], T.vs[:], [], [V("vp")])
-    for b in range(4):
-        act(V("et", 513 * b, 512 * b + 512, 4), V("ident"))
-    act(V("keep"), V("io32"), f=ActivationFunctionType.Sign)
-    fill(V("ind", 0, 96), 0.0)
-    ts(V("pt", 0, 1), V("pid", 0, 1), 31, AluOpType.bitwise_and)
-    ts(V("pt", 1, 2), V("pid", 0, 1), 15, AluOpType.bitwise_and)
-    ts(V("pt", 2, 3), V("pid", 0, 1), 16, AluOpType.bitwise_and)
+        o_ = V("rw", p=(k, 128, 16))
+        last = dma("y", "drw", o_[0], src[:], [], [o_])
+    fill(V("keep"), 1.0)
+    fill(V("keep", 0, 192, 32), 0.0)
+    ts(V("pt", 0, 1), V("pid", 0, 1), 31, AND)
+    ts(V("pt", 1, 2), V("pid", 0, 1), 15, AND)
+    ts(V("pt", 2, 3), V("pid", 0, 1), 16, AND)
     cp(V("ot"), V("oti"))
-    cp(V("pf", 0, 3), V("pt", 0, 3))
+    cp(V("pf", 0, 1), V("pt", 0, 1))
+    cp(V("pf", 1, 3), V("pt", 1, 3))
     ts(V("m32"), V("io32", 0, 96), V("pf", 0, 1), AluOpType.is_gt)
     ts(V("sel", 0, 4), V("io3", 0, 4), V("pf", 1, 2), AluOpType.is_equal)
     ts(V("sel", 4, 6), V("io3", 0, 8, 4), V("pf", 2, 3), AluOpType.is_equal)
-    quant("eq", "es", 0, 512, V("et"))
-    act(V("sw"), V("et", 0, 960), 0.0)
-    act(V("tab", 0, 2048), V("et"), 0.0)
-    act(V("tab", 2048, TABW), V("et", 0, TABW - 2048), 0.0)
+    zero("sw", 960)
+    zero("tab", TABW)
+    act(V("tab", 0, 1), V("sel", 0, 1), -200.0)
     iota(V("io16"), [[0, 2], [16, 32]], 0, 0)
     iota(V("io1"), [[1, NS]], 1, 0)
     for a in (0, 32):
-        iota(V("k160", a, a + 20), [[M, 2], [0, 10]], -1001, 0)
+        iota(V("kc", a, a + 20), [[2 * M, 2], [0, 10]], -640, 0)
+    m1, m2 = new(192), new(192)
     act(V("col", 0, 1), V("pf", 2, 3), -0.5, -8.0)
     act(V("col", 1, 2), V("pf", 2, 3), 0.5, 7.5)
     act(V("col", 2, 3), V("pf", 0, 1), -0.5, V("col", 0, 1))
     act(V("col", 3, 4), V("pf", 0, 1), -0.5, V("col", 1, 2))
     act(V("col", 8, 9), V("pf", 1, 2), 1.0, 384.0)
     act(V("col", 9, 10), V("pf", 1, 2), 1.0, 1280.0)
-    act(V("cuc"), V("io32"), 1.0, V("col", 2, 3), ActivationFunctionType.Abs)
+    act(V(m1), V("io32"), 1.0, V("col", 2, 3), ActivationFunctionType.Abs)
     act(V("dmp", 0, 64), V("io16"), 1.0, V("col", 8, 9))
-    act(V("tr2"), V("cuc"), -1.0, V("col", 3, 4), ActivationFunctionType.Sign)
+    act(V(m2), V(m1), -1.0, V("col", 3, 4), ActivationFunctionType.Sign)
     act(V("dmp", 64, 128), V("io16"), 1.0, V("col", 9, 10))
-    act(V("m16"), V("tr2"), f=ActivationFunctionType.Relu)
-    act(V("iw2", 0, 384), V("et", 0, 384), 0.0)
-    act(V("kp", 0, M), V("io1", 0, M), V("sel", 1, 2))
-    act(V("kp", M, 2 * M), V("io1", 0, M), V("sel", 1, 2), V("sel", 2, 3))
+    act(V("m16"), V(m2), f=ActivationFunctionType.Relu)
+    zero("iw2", 384)
+    zero("iw1", 384)
+    zero("bw", 1280)
+    act(V("col", 10, 11), V("sel", 2, 3), 162.0)
+    act(V("col", 11, 12), V("sel", 2, 3), 482.0)
+    act(V("kp", 0, M), V("io1", 0, M), V("sel", 1, 2), V("col", 10, 11))
+    act(V("kp", M, 2 * M), V("io1", 0, M), V("sel", 1, 2), V("col", 11, 12))
+    act(V("wf", 0, 4 * PF, PF), V("et", 0, 4), 0.0)
+    act(V("wb", 0, 4 * PB_, PB_), V("et", 0, 4), 0.0)
+    fill(V("rl1"), 0)
+    for i, c in enumerate((M, M + NS, 2 * M + NS)):
+        act(V("col", 5 + i, 6 + i), V("sel", 1, 2), float(c))
 
-    def ranks_in_class(mask, n):
-        def W(name):
-            return V(name, 0, n)
-        scan(W("cum"), W("ind"), n)
-        ttg(W("bc"), W("cum"), V("ot", 0, n // 16), W(mask), mul)
-        if n > 96:
-            for e in range(3):
-                act(V("cuc", 64 * e, 64 * e + 64), V("cum", 64 * e, 64 * e + 64), 1.0, float(CAP * e))
-        trn(W("tr"), W("bc"))
-        scan(W("sc"), W("tr"), n)
-        ttg(W("pp"), W("sc"), V("ot", 0, n // 16), W("cuc" if n > 96 else "cum"), add)
-        tt(W("pd"), W("pp"), W("ind"), mul)
-
-    for l in range(3):
-        ts(V("ind", 32 * l, 32 * l + 16), V("lvl"), l, AluOpType.is_equal)
-    ts(V("t3", 0, 16), V("lvl"), M, mul, -1, add)
-    ranks_in_class("m32", 96)
-    tt(V("t1", 0, 16), V("pd", 0, 16), V("pd", 32, 48), add)
-    tt(V("t2", 0, 16), V("pd", 64, 80), V("t3", 0, 16), add)
-    tt(V("tc30"), V("pd", 0, 16), V("pd", 32, 48), sub)
-    tt(V("i1", 0, 16), V("t1", 0, 16), V("t2", 0, 16), add)
-    v = V("tc30")
-    fused("atab", [(v, v[0], T["td%d" % slot_at[e]][:]) for e in range(3)], first)
-    for p0 in (0, 16):
-        o = V("tab", 32 + 512 * rank, 32 + 512 * rank + 512, p=(p0, 128, 32))
-        dma("y", "dtab", o[0], v[0], [v], [o])
-    ts(V("i2", 0, 16), V("i1", 0, 16), 496, AluOpType.bitwise_and)
-    ts(V("i1", 16, 32), V("i1", 0, 16), 16, add)
-    tt(V("t4", 0, 16), V("i1", 0, 16), V("i2", 0, 16), add)
-    tt(V("t4", 16, 32), V("i1", 16, 32), V("i2", 0, 16), add)
-    trn(V("t4", 32, 64), V("t4", 0, 32))
-    quant("sq", "ss", 0, C, V("xs"))
-    cp(V("ofs"), V("t4", 32, 64))
-    cp(V("vu"), V("i1", 0, 16))
-    sca(V("sw"), V("ofs", 0, 30), V("rw"))
-    dma("y", "dpd", T.pdr[:], T.vu[:], [V("vu")], [V("pdr")])
-    landed("atab", len(eng), [V("td0"), V("td1"), V("td2")])
-    for e in range(3):
-        for p0 in (0, 16):
-            a = 32 + 512 * peers[e]
-            o = V("tab", a, a + 512, p=(p0, 128, 32))
-            dma("y", "dtab", o[0], T["td%d" % e][:], [V("td%d" % e)], [o])
-    trn(V("swt", 0, 320), V("sw", 0, 320))
-    tt(V("t1", 0, 10), V("swt", 0, 320, 32), V("swt", 16, 320, 32), add)
-    cp(V("sig", 0, 10), V("t1", 0, 10))
-    pick("pq", "pss", "sq", "ss", C, "sig", 0, M)
-
-    def evac(bank0, tile, c, who="svsv"):
+    def evac(bank0, tile, c, who="svsv", n=M):
         for b in range(4):
-            scaled(who[b], V(tile, b, 4 * M, 4), V("ps", 512 * (bank0 + b), 512 * (bank0 + b) + M), c)
+            scaled(who[b], V(tile, b, 4 * n, 4), V("ps", 512 * (bank0 + b), 512 * (bank0 + b) + n), c)
 
     def to_window(win, pitch, a, n, who, skip=0):
         for b in range(4):
             if who[b] != "-":
                 scaled(who[b], V(win, pitch * b + a, pitch * b + a + n), V("ps", 512 * b + skip, 512 * b + skip + n), -0.5)
 
-    def places():
-        for l in (1, 2):
-            for k in (0, 1):
-                a = 32 * (l - 1) + 10 * k
-                tt(V("pri", a, a + 10), V("swt", 320 * l + 1 + k, 320 * l + 320, 32), V("swt", 320 * l + 17 + k, 320 * l + 320, 32), add)
-        tt(V("t2", 0, 20), V("swt", 320, 960, 32), V("swt", 336, 960, 32), add)
-        ts(V("idx"), V("pri"), -(C - 1) / 2.0, add, 1.0 / C, mul)
-        ts(V("i1"), V("pri"), 15, AluOpType.bitwise_and)
-        ts(V("i2"), V("pri"), 4, AluOpType.arith_shift_right)
-        cp(V("si"), V("idx"))
-        ts(V("t1"), V("i1"), 30, mul, 32, add)
-        cp(V("sig", 10, 30), V("t2", 0, 20))
-        ts(V("t3"), V("si"), 512 - 30, mul)
-        tt(V("t4"), V("t1"), V("i2"), add)
-        for e in range(3):
-            ts(V("ind", 64 * e, 64 * e + 64), V("si"), peers[e], AluOpType.is_equal)
-        tt(V("idx"), V("t3"), V("t4"), add)
-        pick("pq", "pss", "sq", "ss", C, "sig", M, M, "s")
-        scan(V("cum"), V("ind"), 192)
-        ts(V("id2", 0, 128, 2), V("idx"), 0.0, mx_, V("sel", 4, 5), mul)
-        ts(V("id2", 1, 128, 2), V("idx"), 0.0, mx_, V("sel", 5, 6), mul)
+    quant("sq", "ss", 0, C, V("xs"))
+    four(4, "eq", "es", "sq", "ss", 0, C)
+    evac(4, "xa", 1.0, "ssss", C)
+    quant("xaq", "xap", 0, C, V("xa"))
 
-    four(4, "eq", "es", "pq", "pss", 0, M)
-    trn(V("swt", 320, 640), V("sw", 320, 640))
-    evac(4, "xt", 1.0)
-    fill(V("pri"), -1)
-    quant("xq", "xp", 0, M, V("xt"))
-    four(0, "wq", "wp", "xq", "xp", 0, M)
-    trn(V("swt", 640, 960), V("sw", 640, 960))
+    for l in range(3):
+        ts(V("ind0", 32 * l, 32 * l + 32), V("lvl"), l, AluOpType.is_equal)
+    a1, a2, a3, a4, pp0, pd0, j1, j2 = new(16), new(16), new(16), new(64), new(96), new(96), new(32, "ti"), new(16, "ti")
+    ts(V(a3), V("lvl", 0, 16), M, mul, -1, add)
+    scan(V("cum0"), V("ind0"), 96)
+    ttg(V("bc0"), V("cum0"), V("ot", 0, 6), V("m32"), mul)
+    trn(V("tr0"), V("bc0"))
+    scan(V("sc0"), V("tr0"), 96)
+    ttg(V(pp0), V("sc0"), V("ot", 0, 6), V("cum0"), add)
+    tt(V(pd0), V(pp0), V("ind0"), mul)
+    tt(V(a1), V(pd0, 0, 16), V(pd0, 32, 48), add)
+    tt(V(a2), V(pd0, 64, 80), V(a3), add)
+    tt(V(j1, 0, 16), V(a1), V(a2), add)
+    ts(V("tc30"), V(j1, 0, 16), -float(M), add)
+    v = V("tc30", p=(0, 32, 1))
+    tdv = [(None, "td", 1, 1 << r, 0) for r in range(4)]
+    last = dma("y", "dtd", T.td[rank], v[0], [v], [tdv[rank]])
+    last = dma("y", "dw", T.wq[:].bitcast(dt.uint8), T.wc[:], [], [V("wq")], 256, [last])
+    last = dma("y", "dw", T.wp[:], T.ws[:], [], [V("wp")], 64, [last])
+    r_ = remote([(e, first[e], "atab", T.td[rank], T.td[rank]) for e in range(3)], [tdv[rank]], ("table", 0))
+    landed("atab", len(eng), [tdv[s] for s in peers], [r_])
+    for gr in range(8):
+        o_ = V("tab", 32, TABW, p=(16 * gr, 16 * gr + 1, 1))
+        dma("y", "dtab", o_[0], T.td[:], tdv, [o_])
+    ts(V(j2), V(j1, 0, 16), 496, AND)
+    tt(V(a4, 0, 16), V(j1, 0, 16), V(j2), add)
+    ts(V(a4, 16, 32), V(a4, 0, 16), 16.0, add)
+    trn(V(a4, 32, 64), V(a4, 0, 32))
+    cp(V("ofs"), V(a4, 32, 64))
+    cp(V("vu"), V(j1, 0, 16))
+    sca(V("sw"), V("ofs", 0, 30), V("rw"))
+    dma("y", "dpd", T.pdr[:], T.vu[:], [V("vu")], [V("pdr")], 4, [r_])
+    b1 = new(30)
+    trn(V("swt", 0, 320), V("sw", 0, 320))
+    tt(V(b1, 0, 10), V("swt", 0, 320, 32), V("swt", 16, 320, 32), add)
+    cp(V("sig", 0, 10), V(b1, 0, 10))
+
+    pick("x0q", "x0p", 0, "xaq", "xap", C, "sig", 0, M)
+    four(0, "wq", "wp", "x0q", "x0p", 0, M)
     evac(0, "tl", 0.03125)
-    fill(V("wf", 0, 4 * PF, PF), 0.0)
     quant("yq", "yp", 0, M, V("tl"))
-    for e in range(3):
-        rid, pid, _ = topo.addr(cores[peers[e]])
-        b = M * slot_at[e]
-        sem = "aa%d" % slot_at[e]
-        order("g", [V("yq", 0, M), V("yp", 0, M)], [])
-        g.remote_dma(T.laq[:, b:b + M].bitcast(dt.uint8), T.yq[:, 0:M].bitcast(dt.uint8), T.sem[sem], T.sem.sent, pid, rid, emask(eng))
-        g.remote_dma(T.lap[:, b:b + M], T.yp[:, 0:M], T.sem[sem], T.sem.sent, pid, rid, emask(eng))
-        total["sent"] += 2 * len(eng)
-        landed("aa%d" % e, 2 * len(eng), [V("laq", M * e, M * e + M), V("lap", M * e, M * e + M)])
+    send_whole(0, "laq", "lap", "aa")
     four(0, "eq", "es", "yq", "yp", 0, M)
     to_window("wf", PF, 1 + M * rank, M, "ssss")
-    places()
 
-    def scatter_places(out, high, dump):
-        ts(V("i2"), V("i1"), high, AluOpType.bitwise_and)
-        ts(V("t1"), V("i1"), V("pf", 2, 3), add)
-        tt(V("t2"), V("t1"), V("i2"), add)
-        tt(V("t1"), V("t2"), dump, AluOpType.min)
-        cp(V(out), V("t1"))
-
-    def slots():
-        ttg(V("bc"), V("cum"), V("ot"), V("m16"), mul)
-        for e in range(3):
-            act(V("cuc", 64 * e, 64 * e + 64), V("cum", 64 * e, 64 * e + 64), 1.0, float(CAP * e))
-        gat("s", V("g2a"), V("tab"), V("id2", 0, 40))
-        cp(V("idc"), V("idx"))
-        trn(V("tr"), V("bc"))
-        ts(V("s160"), V("si"), M, mul)
-        scan(V("sc"), V("tr"), 192)
-        ts(V("ko"), V("si"), rank, AluOpType.is_equal, 1000.0, mul)
-        ttg(V("pp"), V("sc"), V("ot"), V("cuc"), add)
-        tt(V("pd"), V("pp"), V("ind"), mul)
-        tt(V("t1"), V("pd", 0, 64), V("pd", 64, 128), add)
-        tt(V("qq"), V("t1"), V("pd", 128, 192), add)
-        ts(V("i1"), V("qq"), -1.0, add)
-        scatter_places("iof", 1008, V("dmp", 0, 64))
-
-    def one_list(out, src, c1):
-        ts(V("t4", 0, 12), src, c1, mul, -1.0, add)
-        cp(out, V("t4", 0, 12))
-
-    def codes_of(l):
-        trn(V("g2t"), V("g2a" if l == 1 else "g2b"))
-        yield
-        tt(V("tca", 32 * l - 32, 32 * l - 12), V("g2t", 0, 640, 32), V("g2t", 16, 640, 32), add)
-        yield
-
-    def requests(l):
-        iw, rq, rl, a = "iw%d" % l, "rq%d" % l, "rl%d" % l, 32 * (l - 1)
-        ttg(V("gc"), V("tab"), V("idc", a, a + 20), V("kp"), add)
-        yield
-        sca(V(iw), V("iof", a, a + 20), V("gc"))
-        yield
-        trn(V("iwt"), V(iw, 0, 384))
-        yield
-        tt(V(rq, 0, 24, 2), V("iwt", 0, 384, 32), V("iwt", 16, 384, 32), add)
-        tt(V(rq, 1, 24, 2), V("iwt", 2, 384, 32), V("iwt", 18, 384, 32), add)
-        tt(V("t5", a, a + 12), V("iwt", 1, 384, 32), V("iwt", 17, 384, 32), add)
-        prs = []
-        for e in range(3):
-            v_ = V(rq, 8 * e, 8 * e + 8)
-            prs.append((v_, v_[0], T[rl][:, 8 * slot_at[e]:8 * slot_at[e] + 8]))
-        fused("ar%d" % l, prs, first)
-        landed("ar%d" % l, len(eng), [V(rl)])
-        yield
-
-    def front2():
-        ts(V("t6", 0, 20), V("qq", 32, 52), 0.0, AluOpType.is_gt, float(5 * M), mul)
-        for _ in codes_of(2):
-            yield
-        tc = V("tca", 32, 52)
-        tt(V("t6", 32, 52), V("t6", 0, 20), V("qq", 32, 52), add)
-        ts(V("t3", 0, 20), tc, -1.0, mul, float(4 * M), add)
-        ts(V("t3", 32, 52), tc, 0.0, AluOpType.is_lt)
-        tt(V("t2", 0, 20), tc, V("s160", 32, 52), add)
-        yield
-        tt(V("t6", 0, 20), V("t3", 0, 20), V("t6", 32, 52), mx_)
-        yield
-        tt(V("t3", 0, 20), V("t6", 0, 20), V("t3", 32, 52), mul)
-        yield
-        tt(V("t6", 0, 20), V("t3", 0, 20), V("t2", 0, 20), mx_)
-        yield
-        cp(V("fr2"), V("t6", 0, 20))
-        yield
-
-    def weave(*gens):
-        gens = list(gens)
-        while gens:
-            for x in list(gens):
-                if next(x, 1) == 1:
-                    gens.remove(x)
-
-    def successor_places():
-        for l in (1, 2):
-            a, rl = 32 * l - 12, "rl%d" % l
-            cp(V("tca", a, a + 12), V(rl, 0, 24, 2))
-            ts(V("k160", a, a + 12), V(rl, 1, 24, 2), M, mul, -1.0, add)
-        yield
-        ts(V("t1"), V("tca"), -2.0, mul, 2.0 * M, add)
-        ts(V("t2"), V("tca"), 0.0, AluOpType.is_lt)
-        ts(V("bs", 12, 24), V("t5", 32, 44), -1.0, add, 0.0, mx_)
-        yield
-        tt(V("t4"), V("tca"), V("k160"), add)
-        tt(V("t3"), V("t1"), V("t2"), mul)
-        yield
-        tt(V("t6"), V("t4"), V("ko"), add)
-        tt(V("i1"), V("t3"), V("t6"), add)
-        scatter_places("bof", 4080, V("dmp", 64, 128))
-        yield
-
-    def successors(l, out, between=None):
-        a = 32 * l - 32
-        if between:
-            sca(V("bw"), V("bof", a + 20, a + 32), V("pb%d" % l, 2 * M, 512))
-            between()
-            sca(V("bw"), V("bof", a, a + 20), V("pb%d" % l, 0, 2 * M))
+    pri, si, i1, i2 = new(64, "ti"), new(64, "ti"), new(64, "ti"), new(64, "ti")
+    idx, idy, c1, c3, c4, s160, ko, tca = [new(64) for _ in range(8)]
+    trn(V("swt", 320, 640), V("sw", 320, 640))
+    trn(V("swt", 640, 960), V("sw", 640, 960))
+    fill(V(pri), -1)
+    for l in (1, 2):
+        for k in (0, 1):
+            a = 32 * (l - 1) + 10 * k
+            tt(V(pri, a, a + 10), V("swt", 320 * l + 1 + k, 320 * l + 320, 32), V("swt", 320 * l + 17 + k, 320 * l + 320, 32), add)
+    tt(V(b1, 10, 30), V("swt", 320, 960, 32), V("swt", 336, 960, 32), add)
+    cp(V("sig", 10, 30), V(b1, 10, 30))
+    ts(V(idx), V(pri), -(C - 1) / 2.0, add, 1.0 / C, mul)
+    ts(V(i1), V(pri), 15, AND)
+    ts(V(i2), V(pri), 4, SHR)
+    cp(V(si), V(idx))
+    ts(V(c1), V(i1), 30, mul, 32, add)
+    ts(V(c3), V(si), 512 - 30, mul)
+    tt(V(c4), V(c1), V(i2), add)
+    tt(V(idy), V(c3), V(c4), add)
+    ts(V("id2", 0, 128, 2), V(idy), 0.0, mx_, V("sel", 4, 5), mul)
+    ts(V("id2", 1, 128, 2), V(idy), 0.0, mx_, V("sel", 5, 6), mul)
+    ts(V(s160), V(si), M, mul, 361.0, add)
+    cp(V("idc"), V(idy))
+    for l, gb_ in ((1, "g2a"), (2, "g2b")):
+        a, w0 = 32 * (l - 1), 640 * (l - 1)
+        gat("s", V(gb_), V("tab"), V("id2", 2 * a, 2 * a + 40))
+        trn(V("g2t", w0, w0 + 640), V(gb_))
+        tt(V(tca, a, a + 20), V("g2t", w0, w0 + 640, 32), V("g2t", w0 + 16, w0 + 640, 32), add)
+        d1, d2, d3 = new(20), new(20), new(20)
+        tt(V(d1), V(tca, a, a + 20), V(s160, a, a + 20), add)
+        if l == 1:
+            cp(V("fr1"), V(d1))
         else:
-            sca(V("bw"), V("bof", a, a + 32), V("pb%d" % l))
-        a = 640 * (l - 1)
-        trn(V("g2t"), V("bw", a, a + 640))
-        tt(V("t1", 0, 40), V("g2t", 0, 640, 16), V("g2t", 1, 640, 16), add)
-        tt(V("t3", 0, 20), V("t1", 0, 40, 2), V("t1", 1, 40, 2), add)
-        cp(V(out), V("t3", 0, 20))
+            ts(V(d2), V(tca, a, a + 20), -200.0, AluOpType.is_ge, float(3 * M), mul)
+            tt(V(d3), V(d1), V(d2), add)
+            cp(V("fr2"), V(d3))
+    pick("pq", "pss", 0, "sq", "ss", C, "sig", 10, M)
+
+    def scatter_places(out, src, a, n, high, dump):
+        e2, e1, e3, e4 = new(n, "ti"), new(n), new(n), new(n)
+        ts(V(e2), src, high, AND)
+        ts(V(e1), src, V("pf", 2, 3), add)
+        tt(V(e3), V(e1), V(e2), add)
+        tt(V(e4), V(e3), dump, AluOpType.min)
+        cp(V(out, a, a + n), V(e4))
+
+    for e in range(3):
+        ts(V("ind", 64 * e, 64 * e + 64), V(si), peers[e], AluOpType.is_equal)
+    scan(V("cum"), V("ind"), 192)
+    ttg(V("bc"), V("cum"), V("ot"), V("m16"), mul)
+    for e in range(3):
+        act(V("cuc", 64 * e, 64 * e + 64), V("cum", 64 * e, 64 * e + 64), 1.0, float(CAP * e))
+    trn(V("tr"), V("bc"))
+    scan(V("sc"), V("tr"), 192)
+    ts(V(ko), V(si), rank, AluOpType.is_equal, 1000.0, mul)
+    ttg(V("pp"), V("sc"), V("ot"), V("cuc"), add)
+    tt(V("pd"), V("pp"), V("ind"), mul)
+    f1, f2, f3 = new(64), new(64), new(64, "ti")
+    tt(V(f1), V("pd", 0, 64), V("pd", 64, 128), add)
+    ts(V(f2), V("pd", 128, 192), -1.0, add)
+    tt(V(f3), V(f1), V(f2), add)
+    scatter_places("iof", V(f3), 0, 64, 1008, V("dmp", 0, 64))
+
+    def requests(l, after):
+        iw, rq, rl, a, w0 = "iw%d" % l, "rq%d" % l, "rl%d" % l, 32 * (l - 1), 384 * (l - 1)
+        gc = V("gc", 320 * (l - 1), 320 * l)
+        ttg(gc, V("tab"), V("idc", a, a + 20), V("kp"), add)
+        sca(V(iw), V("iof", a, a + 20), gc)
+        trn(V("iwt", w0, w0 + 384), V(iw, 0, 384))
+        n1, n2, n3, n4 = new(12), new(12), new(12, "ti"), new(12)
+
+        def row(k):
+            return V("iwt", w0 + k, w0 + 384, 32)
+        tt(V(n1), row(0), row(16), add)
+        tt(V(n2), row(2), row(18), add)
+        tt(V(n3), V(n1), V(n2), add)
+        tt(V(n4), row(1), row(17), add)
+        ts(V("bs", 12 * (l - 1), 12 * l), V(n4), -1.0, add, 0.0, mx_)
+        k = 4
+        if l == 1:
+            k, m_ = 3, new(12, "ti")
+            ts(V(m_, 0, 3), V(n3, 3, 12, 4), 512.0, mul)
+            ts(V(m_, 4, 7), V(m_, 0, 3), 127 * 512, AND)
+            ts(V(m_, 8, 11), V(m_, 0, 3), 7, SHR, 127 * 512, AND)
+            tt(V(n3, 0, 12, 4), V(n3, 0, 12, 4), V(m_, 4, 7), add)
+            tt(V(n3, 1, 12, 4), V(n3, 1, 12, 4), V(m_, 8, 11), add)
+        cp(V(rq), V(n3))
+        r = remote([(e, first[e], "ar%d" % l, T[rq][:, 4 * e:4 * e + k], T[rl][:, 4 * slot_at[e]:4 * slot_at[e] + k]) for e in range(3)],
+                   [V(rq)], ("rows", 64, 2 * k), after)
+        landed("ar%d" % l, len(eng), [V(rl)], [r])
+        return [r]
+
+    def successors(l, out):
+        a, rl = 32 * l - 32, "rl%d" % l
+        pl, q1, u = new(32, "ti"), new(20), new(12, "ti")
+        tt(V(q1), V("kc", a, a + 20), V(ko, a, a + 20), add)
+        tt(V(pl, 0, 20), V(q1), V(tca, a, a + 20), add)
+        if l == 2:
+            ts(V(pl, 20, 32), V(rl, 0, 12), -2.0, add)
+        else:
+            lo, hi = new(12, "ti"), new(8, "ti")
+            cp(V(u), V(rl, 0, 12))
+            ts(V(lo), V(u), 511, AND)
+            ts(V(hi, 0, 3), V(u, 0, 12, 4), 9, SHR)
+            ts(V(hi, 4, 7), V(u, 1, 12, 4), 2, SHR, 384, AND)
+            tt(V(lo, 3, 12, 4), V(hi, 0, 3), V(hi, 4, 7), add)
+            ts(V(pl, 20, 32), V(lo), -2.0, add)
+        scatter_places("bof", V(pl), a, 32, 4080, V("dmp", 64 + a, 96 + a))
+        sca(V("bw"), V("bof", a, a + 20), V("pb%d" % l, 0, 2 * M))
+        sca(V("bw"), V("bof", a + 20, a + 32), V("pb%d" % l, 2 * M, 512))
+        w0 = 1280 + 640 * (l - 1)
+        for k in range(2):
+            s0 = 320 * (l - 1) + 640 * k
+            trn(V("g2t", w0 + 320 * k, w0 + 320 * k + 320), V("bw", s0, s0 + 320))
+        q2, q3 = new(40), new(20)
+        tt(V(q2), V("g2t", w0, w0 + 640, 16), V("g2t", w0 + 1, w0 + 640, 16), add)
+        tt(V(q3), V(q2, 0, 40, 2), V(q2, 1, 40, 2), add)
+        cp(V(out), V(q3))
 
     def payload(name, own, far):
         for a, n, c in ((0, M, own), (M, M, own), (2 * M, NS, far)):
@@ -536,146 +507,153 @@ def rank_program(g, core, T, topo):
             else:
                 act(V(name, a, a + n), V("io1", 0, n), V("sel", 0, 1), c)
 
-    def make(win, pitch, wn, a, n, lst, lq, lp, between=None, early=False):
+    def layer(lq, lp):
+        quant("xq", "xp", 0, M, V("xt"))
+        four(0, lq, lp, "xq", "xp", 0, M)
+
+    def make(win, pitch, wn, a, n, skip, lst, lq, lp):
         def w(b):
             return V(win, pitch * b, pitch * b + wn)
-
-        def ga(b, q):
-            gat(q, V("ab", M * b, M * b + M), w(b), V(lst, 0, 10))
-
-        def gb(b):
+        for b in range(4):
+            to_window(win, pitch, a, n, "-" * b + "vsss"[b] + "-" * (3 - b), skip)
+            gat("vsss"[b], V("ab", M * b, M * b + M), w(b), V(lst, 0, 10))
+        for b in range(4):
             ttg(V("sm", M * b, M * b + M), w(b), V(lst, 10, 20), V("ab", M * b, M * b + M), add)
-
-        def fin(b):
             tt(V("xt", b, 4 * M, 4), V("ps", 512 * (4 + b), 512 * (4 + b) + M), V("sm", M * b, M * b + M), add)
-        if early:
-            for b in range(4):
-                to_window(win, pitch, a, n, "-" * b + "s" + "-" * (3 - b))
-                ga(b, "s")
-            gat("s", V("g2b"), V("tab"), V("id2", 64, 104))
-        else:
-            to_window(win, pitch, a, n, "vs--", CAP)
-            ga(0, "v")
-            ga(1, "s")
-            to_window(win, pitch, a, n, "--s-", CAP)
-            ga(2, "s")
-            to_window(win, pitch, a, n, "---s", CAP)
-            ga(3, "s")
-        gb(0)
-        gb(1)
-        fin(0)
-        gb(2)
-        fin(1)
-        gb(3)
-        fin(2)
-        fin(3)
-        layer(lq, lp, between)
+        layer(lq, lp)
 
     def arrive(lq, lp, win, pitch, a):
         four(0, "eq", "es", lq, lp, 0, 2 * CAP)
         to_window(win, pitch, a, 2 * CAP, "ssss")
         four(0, "eq", "es", lq, lp, CAP, 2 * CAP)
 
-    def layer(lq, lp, between=None):
-        quant("xq", "xp", 0, M, V("xt"))
-        four(0, lq, lp, "xq", "xp", 0, M)
-        if between:
-            between()
+    def arrive_whole(lq, lp, a):
+        for e in range(3):
+            four(0, "eq", "es", lq, lp, M * e, M)
+            if e < 2:
+                to_window("wf", PF, a + M * peers[e], M, "ssss")
 
-    def pack(lst, sem, sq_, sp_, lq, lp):
+    def pack(c0, sem, sq_, sp_, lq, lp):
         for b in range(4):
             scaled("svsv"[b], V("tp", M * b, M * b + M), V("ps", 512 * b, 512 * b + M), 0.03125)
         for b in range(4):
-            gat("svsv"[b], V("st", b, 8 * CAP, 4), V("tp", M * b, M * b + M), V(lst[0], lst[1], lst[1] + 8))
+            gat("svsv"[b], V("st", b, 8 * CAP, 4), V("tp", M * b, M * b + M), V("bs", c0, c0 + 8))
         quant(sq_, sp_, 0, 2 * CAP, V("st", 0, 8 * CAP))
-        send_part(sem, sq_, sp_, lq, lp, [0, 1])
+        prev = send_part(sem, sq_, sp_, lq, lp, [0, 1], [])
         for b in range(4):
-            gat("svss"[b], V("st", 8 * CAP + b, 4 * NS, 4), V("tp", M * b, M * b + M), V(lst[0], lst[1] + 8, lst[1] + 12))
+            gat("svss"[b], V("st", 8 * CAP + b, 4 * NS, 4), V("tp", M * b, M * b + M), V("bs", c0 + 8, c0 + 12))
         quant(sq_, sp_, 2 * CAP, 2 * CAP, V("st", 4 * CAP, 4 * NS))
-        send_part(sem + "2", sq_, sp_, lq, lp, [2])
+        send_part(sem + "2", sq_, sp_, lq, lp, [2], prev)
         evac(0, "tl", 0.03125, "ssss")
 
-    slots()
-    act(V("wb", 0, 4 * PB_, PB_), V("et", 0, 4), 0.0)
-    for i, c in enumerate((M, M + NS, 2 * M + NS)):
-        act(V("col", 5 + i, 6 + i), V("sel", 1, 2), float(c))
-    for e in range(3):
-        four(0, "eq", "es", "laq", "lap", M * e, M)
-        if e < 2:
-            to_window("wf", PF, 1 + M * peers[e], M, "ssss")
-    act(V("bw", 0, 1280), V("et", 0, 1280), 0.0)
-    r2, c1 = requests(2), codes_of(1)
-    next(c1)
-    next(r2)
-    weave(c1)
-    tt(V("t3", 0, 20), V("tca", 0, 20), V("s160", 0, 20), add)
-    cp(V("fr1"), V("t3", 0, 20))
-    weave(r2)
-    pick("pq", "pss", "sq", "ss", C, "sig", M, M, "v")
-    four(4, "eq", "es", "pq", "pss", M, M)
-    make("wf", PF, 1 + 4 * M, 1 + M * peers[2], M, "fr1", "wq", "wp",
-         lambda: one_list(V("fs"), V("rl2", 0, 24, 2), -1.0), True)
-    pack(("fs", 0), "ab_", "sbq", "sbp", "lbq", "lbp")
-
-    act(V("iw1", 0, 384), V("et", 0, 384), 0.0)
-    pick("pq", "pss", "sq", "ss", C, "sig", 2 * M, M)
-    four(4, "eq", "es", "pq", "pss", 2 * M, M)
-    w1, w2 = front2(), requests(1)
-    next(w1)
-    next(w2)
+    arrive_whole("laq", "lap", 1)
+    four(4, "eq", "es", "pq", "pss", 0, M)
+    dma("y", "dv", T.vq[:].bitcast(dt.uint8), T.vc[:], [V("laq")], [V("vq")], 256)
+    dma("y", "dv", T.vp[:], T.vs[:], [V("laq")], [V("vp")], 64)
+    make("wf", PF, 1 + 4 * M, 1 + M * peers[2], M, 0, "fr1", "wq", "wp")
+    evac(0, "tl", 0.03125)
     quant("yq", "yp", M, M, V("tl"))
+    last = send_whole(M, "lbq", "lbp", "ab")
+    last = requests(2, last)
+    requests(1, last)
+
+    pick("pq", "pss", M, "sq", "ss", C, "sig", 20, M)
+    four(4, "eq", "es", "pq", "pss", M, M)
     four(0, "eq", "es", "yq", "yp", M, M)
-    to_window("wf", PF, 1 + 4 * M, M, "ssss")
-    payload("pb2", None, V("col", 5, 6))
-    weave(w1, w2)
-    arrive("lbq", "lbp", "wf", PF, 1 + 5 * M)
-    order("y", [V("lbq")], [])
-    dma("y", "du", T.us[:], T.u[:], [], [V("us")])
+    to_window("wf", PF, 1 + 4 * M + M * rank, M, "ssss")
+    arrive_whole("lbq", "lbp", 1 + 4 * M)
+    dma("y", "du", T.us[:], T.u[:], [V("lbq")], [V("us")], 128)
     for gr in range(8):
-        o = V("pij", 0, 30, p=(16 * gr, 16 * gr + 16, 1))
-        dma("y", "dpij", o[0], T.pdr[0:30, :], [V("pdr")], [o])
-    sp = successor_places()
-    make("wf", PF, 1 + 5 * M + NS, 1 + 5 * M + 2 * CAP, CAP, "fr2", "wq", "wp", lambda: next(sp))
+        o_ = V("pij", 0, 30, p=(16 * gr, 16 * gr + 16, 1))
+        dma("y", "dpij", o_[0], T.pdr[0:30, :], [V("pdr"), V("lbq")], [o_])
+    make("wf", PF, 1 + 8 * M, 1 + 4 * M + M * peers[2], M, 0, "fr2", "wq", "wp")
 
     evac(0, "tl", 0.03125)
     quant("yq", "yp", 2 * M, M, V("tl"))
     four(4, "eq", "es", "yq", "yp", 2 * M, M)
-    next(sp)
     evac(4, "xt", 1.0)
-    layer("vq", "vp", lambda: next(sp))
-    pack(("bs", 12), "ac_", "scq", "scp", "lcq", "lcp")
+    layer("vq", "vp")
+    pack(12, "ac_", "scq", "scp", "lcq", "lcp")
 
-    weave(sp)
     four(4, "eq", "es", "yq", "yp", M, M)
     quant("zq", "zp", 2 * M, M, V("tl"))
     four(0, "eq", "es", "zq", "zp", 2 * M, M)
     to_window("wb", PB_, 1, M, "ssss")
+    payload("pb2", None, V("col", 5, 6))
     successors(2, "br1")
-    payload("pb1", V("col", 6, 7), V("col", 7, 8))
     arrive("lcq", "lcp", "wb", PB_, 1 + M)
-    make("wb", PB_, 1 + M + NS, 1 + M + 2 * CAP, CAP, "br1", "vq", "vp",
-         lambda: ts(V("bs", 0, 12), V("t5", 0, 12), -1.0, add, 0.0, mx_))
-    pack(("bs", 0), "ad_", "sdq", "sdp", "ldq", "ldp")
+    make("wb", PB_, 1 + M + NS, 1 + M + 2 * CAP, CAP, CAP, "br1", "vq", "vp")
+    pack(0, "ad_", "sdq", "sdp", "ldq", "ldp")
 
     four(4, "eq", "es", "yq", "yp", 0, M)
-    successors(1, "br0", lambda: (quant("zq", "zp", M, M, V("tl")), four(0, "eq", "es", "zq", "zp", M, M),
-                                  to_window("wb", PB_, 1 + M + NS, M, "ssss")))
+    quant("zq", "zp", M, M, V("tl"))
+    four(0, "eq", "es", "zq", "zp", M, M)
+    to_window("wb", PB_, 1 + M + NS, M, "ssss")
+    payload("pb1", V("col", 6, 7), V("col", 7, 8))
+    successors(1, "br0")
     arrive("ldq", "ldp", "wb", PB_, 1 + 2 * M + NS)
-    make("wb", PB_, 1 + 2 * M + 2 * NS, 1 + 2 * M + NS + 2 * CAP, CAP, "br0", "vq", "vp",
-         lambda: quant("uq", "up", 0, 128, V("us")))
+    make("wb", PB_, 1 + 2 * M + 2 * NS, 1 + 2 * M + NS + 2 * CAP, CAP, CAP, "br0", "vq", "vp")
+    quant("uq", "up", 0, 128, V("us"))
     evac(0, "tl", 0.03125)
 
     quant("zq", "zp", 0, M, V("tl"))
     halves = ((0, 256), (256, 224))
-    for a, n in halves:
-        pick("oq", "op", "zq", "zp", C, "pij", a, n)
     for i, (a, n) in enumerate(halves):
+        pick("oq", "op", a, "zq", "zp", C, "pij", a // 16, n)
         mm(4 + i, "uq", "up", 0, "oq", "op", a, n)
-    dma("y", "dout", T.oc[:], T.oq[:].bitcast(dt.uint8), [V("oq")], [])
     for i, (a, n) in enumerate(halves):
         scaled("vs"[i], V("yo", a, a + n), V("ps", 512 * (4 + i), 512 * (4 + i) + n), 1.0)
+    dma("y", "dout", T.oc[:], T.oq[:].bitcast(dt.uint8), [V("oq")], [], 240)
+    dma("s", "dout", T.y[:], T.yo[:], [V("yo")], [], 240)
     for k in range(4):
         dma("y", "dout", T.osc[4 * k:4 * k + 4, :], T.op[32 * k:32 * k + 4, :], [V("op")], [])
-    dma("s", "dout", T.y[:], T.yo[:], [V("yo")], [])
+
+    group = {}
+    for i, o_ in enumerate(ops):
+        if o_["kind"] == "d":
+            group.setdefault(o_["sem"], []).append(i)
+    for i, o_ in enumerate(ops):
+        for j in list(o_["deps"]):
+            if ops[j]["kind"] == "d" and j not in o_["soft"]:
+                assert ops[j]["sem"] != o_["sem"]
+                o_["deps"].update(group[ops[j]["sem"]])
+    order = ORDER
+    assert sorted(order) == list(range(len(ops)))
+    total, known, token = {}, {q: {} for q in queues}, {}
+    for o_ in ops:
+        if o_["kind"] != "c":
+            total[o_["sem"]] = total.get(o_["sem"], 0) + o_["n"]
+
+    def need(q, sem, cnt, snap):
+        k = known[q]
+        if k.get(sem, 0) >= cnt:
+            return
+        queues[q].wait_ge(T.sem[sem], cnt)
+        k[sem] = cnt
+        for s_, c_ in snap.items():
+            if k.get(s_, 0) < c_:
+                k[s_] = c_
+
+    place = {i: k for k, i in enumerate(order)}
+    for i in order:
+        o_ = ops[i]
+        q = o_["q"]
+        assert all(place[j] < place[i] for j in o_["deps"])
+        if o_["kind"] == "l":
+            token[i] = (o_["sem"], o_["n"], {})
+            continue
+        for j in sorted(o_["deps"], key=lambda j: -place[j]):
+            if j not in o_["soft"]:
+                need(q, *token[j])
+        if o_["kind"] == "c":
+            sem = csem[q]
+            o_["fn"]().then_inc(T.sem[sem], 1)
+            total[sem] = total.get(sem, 0) + 1
+            token[i] = (sem, total[sem], dict(known[q]))
+        elif o_["kind"] == "d":
+            o_["fn"]().then_inc(T.sem[o_["sem"]], 16)
+            token[i] = (o_["sem"], total[o_["sem"]], dict(known[q]))
+        else:
+            o_["fn"]()
     for sem in total:
-        need("g", (sem, None, {}))
+        need("g", sem, total[sem], {})

@@ -1,10 +1,14 @@
 from concourse.bass import DstId, RemoteDMATransfer
-from concourse.mybir import dt, AluOpType, ActivationFunctionType
+from concourse.mybir import dt, AluOpType, ActivationFunctionType, AxisListType
 
 C, M, CAP = 480, 160, 64
 NS = 3 * CAP
-PF, PB_ = 1296, 768
-TABW = 32 + 4 * 512
+ZW = 128
+Z2, A2, Z1, A1, Z0 = ZW, ZW + M, ZW + M + NS, ZW + 2 * M + NS, ZW + 2 * M + 2 * NS
+S0 = 4 * NS + 16
+D0 = S0 + 3 * 512 + 2 * M + 16
+WW = D0 + 2 * M
+BIG = 4096.0
 Q4, U8, BF, F32, I32, U16 = "float8_e4m3fn_x4", "uint8", "bfloat16", "float32", "int32", "uint16"
 
 
@@ -14,41 +18,30 @@ def _sb(n, d):
 
 SCRATCH = {
     "ps": ("psum", [128, 4096], F32),
-    "xs": _sb(4 * C, BF), "sq": _sb(C, Q4), "ss": _sb(C, U8), "pq": _sb(2 * M, Q4), "pss": _sb(2 * M, U8),
-    "xa": _sb(4 * C, BF), "xaq": _sb(C, Q4), "xap": _sb(C, U8), "x0q": _sb(M, Q4), "x0p": _sb(M, U8),
-    "et": _sb(520, BF), "eq": _sb(512, Q4), "es": _sb(512, U8), "one": _sb(128, BF),
+    "xs": _sb(4 * C, BF), "sq": _sb(C, Q4), "ss": _sb(C, U8), "pq": _sb(C, Q4), "pss": _sb(C, U8),
+    "et": _sb(520, BF), "em": _sb(2 * 520, BF), "eq": _sb(1536, Q4), "es": _sb(1536, U8), "one": _sb(128, BF),
+    "zt": _sb(4 * ZW, BF),
     "wq": _sb(512, Q4), "wp": _sb(512, U8), "vq": _sb(512, Q4), "vp": _sb(512, U8),
     "us": _sb(512, BF), "uq": _sb(128, Q4), "up": _sb(128, U8),
     "xt": _sb(4 * M, BF), "xq": _sb(M, Q4), "xp": _sb(M, U8), "tl": _sb(4 * M, BF),
-    "yq": _sb(C, Q4), "yp": _sb(C, U8), "zq": _sb(C, Q4), "zp": _sb(C, U8), "oq": _sb(C, Q4), "op": _sb(C, U8),
-    "wf": _sb(4 * PF, BF), "wb": _sb(4 * PB_, BF), "ab": _sb(4 * M, F32), "sm": _sb(4 * M, F32),
+    "yq": _sb(C, Q4), "yp": _sb(C, U8), "oq": _sb(C, Q4), "op": _sb(C, U8),
+    "fq": _sb(ZW + 8 * M, Q4), "fp": _sb(ZW + 8 * M, U8), "bq": _sb(Z0 + M, Q4), "bp": _sb(Z0 + M, U8),
+    "k1q": _sb(4 * M, Q4), "k1p": _sb(4 * M, U8), "k2q": _sb(4 * M, Q4), "k2p": _sb(4 * M, U8),
+    "k3q": _sb(4 * M, Q4), "k3p": _sb(4 * M, U8), "k4q": _sb(4 * M, Q4), "k4p": _sb(4 * M, U8),
     "tp": _sb(4 * M, BF), "st": _sb(4 * NS, BF), "yo": _sb(C, F32),
-    "laq": _sb(3 * M, Q4), "lap": _sb(3 * M, U8), "lbq": _sb(3 * M, Q4), "lbp": _sb(3 * M, U8),
-    "scq": _sb(256, Q4), "scp": _sb(256, U8), "lcq": _sb(NS, Q4), "lcp": _sb(NS, U8),
-    "sdq": _sb(256, Q4), "sdp": _sb(256, U8), "ldq": _sb(NS, Q4), "ldp": _sb(NS, U8),
-    "pid": _sb(2, I32), "pt": _sb(4, I32), "pf": _sb(4, F32), "io32": _sb(192, F32), "keep": _sb(192, BF),
-    "m32": _sb(96, F32), "m16": _sb(192, F32), "oti": _sb(12, I32), "ot": _sb(12, U16),
-    "io3": _sb(8, F32), "sel": _sb(8, F32), "io16": _sb(64, F32), "dmp": _sb(128, F32), "col": _sb(16, F32),
-    "io1": _sb(NS, F32), "kp": _sb(2 * M, BF), "pb1": _sb(512, BF), "pb2": _sb(512, BF), "kc": _sb(64, F32),
-    "lvl": _sb(32, I32), "rw": _sb(C, I32), "sw": _sb(2 * C, F32), "swt": _sb(2 * C, F32),
-    "ind": _sb(192, BF), "cum": _sb(192, BF), "bc": _sb(192, BF), "tr": _sb(192, BF), "sc": _sb(192, BF),
-    "ind0": _sb(96, BF), "cum0": _sb(96, BF), "bc0": _sb(96, BF), "tr0": _sb(96, BF), "sc0": _sb(96, BF),
-    "cuc": _sb(192, F32), "pp": _sb(192, F32), "pd": _sb(192, F32),
-    "tf": _sb(3072, F32), "ti": _sb(1024, I32), "ofs": _sb(32, U16),
-    "tc30": _sb(16, BF), "vu": _sb(16, U16), "pij": _sb(32, U16), "sig": _sb(32, U16),
-    "idc": _sb(64, U16), "id2": _sb(128, U16), "tab": _sb(TABW, BF),
-    "g2a": _sb(4 * M, BF), "g2b": _sb(4 * M, BF), "g2t": _sb(16 * M, BF), "gc": _sb(4 * M, BF),
-    "iw1": _sb(704, BF), "iw2": _sb(704, BF), "iwt": _sb(768, BF), "iof": _sb(64, U16),
-    "rq1": _sb(12, U16), "rq2": _sb(12, U16), "rl1": _sb(16, U16), "rl2": _sb(16, U16),
-    "fr1": _sb(20, U16), "fr2": _sb(20, U16), "br1": _sb(20, U16), "br0": _sb(20, U16),
-    "bs": _sb(24, U16), "bw": _sb(1792, BF), "bof": _sb(64, U16),
-    "td": ("dram", [4, 128, 4], BF), "pdr": ("dram", [128, 16], U16),
+    "scq": _sb(NS, Q4), "scp": _sb(NS, U8), "sdq": _sb(NS, Q4), "sdp": _sb(NS, U8),
+    "pid": _sb(2, I32), "pt": _sb(8, I32), "col": _sb(96, F32), "cf": _sb(2048, F32), "cu": _sb(160, U16),
+    "keep": _sb(240, BF), "rj": _sb(240, F32), "kp": _sb(4 * M, BF), "pb": _sb(2 * NS, BF),
+    "lvn": _sb(32, I32), "rw": _sb(C, I32), "sw": _sb(512, F32), "swt": _sb(1024, F32),
+    "tf": _sb(4096, F32), "ti": _sb(512, I32), "tu": _sb(768, U16), "th": _sb(512, BF),
+    "tab": _sb(16 + 4 * C, BF), "lk": _sb(704, BF), "lkt": _sb(1344, BF),
+    "ww": _sb(WW, BF), "slt": _sb(4 * NS, BF), "sut": _sb(2688, BF), "rl": _sb(32, U16), "dd": _sb(2 * M, BF),
+    "td": ("dram", [4, 128, 4], BF),
 }
-SEMAPHORES = ["cv", "cs", "ct", "cg", "dlv", "dx", "drw", "dw", "dv", "du", "dtd", "dtab", "dpd", "dpij", "dout",
-              "sent", "atab", "aa0", "aa1", "aa2", "ab0", "ab1", "ab2", "ar1", "ar2", "ac_", "ad_", "ac_2", "ad_2"]
-SIZE = {Q4: 4, U8: 1, BF: 2, F32: 4, I32: 4, U16: 2}
+SEMAPHORES = ["cv", "cs", "ct", "cg", "dlv", "dx", "drw", "dw", "dv", "du", "dtd", "dtab", "dout",
+              "sent", "atab", "ac0", "as0", "ac1", "as1", "ar0", "ar1", "ac2", "as2", "ac3", "as3"]
 ORDER = [
-    0, 8, 7, 6, 4, 2, 14, 1, 3, 5, 23, 24, 9, 27, 21, 29, 22, 15, 16, 42, 18, 12, 10, 79, 81, 80, 26, 83, 84, 34, 33, 32, 58, 35, 54, 36, 37, 40, 17, 20, 19, 85, 86, 25, 87, 82, 88, 28, 90, 89, 13, 91, 11, 106, 92, 107, 108, 69, 109, 93, 94, 95, 70, 74, 73, 72, 71, 41, 96, 77, 76, 75, 110, 147, 112, 31, 114, 115, 44, 56, 116, 78, 118, 117, 145, 48, 119, 120, 121, 43, 123, 122, 124, 125, 126, 47, 45, 63, 127, 146, 128, 137, 138, 46, 49, 97, 139, 140, 105, 99, 100, 102, 98, 103, 104, 101, 129, 148, 149, 151, 150, 30, 155, 156, 154, 158, 157, 160, 159, 131, 132, 134, 65, 161, 135, 39, 111, 163, 162, 142, 51, 143, 59, 144, 64, 141, 38, 60, 53, 190, 180, 182, 165, 499, 166, 130, 181, 183, 152, 153, 179, 202, 201, 203, 185, 207, 206, 204, 133, 210, 186, 136, 205, 208, 209, 214, 187, 213, 212, 211, 215, 216, 62, 411, 178, 289, 167, 184, 188, 164, 189, 168, 500, 221, 222, 169, 191, 170, 225, 217, 218, 219, 229, 231, 224, 220, 223, 227, 230, 228, 235, 232, 233, 67, 234, 290, 171, 236, 237, 239, 238, 241, 240, 242, 243, 192, 247, 246, 244, 245, 250, 248, 251, 249, 252, 295, 194, 193, 253, 195, 172, 254, 197, 196, 256, 257, 66, 68, 498, 408, 61, 55, 297, 301, 50, 173, 198, 262, 259, 199, 175, 200, 174, 260, 296, 298, 302, 57, 299, 263, 176, 264, 273, 255, 292, 300, 410, 497, 496, 261, 304, 308, 306, 305, 303, 307, 309, 265, 266, 268, 267, 269, 177, 270, 271, 274, 272, 258, 312, 313, 409, 316, 311, 310, 315, 317, 314, 318, 319, 320, 321, 334, 322, 293, 294, 291, 323, 226, 113, 327, 325, 330, 324, 326, 329, 331, 328, 332, 412, 333, 335, 336, 338, 337, 340, 342, 339, 341, 343, 344, 346, 345, 347, 348, 413, 414, 415, 349, 350, 353, 352, 351, 354, 355, 52, 356, 416, 357, 358, 359, 362, 417, 552, 360, 361, 363, 364, 365, 366, 275, 398, 367, 371, 368, 372, 369, 370, 374, 373, 375, 376, 377, 378, 386, 276, 379, 277, 384, 279, 418, 385, 383, 380, 392, 393, 394, 391, 381, 387, 388, 389, 419, 278, 399, 397, 401, 400, 402, 395, 405, 403, 406, 404, 407, 281, 420, 282, 421, 422, 283, 285, 280, 423, 284, 424, 425, 286, 287, 288, 382, 390, 426, 427, 429, 396, 428, 430, 431, 435, 433, 432, 440, 434, 437, 436, 441, 442, 438, 439, 443, 444, 448, 445, 446, 450, 449, 452, 447, 453, 451, 454, 501, 484, 455, 456, 457, 459, 458, 460, 461, 462, 463, 464, 465, 466, 504, 467, 503, 502, 468, 505, 506, 472, 469, 508, 507, 474, 481, 479, 480, 471, 473, 509, 482, 510, 475, 476, 477, 511, 487, 512, 513, 488, 491, 470, 489, 485, 490, 493, 495, 494, 492, 515, 514, 516, 517, 478, 518, 522, 519, 521, 520, 483, 486, 523, 526, 524, 527, 528, 525, 530, 529, 533, 534, 537, 535, 536, 531, 532, 539, 538, 541, 540, 542, 543, 545, 544, 546, 547, 548, 549, 550, 551, 553, 554, 555, 556, 557, 559, 558, 561, 562, 560, 564, 566, 563, 570, 568, 571, 569, 565, 567,
+    20, 5, 4, 11, 0, 1, 54, 6, 7, 180, 195, 2, 3, 8, 25, 32, 30, 27, 37, 29, 26, 17, 28, 21, 31, 9, 22, 50, 55, 35, 23, 36, 33, 177, 10, 251, 196, 47, 88, 182, 86, 73, 81, 175, 135, 12, 41, 18, 34, 19, 199, 58, 38, 57, 82, 56, 44, 61, 49, 42, 60, 163, 59, 39, 64, 230, 90, 62, 84, 63, 48, 65, 51, 66, 45, 52, 257, 67, 248, 40, 69, 256, 70, 68, 181, 169, 71, 89, 15, 218, 74, 72, 75, 219, 229, 243, 43, 76, 100, 162, 77, 78, 164, 262, 165, 174, 178, 167, 216, 85, 217, 179, 247, 46, 166, 101, 91, 53, 79, 170, 102, 83, 246, 133, 87, 16, 103, 14, 104, 172, 13, 106, 105, 136, 548, 197, 110, 205, 145, 109, 107, 108, 113, 114, 111, 112, 168, 176, 24, 115, 249, 134, 146, 119, 118, 117, 80, 204, 96, 99, 198, 116, 92, 93, 147, 98, 95, 549, 97, 94, 122, 123, 120, 121, 171, 148, 124, 245, 157, 149, 125, 144, 173, 137, 126, 130, 150, 140, 129, 151, 265, 254, 267, 261, 161, 138, 206, 152, 263, 258, 220, 242, 244, 131, 153, 154, 139, 231, 259, 156, 159, 183, 241, 142, 184, 185, 143, 186, 127, 158, 187, 274, 155, 272, 141, 276, 232, 282, 128, 271, 277, 288, 270, 269, 283, 294, 279, 278, 281, 289, 188, 280, 284, 295, 285, 291, 287, 255, 293, 273, 298, 250, 301, 252, 303, 290, 275, 296, 190, 297, 286, 200, 305, 302, 292, 299, 203, 201, 300, 202, 189, 304, 306, 209, 192, 308, 207, 191, 309, 210, 310, 193, 313, 307, 312, 314, 311, 208, 315, 211, 260, 316, 233, 542, 317, 212, 234, 227, 160, 213, 228, 333, 235, 335, 214, 336, 215, 334, 240, 221, 222, 320, 236, 224, 223, 225, 237, 226, 194, 238, 239, 318, 337, 343, 349, 355, 319, 321, 338, 344, 339, 341, 342, 350, 340, 346, 268, 345, 347, 356, 353, 550, 352, 322, 348, 253, 354, 351, 360, 359, 362, 364, 361, 357, 366, 365, 358, 326, 325, 363, 367, 327, 371, 328, 368, 132, 370, 375, 372, 369, 374, 373, 329, 376, 330, 264, 378, 331, 377, 382, 380, 381, 379, 323, 384, 383, 324, 385, 388, 389, 392, 386, 393, 387, 390, 391, 396, 397, 394, 395, 406, 266, 398, 434, 332, 403, 408, 399, 404, 405, 401, 432, 433, 407, 409, 412, 411, 410, 413, 414, 415, 416, 400, 436, 417, 402, 442, 437, 420, 443, 448, 441, 438, 440, 449, 421, 454, 439, 444, 455, 445, 422, 447, 446, 424, 435, 452, 425, 450, 423, 426, 453, 418, 427, 451, 428, 461, 459, 465, 460, 458, 429, 464, 456, 430, 463, 457, 462, 466, 419, 467, 468, 471, 469, 472, 470, 473, 474, 475, 476, 477, 478, 486, 485, 479, 487, 503, 484, 480, 431, 505, 504, 489, 482, 490, 491, 492, 488, 493, 494, 495, 497, 498, 499, 496, 500, 501, 502, 481, 507, 513, 483, 519, 508, 525, 514, 509, 512, 511, 520, 510, 515, 526, 517, 518, 516, 506, 521, 522, 529, 524, 534, 532, 527, 536, 528, 523, 533, 530, 531, 535, 537, 540, 539, 545, 538, 544, 541, 543, 546, 547, 558, 557, 551, 552, 559, 560, 561, 553, 554, 563, 562, 555, 565, 566, 564, 556,
 ]
 
 
@@ -57,7 +50,8 @@ def rank_program(g, core, T, topo):
     if rank is None:
         return
     cores = list(T.cores)
-    add, sub, mul, mx_ = AluOpType.add, AluOpType.subtract, AluOpType.mult, AluOpType.max
+    add, mul, mx_, mn_ = AluOpType.add, AluOpType.mult, AluOpType.max, AluOpType.min
+    EQ, NE, GT, GE = AluOpType.is_equal, AluOpType.not_equal, AluOpType.is_gt, AluOpType.is_ge
     AND, SHR = AluOpType.bitwise_and, AluOpType.arith_shift_right
     COPY, IDENT = ActivationFunctionType.Copy, ActivationFunctionType.Identity
 
@@ -74,7 +68,7 @@ def rank_program(g, core, T, topo):
     csem = {"v": "cv", "s": "cs", "t": "ct", "g": "cg"}
     ops = []
     hist = {}
-    used = {"tf": 0, "ti": 0}
+    used = {"tf": 0, "ti": 0, "tu": 0, "th": 0, "cf": 0, "cu": 0, "col": 0}
 
     def bits(a, b, st):
         if st == 1:
@@ -99,87 +93,95 @@ def rank_program(g, core, T, topo):
 
     def new(n, pool="tf"):
         a = used[pool]
-        used[pool] += n
+        used[pool] += n if pool == "col" else -(-n // 16) * 16
         assert used[pool] <= SCRATCH[pool][1][1]
         return (pool, a, n)
 
-    def note(q, kind, fn, reads, writes, size, sem=None, n=0, after=()):
-        deps = set(after)
+    def note(q, kind, fn, reads, writes, sem=None, n=0, after=()):
+        deps, soft = set(after), set(after)
         for views, w in ((reads, False), (writes, True)):
             for v_ in views:
                 for (j, pm2, cm2, w2) in hist.get(v_[1], []):
                     if (w or w2 or v_[1] == "ps") and (v_[2] & pm2) and (v_[3] & cm2):
                         deps.add(j)
+                        if q == "t" and ops[j]["q"] == "t":
+                            soft.add(j)
         i = len(ops)
-        ops.append({"q": q, "kind": kind, "fn": fn, "size": size, "sem": sem, "n": n, "deps": deps, "soft": list(after)})
+        ops.append({"q": q, "kind": kind, "fn": fn, "sem": sem, "n": n, "deps": deps, "soft": soft})
         for views, w in ((reads, False), (writes, True)):
             for v_ in views:
                 hist.setdefault(v_[1], []).append((i, v_[2], v_[3], w))
         return i
 
-    def op(q, fn, reads, writes, size):
-        return note(q, "c", fn, reads, writes, size)
+    def op(q, fn, reads, writes):
+        return note(q, "c", fn, reads, writes)
 
-    def dma(q, sem, out, in_, reads, writes, kb=0, after=()):
-        return note(q, "d", lambda: queues[q].dma_start(out, in_), reads, writes, ("dma", kb), sem, 16, after)
+    def dma(q, sem, out, in_, reads, writes, after=()):
+        return note(q, "d", lambda: queues[q].dma_start(out, in_), reads, writes, sem, 16, after)
 
     def landed(sem, n, views, after):
-        return note(None, "l", None, [], views, ("land", 0), sem, n, after)
-
-    def plain(n, *vs):
-        return ("half" if all(SIZE[SCRATCH[v_[1]][2]] == 2 for v_ in vs) else "one", n)
+        return note(None, "l", None, [], views, sem, n, after)
 
     def cp(o, i):
-        op("v", lambda: g.vector.tensor_copy(o[0], i[0]), [i], [o], plain(o[4], o, i))
+        op("v", lambda: g.vector.tensor_copy(o[0], i[0]), [i], [o])
 
     def fill(o, c):
-        op("v", lambda: g.vector.memset(o[0], c), [], [o], plain(o[4], o))
+        op("v", lambda: g.vector.memset(o[0], c), [], [o])
 
     def tt(o, a, b, f):
-        op("v", lambda: g.vector.tensor_tensor(o[0], a[0], b[0], f), [a, b], [o], ("one" if "ps" in (a[1], b[1]) else "two", o[4]))
+        op("v", lambda: g.vector.tensor_tensor(o[0], a[0], b[0], f), [a, b], [o])
 
-    def ts(o, a, s1, f1, s2=None, f2=None):
-        rd = [a] + [s for s in (s1, s2) if isinstance(s, tuple)]
+    def ts(o, a, s1, f1, s2=None, f2=None, off=None):
+        rd = [a] + [s for s in (s1, s2, off) if isinstance(s, tuple)]
         x1 = s1[0] if isinstance(s1, tuple) else s1
         x2 = s2[0] if isinstance(s2, tuple) else s2
+        src = a[0] if off is None else a[0].indirect(off[0])
         if f2 is None:
-            op("v", lambda: g.vector.tensor_scalar(o[0], a[0], x1, None, f1), rd, [o], plain(o[4], o, a))
+            op("v", lambda: g.vector.tensor_scalar(o[0], src, x1, None, f1), rd, [o])
         else:
-            op("v", lambda: g.vector.tensor_scalar(o[0], a[0], x1, x2, f1, f2), rd, [o], plain(o[4], o, a))
+            op("v", lambda: g.vector.tensor_scalar(o[0], src, x1, x2, f1, f2), rd, [o])
 
     def ttg(o, w, off, b, f):
-        op("v", lambda: g.vector.tensor_tensor(o[0], w[0].indirect(off[0]), b[0], f), [w, off, b], [o], ("gather", o[4]))
+        op("v", lambda: g.vector.tensor_tensor(o[0], w[0].indirect(off[0]), b[0], f), [w, off, b], [o])
 
     def gat(q, o, w, off):
         if q == "v":
-            op("v", lambda: g.vector.tensor_copy(o[0], w[0].indirect(off[0])), [w, off], [o], ("gather", o[4]))
+            op("v", lambda: g.vector.tensor_copy(o[0], w[0].indirect(off[0])), [w, off], [o])
         else:
-            op("s", lambda: g.scalar.activation(o[0], w[0].indirect(off[0]), COPY), [w, off], [o], ("gather", o[4]))
+            op("s", lambda: g.scalar.activation(o[0], w[0].indirect(off[0]), COPY), [w, off], [o])
 
     def sca(w, off, i):
-        op("v", lambda: g.vector.tensor_copy(w[0].indirect(off[0]), i[0]), [i, off], [w], ("scatter", i[4]))
+        op("v", lambda: g.vector.tensor_copy(w[0].indirect(off[0]), i[0]), [i, off], [w])
 
-    def scan(o, d, n):
-        k = V("keep", 0, n)
-        op("v", lambda: g.vector.tensor_tensor_scan(o[0], k[0], d[0], 0.0, mul, add), [k, d], [o], plain(n, o, d))
+    def scan(o, k, d, init=0.0, f=add):
+        x = init[0] if isinstance(init, tuple) else init
+        op("v", lambda: g.vector.tensor_tensor_scan(o[0], k[0], d[0], x, mul, f), [k, d] + ([init] if isinstance(init, tuple) else []), [o])
 
     def trn(o, i):
-        op("v", lambda: g.vector.transpose(o[0], i[0]), [i], [o], plain(o[4], o, i))
+        op("v", lambda: g.vector.transpose(o[0], i[0]), [i], [o])
+
+    def total_of(o, i):
+        op("v", lambda: g.vector.tensor_reduce(o[0], i[0], AxisListType.X, add), [i], [o])
 
     def act(o, i, scale=1.0, bias=None, f=None):
         rd = [i] + [s for s in (scale, bias) if isinstance(s, tuple)]
         sc_ = scale[0] if isinstance(scale, tuple) else scale
         if bias is None:
             f = f or (IDENT if isinstance(scale, tuple) else COPY)
-            op("s", lambda: g.scalar.activation(o[0], i[0], f, scale=sc_), rd, [o], ("act", o[4]))
+            op("s", lambda: g.scalar.activation(o[0], i[0], f, scale=sc_), rd, [o])
         else:
             b_ = bias[0] if isinstance(bias, tuple) else bias
-            op("s", lambda: g.scalar.activation(o[0], i[0], f or IDENT, bias=b_, scale=sc_), rd, [o], ("act", o[4]))
+            op("s", lambda: g.scalar.activation(o[0], i[0], f or IDENT, bias=b_, scale=sc_), rd, [o])
 
-    def zero(name, n):
-        for a in range(0, n, 520):
-            k = min(520, n - a)
-            act(V(name, a, a + k), V("et", 0, k), 0.0)
+    def column(i, scale=1.0, bias=None, f=None):
+        o = V(new(1, "col"))
+        act(o, i, scale, bias, f)
+        return o
+
+    def zero(name, a, n, bias=None):
+        for c in range(a, a + n, 512):
+            k = min(512, a + n - c)
+            act(V(name, c, c + k), V("et", 0, k), 0.0, bias)
 
     def scaled(q, o, i, c):
         if q == "s":
@@ -189,29 +191,37 @@ def rank_program(g, core, T, topo):
         else:
             ts(o, i, c, mul)
 
-    def iota(o, pat, base, cm, fl=True):
+    def iota(o, pat, base=0, cm=0, fl=True):
         if fl:
-            op("g", lambda: g.iota(o[0], pat, base, cm, allow_small_or_imprecise_dtypes=True), [], [o], ("iota", o[4]))
+            op("g", lambda: g.iota(o[0], pat, base, cm, allow_small_or_imprecise_dtypes=True), [], [o])
         else:
-            op("g", lambda: g.iota(o[0], pat, base, cm), [], [o], ("iota", o[4]))
+            op("g", lambda: g.iota(o[0], pat, base, cm), [], [o])
+
+    def ramp(pat, base=0):
+        n = 1
+        for _, k in pat:
+            n *= k
+        o = new(n, "cf")
+        iota(V(o), pat, base)
+        return o
 
     def quant(qn, pn, a, n, i):
         o, s_ = V(qn, a, a + n), V(pn, a, a + n)
-        op("v", lambda: g.vector.quantize_mx(o[0], s_[0], i[0]), [i], [o, s_], ("quant", n))
+        op("v", lambda: g.vector.quantize_mx(o[0], s_[0], i[0]), [i], [o, s_])
 
-    def mm(bank, lq, lp, b, rq, rp, a, n):
+    def mm(bank, lq, lp, b, rq, rp, a, n, start=True, stop=True):
         o, l1, l2 = V("ps", 512 * bank, 512 * bank + n), V(lq, 128 * b, 128 * b + 128), V(lp, 128 * b, 128 * b + 128)
         r1, r2 = V(rq, a, a + n), V(rp, a, a + n)
-        op("t", lambda: g.tensor.matmul_mx(o[0], l1[0], l2[0], r1[0], r2[0], True, True), [l1, l2, r1, r2], [o], ("mm", n))
+        op("t", lambda: g.tensor.matmul_mx(o[0], l1[0], l2[0], r1[0], r2[0], start, stop), [l1, l2, r1, r2], [o])
 
     def four(bank0, lq, lp, rq, rp, a, n):
         for b in range(4):
             mm(bank0 + b, lq, lp, b, rq, rp, a, n)
 
-    def pick(oq, op_, a, sq_, sp_, n, off, c, k):
-        o, w, f = V(oq, a, a + k), V(sq_, 0, n), V(off, c, c + k // 16)
-        op("v", lambda: g.vector.tensor_copy(o[0].bitcast(dt.uint32), w[0].bitcast(dt.uint32).indirect(f[0])), [w, f], [o], ("gather", k))
-        gat("s", V(op_, a, a + k), V(sp_, 0, n), f)
+    def pick(oq, op_, a, sq_, sp_, n, f, k, who="s"):
+        o, w = V(oq, a, a + k), V(sq_, 0, n)
+        op("v", lambda: g.vector.tensor_copy(o[0].bitcast(dt.uint32), w[0].bitcast(dt.uint32).indirect(f[0])), [w, f], [o])
+        gat(who, V(op_, a, a + k), V(sp_, 0, n), f)
 
     eng = topo.engines(core, cores[peers[0]])
     for s in peers:
@@ -224,387 +234,400 @@ def rank_program(g, core, T, topo):
             m |= 1 << e
         return m
 
-    def remote(trs, reads, size, after=()):
+    def remote(trs, reads, after=()):
         def fn():
             out = []
-            for e, es, sem, src, dst in trs:
-                rid, pid, _ = topo.addr(cores[peers[e]])
-                out.append(RemoteDMATransfer(dst_ids=[DstId(rid=rid, pnc=pid)], dma_engine_mask=emask(es), remote_sem=T.sem[sem], src=src, dst=dst))
-            g.remote_dma_fused(out, local_sem=T.sem.sent)
-        return note("g", "r", fn, reads, [], size, "sent", sum(len(t_[1]) for t_ in trs), after)
+            for es_, en, sem, src, dst in trs:
+                ids = [DstId(rid=topo.addr(cores[peers[e]])[0], pnc=topo.addr(cores[peers[e]])[1]) for e in es_]
+                out.append(RemoteDMATransfer(dst_ids=ids, dma_engine_mask=emask(en), remote_sem=T.sem[sem], srcs=[src], dsts=[dst] * len(ids)))
+            return g.remote_dma_fused(out, local_sem=T.sem.sent)
+        return note("g", "r", fn, reads, [], "sent", sum(len(t_[1]) for t_ in trs), after)
 
     first = [eng[0:2 * h], eng[2 * h:3 * h], eng[3 * h:4 * h]]
+    second = [eng[2 * h:4 * h], eng[0:h], eng[h:2 * h]]
 
-    def send_part(sem, sq_, sp_, lq, lp, es, prev):
-        k = len(eng) // len(es)
-        for src, dst, codes in ((sq_, lq, True), (sp_, lp, False)):
-            trs, rd = [], []
-            for i, e in enumerate(es):
-                a, b = (CAP * e if e < 2 else 3 * CAP), CAP * slot_at[e]
-                v = V(src, a, a + CAP)
-                o = T[dst][:, b:b + CAP]
-                rd.append(v)
-                trs.append((e, eng[k * i:k * i + k], sem, v[0].bitcast(dt.uint8) if codes else v[0], o.bitcast(dt.uint8) if codes else o))
-            prev = [remote(trs, rd, ("rows", 16 * len(es), CAP * (4 if codes else 1)), prev)]
-        a, b = CAP * es[0], CAP * es[-1] + CAP
-        landed(sem, 2 * len(eng), [V(lq, a, b), V(lp, a, b)], prev)
-        return prev
+    def send_whole(l):
+        a, b = M * l, ZW + 4 * M * l + M * rank
+        vq_, vp_ = V("yq", a, a + M), V("yp", a, a + M)
+        r1 = remote([([0, 1, 2], eng, "ac%d" % l, vq_[0].bitcast(dt.uint8), T.fq[:, b:b + M].bitcast(dt.uint8))], [vq_])
+        r2 = remote([([0, 1, 2], eng, "as%d" % l, vp_[0], T.fp[:, b:b + M])], [vp_, V("rl", 0, 16)], [r1])
+        for nm, sem, r in (("fq", "ac%d" % l, r1), ("fp", "as%d" % l, r2)):
+            landed(sem, 3 * len(eng), [V(nm, ZW + 4 * M * l + M * s, ZW + 4 * M * l + M * s + M) for s in peers], [r])
+        return r2
 
-    def send_whole(a, lq, lp, sem):
+    def send_packed(k, sq_, sp_, a):
         prev = []
-        for e in range(3):
-            b, vq_, vp_ = M * slot_at[e], V("yq", a, a + M), V("yp", a, a + M)
-            prev = [remote([(e, eng, sem + str(slot_at[e]), vq_[0].bitcast(dt.uint8), T[lq][:, b:b + M].bitcast(dt.uint8))], [vq_], ("rows", 16, 4 * M), prev)]
-            prev = [remote([(e, eng, sem + str(slot_at[e]), vp_[0], T[lp][:, b:b + M])], [vp_], ("rows", 16, M), prev)]
-            landed(sem + str(e), 2 * len(eng), [V(lq, M * e, M * e + M), V(lp, M * e, M * e + M)], prev)
-        return prev
+        for src, dst, sem, en in ((sq_, "bq", "ac%d" % k, first), (sp_, "bp", "as%d" % k, second)):
+            trs = []
+            for e in range(3):
+                v, o = T[src][:, CAP * e:CAP * e + CAP], T[dst][:, a + CAP * slot_at[e]:a + CAP * slot_at[e] + CAP]
+                if dst == "bq":
+                    v, o = v.bitcast(dt.uint8), o.bitcast(dt.uint8)
+                trs.append(([e], en[e], sem, v, o))
+            prev = [remote(trs, [V(src)], prev)]
+            landed(sem, len(eng), [V(dst, a, a + NS)], prev)
 
-    fill(V("lvl"), 7)
-    for a in range(4):
-        o = V("lvl", 0, 16, p=(32 * a, 32 * a + 30, 1))
-        last = dma("y" if a % 2 == 0 else "s", "dlv", o[0], T.lv[:], [], [o])
-    last = dma("y", "dx", T.xs[:], T.x[:], [], [V("xs")], 480, [last])
+    last = []
+    for gr in range(8):
+        o = V("lvn", 0, 30, p=(16 * gr, 16 * gr + 16, 1))
+        i_ = dma("ys"[gr % 2], "dlv", o[0], T.lv[:], [], [o])
+        if gr % 2 == 0:
+            last = [i_]
+    last = [dma("y", "dx", T.xs[:], T.x[:], [], [V("xs")], last)]
     fill(V("one"), 1.0)
     fill(V("et"), 0.0)
     iota(V("pid"), [[0, 2]], 0, 1, False)
     o = V("et", 3, 515, 4)
-    op("g", lambda: g.affine_select(o[0], T.one[:], [[-1, 128]], AluOpType.is_equal, 0.0, 0, 1), [V("one")], [o], ("iota", 150))
+    op("g", lambda: g.affine_select(o[0], T.one[:], [[-1, 128]], EQ, 0.0, 0, 1), [V("one")], [o])
     for b in range(4):
         quant("eq", "es", 128 * b, 128, V("et", 3 - b, 515 - b))
-    iota(V("io32", 0, 96), [[0, 3], [1, 32]], 0, 0)
-    iota(V("io32", 96, 192), [[0, 3], [1, 32]], 0, 0)
-    iota(V("oti"), [[32, 6], [0, 2]], 31, 0, False)
-    iota(V("io3"), [[16, 2], [1, 4]], 0, 0)
-    iota(V("rw"), [[1, 16], [16, 30]], 0, 0, False)
+    iota(V("rw"), [[0, C]], 0, 0, False)
     for k, src in ((1, T.pr0), (2, T.pr1)):
         o_ = V("rw", p=(k, 128, 16))
-        last = dma("y", "drw", o_[0], src[:], [], [o_])
+        dma("y", "drw", o_[0], src[:], [], [o_], last)
+    fill(V("rl", 0, 16), 0)
     fill(V("keep"), 1.0)
-    fill(V("keep", 0, 192, 32), 0.0)
-    ts(V("pt", 0, 1), V("pid", 0, 1), 31, AND)
-    ts(V("pt", 1, 2), V("pid", 0, 1), 15, AND)
-    ts(V("pt", 2, 3), V("pid", 0, 1), 16, AND)
-    cp(V("ot"), V("oti"))
-    cp(V("pf", 0, 1), V("pt", 0, 1))
-    cp(V("pf", 1, 3), V("pt", 1, 3))
-    ts(V("m32"), V("io32", 0, 96), V("pf", 0, 1), AluOpType.is_gt)
-    ts(V("sel", 0, 4), V("io3", 0, 4), V("pf", 1, 2), AluOpType.is_equal)
-    ts(V("sel", 4, 6), V("io3", 0, 8, 4), V("pf", 2, 3), AluOpType.is_equal)
-    zero("sw", 960)
-    zero("tab", TABW)
-    act(V("tab", 0, 1), V("sel", 0, 1), -200.0)
-    iota(V("io16"), [[0, 2], [16, 32]], 0, 0)
-    iota(V("io1"), [[1, NS]], 1, 0)
-    for a in (0, 32):
-        iota(V("kc", a, a + 20), [[2 * M, 2], [0, 10]], -640, 0)
-    m1, m2 = new(192), new(192)
-    act(V("col", 0, 1), V("pf", 2, 3), -0.5, -8.0)
-    act(V("col", 1, 2), V("pf", 2, 3), 0.5, 7.5)
-    act(V("col", 2, 3), V("pf", 0, 1), -0.5, V("col", 0, 1))
-    act(V("col", 3, 4), V("pf", 0, 1), -0.5, V("col", 1, 2))
-    act(V("col", 8, 9), V("pf", 1, 2), 1.0, 384.0)
-    act(V("col", 9, 10), V("pf", 1, 2), 1.0, 1280.0)
-    act(V(m1), V("io32"), 1.0, V("col", 2, 3), ActivationFunctionType.Abs)
-    act(V("dmp", 0, 64), V("io16"), 1.0, V("col", 8, 9))
-    act(V(m2), V(m1), -1.0, V("col", 3, 4), ActivationFunctionType.Sign)
-    act(V("dmp", 64, 128), V("io16"), 1.0, V("col", 9, 10))
-    act(V("m16"), V(m2), f=ActivationFunctionType.Relu)
-    zero("iw2", 384)
-    zero("iw1", 384)
-    zero("bw", 1280)
-    act(V("col", 10, 11), V("sel", 2, 3), 162.0)
-    act(V("col", 11, 12), V("sel", 2, 3), 482.0)
-    act(V("kp", 0, M), V("io1", 0, M), V("sel", 1, 2), V("col", 10, 11))
-    act(V("kp", M, 2 * M), V("io1", 0, M), V("sel", 1, 2), V("col", 11, 12))
-    act(V("wf", 0, 4 * PF, PF), V("et", 0, 4), 0.0)
-    act(V("wb", 0, 4 * PB_, PB_), V("et", 0, 4), 0.0)
-    fill(V("rl1"), 0)
-    for i, c in enumerate((M, M + NS, 2 * M + NS)):
-        act(V("col", 5 + i, 6 + i), V("sel", 1, 2), float(c))
+    fill(V("keep", 0, 90, 30), 0.0)
+    fill(V("keep", 90, 180, 3), 0.0)
+    fill(V("keep", 180, 240, 10), 0.0)
+    for i, m in enumerate((15, 16, 14, 1, 28, 96)):
+        ts(V("pt", i, i + 1), V("pid", 0, 1), m, AND)
+    pf = new(6, "col")
+    cp(V(pf), V("pt", 0, 6))
+    pr_, ph, p14, p1, p28, p96 = [V(pf, i, i + 1) for i in range(6)]
+    r5 = ramp([[1, 5]])
+    sel = new(5, "col")
+    ts(V(sel), V(r5), pr_, EQ)
+    sel = [V(sel, i, i + 1) for i in range(5)]
+    flip = column(ph, -1.0 / 16, p1, ActivationFunctionType.Abs)
+    half = column(p14, 0.5)
+    odd = column(ph, 1.0 / 16)
+
+    def spread(b):
+        return column(column(odd, -1.0, float(b)), flip, half)
+
+    def offsets(src, c, top, n, o=None):
+        o = o or V(new(n, "cu"))
+        ts(o, src, c, add, float(top), mn_)
+        return o
+
+    r8 = ramp([[8, 2]])
+    c_half = offsets(column(pr_, 3.0, column(odd, 45.0)), 2.0, 89, 1)
+    c_sig0 = offsets(spread(6), 0.0, 10, 1)
+    c_sig = offsets(V(r8), spread(11), 20, 2)
+    cst = new(3, "col")
+    act(V(cst), V(r5, 0, 3), float(M), column(odd, -float(M), -1.0))
+    iota(V("rj"), [[16 * 512 + 1, 15], [512 + 30, 16]], 0, 16 * 512 + 1)
+    c_m = column(p96, -(16 * 512 + 1.0), -(16 * 512 + 1.0))
+    c_j = column(p96, -(16 * 512 + 1.0), -(16 * 512 + 1.0) - (C - 1) / 2.0)
+    zero("sw", 0, 512)
 
     def evac(bank0, tile, c, who="svsv", n=M):
         for b in range(4):
             scaled(who[b], V(tile, b, 4 * n, 4), V("ps", 512 * (bank0 + b), 512 * (bank0 + b) + n), c)
 
-    def to_window(win, pitch, a, n, who, skip=0):
-        for b in range(4):
-            if who[b] != "-":
-                scaled(who[b], V(win, pitch * b + a, pitch * b + a + n), V("ps", 512 * b + skip, 512 * b + skip + n), -0.5)
-
     quant("sq", "ss", 0, C, V("xs"))
-    four(4, "eq", "es", "sq", "ss", 0, C)
-    evac(4, "xa", 1.0, "ssss", C)
-    quant("xaq", "xap", 0, C, V("xa"))
-
+    ind, cum, ib, cb, tot, tr1, ex, pre, pi, pl = [new(n) for n in (90, 90, 90, 90, 32, 32, 33, 32, 90, 90)]
+    fill(V(tot), 0.0)
+    fill(V(ex, 0, 1), 0.0)
     for l in range(3):
-        ts(V("ind0", 32 * l, 32 * l + 32), V("lvl"), l, AluOpType.is_equal)
-    a1, a2, a3, a4, pp0, pd0, j1, j2 = new(16), new(16), new(16), new(64), new(96), new(96), new(32, "ti"), new(16, "ti")
-    ts(V(a3), V("lvl", 0, 16), M, mul, -1, add)
-    scan(V("cum0"), V("ind0"), 96)
-    ttg(V("bc0"), V("cum0"), V("ot", 0, 6), V("m32"), mul)
-    trn(V("tr0"), V("bc0"))
-    scan(V("sc0"), V("tr0"), 96)
-    ttg(V(pp0), V("sc0"), V("ot", 0, 6), V("cum0"), add)
-    tt(V(pd0), V(pp0), V("ind0"), mul)
-    tt(V(a1), V(pd0, 0, 16), V(pd0, 32, 48), add)
-    tt(V(a2), V(pd0, 64, 80), V(a3), add)
-    tt(V(j1, 0, 16), V(a1), V(a2), add)
-    ts(V("tc30"), V(j1, 0, 16), -float(M), add)
-    v = V("tc30", p=(0, 32, 1))
+        ts(V(ind, 30 * l, 30 * l + 30), V("lvn", 0, 30), l, EQ)
+    for l in range(3):
+        total_of(V(tot, l, l + 1), V(ind, 30 * l, 30 * l + 30))
+    trn(V(tr1), V(tot))
+    scan(V(cum), V("keep", 0, 90), V(ind))
+    ts(V(ib), V(ind), 1024.0, mul)
+    scan(V(ex, 1, 33), V("one", 0, 32), V(tr1))
+    tt(V(cb), V(cum), V(ib), add)
+    trn(V(pre), V(ex, 0, 32))
+    for l in range(3):
+        ts(V(pi, l, 90, 3), V(cb, 30 * l, 30 * l + 30), V(pre, l, l + 1), add, V(cst, l, l + 1), add)
+    scan(V(pl), V("keep", 90, 180), V(pi), 0.0, mx_)
+    place = V(pl, 2, 90, 3)
+    hs = new(16, "tu")
+    ts(V(hs), V(pl), 16.0 - 1024.0, add, off=c_half)
+    tb, tbt = new(32, "th"), new(32, "th")
+    fill(V(tb, 30, 32), 0.0)
+    ts(V(tb, 0, 30), place, -1024.0 - (M - 1), add)
+    trn(V(tbt), V(tb))
+    v = V(tbt, 0, 16, p=(0, 32, 1))
     tdv = [(None, "td", 1, 1 << r, 0) for r in range(4)]
     last = dma("y", "dtd", T.td[rank], v[0], [v], [tdv[rank]])
-    last = dma("y", "dw", T.wq[:].bitcast(dt.uint8), T.wc[:], [], [V("wq")], 256, [last])
-    last = dma("y", "dw", T.wp[:], T.ws[:], [], [V("wp")], 64, [last])
-    r_ = remote([(e, first[e], "atab", T.td[rank], T.td[rank]) for e in range(3)], [tdv[rank]], ("table", 0))
+    last = dma("y", "dw", T.wq[:].bitcast(dt.uint8), T.wc[:], [], [V("wq")], [last])
+    last = dma("y", "dw", T.wp[:], T.ws[:], [], [V("wp")], [last])
+    r_ = remote([([e], first[e], "atab", T.td[rank], T.td[rank]) for e in range(3)], [tdv[rank]])
     landed("atab", len(eng), [tdv[s] for s in peers], [r_])
+    zero("tab", 0, 16, column(sel[0], -199.0, column(sel[1], 200.0)))
+    for s in range(4):
+        zero("tab", 16 + C * s, C, column(sel[1], float(ZW + M + M * s)))
     for gr in range(8):
-        o_ = V("tab", 32, TABW, p=(16 * gr, 16 * gr + 1, 1))
-        dma("y", "dtab", o_[0], T.td[:], tdv, [o_])
-    ts(V(j2), V(j1, 0, 16), 496, AND)
-    tt(V(a4, 0, 16), V(j1, 0, 16), V(j2), add)
-    ts(V(a4, 16, 32), V(a4, 0, 16), 16.0, add)
-    trn(V(a4, 32, 64), V(a4, 0, 32))
-    cp(V("ofs"), V(a4, 32, 64))
-    cp(V("vu"), V(j1, 0, 16))
-    sca(V("sw"), V("ofs", 0, 30), V("rw"))
-    dma("y", "dpd", T.pdr[:], T.vu[:], [V("vu")], [V("pdr")], 4, [r_])
-    b1 = new(30)
-    trn(V("swt", 0, 320), V("sw", 0, 320))
-    tt(V(b1, 0, 10), V("swt", 0, 320, 32), V("swt", 16, 320, 32), add)
-    cp(V("sig", 0, 10), V(b1, 0, 10))
-
-    pick("x0q", "x0p", 0, "xaq", "xap", C, "sig", 0, M)
-    four(0, "wq", "wp", "x0q", "x0p", 0, M)
-    evac(0, "tl", 0.03125)
-    quant("yq", "yp", 0, M, V("tl"))
-    send_whole(0, "laq", "lap", "aa")
-    four(0, "eq", "es", "yq", "yp", 0, M)
-    to_window("wf", PF, 1 + M * rank, M, "ssss")
-
-    pri, si, i1, i2 = new(64, "ti"), new(64, "ti"), new(64, "ti"), new(64, "ti")
-    idx, idy, c1, c3, c4, s160, ko, tca = [new(64) for _ in range(8)]
-    trn(V("swt", 320, 640), V("sw", 320, 640))
-    trn(V("swt", 640, 960), V("sw", 640, 960))
-    fill(V(pri), -1)
-    for l in (1, 2):
-        for k in (0, 1):
-            a = 32 * (l - 1) + 10 * k
-            tt(V(pri, a, a + 10), V("swt", 320 * l + 1 + k, 320 * l + 320, 32), V("swt", 320 * l + 17 + k, 320 * l + 320, 32), add)
-    tt(V(b1, 10, 30), V("swt", 320, 960, 32), V("swt", 336, 960, 32), add)
-    cp(V("sig", 10, 30), V(b1, 10, 30))
-    ts(V(idx), V(pri), -(C - 1) / 2.0, add, 1.0 / C, mul)
-    ts(V(i1), V(pri), 15, AND)
-    ts(V(i2), V(pri), 4, SHR)
-    cp(V(si), V(idx))
-    ts(V(c1), V(i1), 30, mul, 32, add)
-    ts(V(c3), V(si), 512 - 30, mul)
-    tt(V(c4), V(c1), V(i2), add)
-    tt(V(idy), V(c3), V(c4), add)
-    ts(V("id2", 0, 128, 2), V(idy), 0.0, mx_, V("sel", 4, 5), mul)
-    ts(V("id2", 1, 128, 2), V(idy), 0.0, mx_, V("sel", 5, 6), mul)
-    ts(V(s160), V(si), M, mul, 361.0, add)
-    cp(V("idc"), V(idy))
-    for l, gb_ in ((1, "g2a"), (2, "g2b")):
-        a, w0 = 32 * (l - 1), 640 * (l - 1)
-        gat("s", V(gb_), V("tab"), V("id2", 2 * a, 2 * a + 40))
-        trn(V("g2t", w0, w0 + 640), V(gb_))
-        tt(V(tca, a, a + 20), V("g2t", w0, w0 + 640, 32), V("g2t", w0 + 16, w0 + 640, 32), add)
-        d1, d2, d3 = new(20), new(20), new(20)
-        tt(V(d1), V(tca, a, a + 20), V(s160, a, a + 20), add)
-        if l == 1:
-            cp(V("fr1"), V(d1))
-        else:
-            ts(V(d2), V(tca, a, a + 20), -200.0, AluOpType.is_ge, float(3 * M), mul)
-            tt(V(d3), V(d1), V(d2), add)
-            cp(V("fr2"), V(d3))
-    pick("pq", "pss", 0, "sq", "ss", C, "sig", 10, M)
-
-    def scatter_places(out, src, a, n, high, dump):
-        e2, e1, e3, e4 = new(n, "ti"), new(n), new(n), new(n)
-        ts(V(e2), src, high, AND)
-        ts(V(e1), src, V("pf", 2, 3), add)
-        tt(V(e3), V(e1), V(e2), add)
-        tt(V(e4), V(e3), dump, AluOpType.min)
-        cp(V(out, a, a + n), V(e4))
-
-    for e in range(3):
-        ts(V("ind", 64 * e, 64 * e + 64), V(si), peers[e], AluOpType.is_equal)
-    scan(V("cum"), V("ind"), 192)
-    ttg(V("bc"), V("cum"), V("ot"), V("m16"), mul)
-    for e in range(3):
-        act(V("cuc", 64 * e, 64 * e + 64), V("cum", 64 * e, 64 * e + 64), 1.0, float(CAP * e))
-    trn(V("tr"), V("bc"))
-    scan(V("sc"), V("tr"), 192)
-    ts(V(ko), V(si), rank, AluOpType.is_equal, 1000.0, mul)
-    ttg(V("pp"), V("sc"), V("ot"), V("cuc"), add)
-    tt(V("pd"), V("pp"), V("ind"), mul)
-    f1, f2, f3 = new(64), new(64), new(64, "ti")
-    tt(V(f1), V("pd", 0, 64), V("pd", 64, 128), add)
-    ts(V(f2), V("pd", 128, 192), -1.0, add)
-    tt(V(f3), V(f1), V(f2), add)
-    scatter_places("iof", V(f3), 0, 64, 1008, V("dmp", 0, 64))
-
-    def requests(l, after):
-        iw, rq, rl, a, w0 = "iw%d" % l, "rq%d" % l, "rl%d" % l, 32 * (l - 1), 384 * (l - 1)
-        gc = V("gc", 320 * (l - 1), 320 * l)
-        ttg(gc, V("tab"), V("idc", a, a + 20), V("kp"), add)
-        sca(V(iw), V("iof", a, a + 20), gc)
-        trn(V("iwt", w0, w0 + 384), V(iw, 0, 384))
-        n1, n2, n3, n4 = new(12), new(12), new(12, "ti"), new(12)
-
-        def row(k):
-            return V("iwt", w0 + k, w0 + 384, 32)
-        tt(V(n1), row(0), row(16), add)
-        tt(V(n2), row(2), row(18), add)
-        tt(V(n3), V(n1), V(n2), add)
-        tt(V(n4), row(1), row(17), add)
-        ts(V("bs", 12 * (l - 1), 12 * l), V(n4), -1.0, add, 0.0, mx_)
-        k = 4
-        if l == 1:
-            k, m_ = 3, new(12, "ti")
-            ts(V(m_, 0, 3), V(n3, 3, 12, 4), 512.0, mul)
-            ts(V(m_, 4, 7), V(m_, 0, 3), 127 * 512, AND)
-            ts(V(m_, 8, 11), V(m_, 0, 3), 7, SHR, 127 * 512, AND)
-            tt(V(n3, 0, 12, 4), V(n3, 0, 12, 4), V(m_, 4, 7), add)
-            tt(V(n3, 1, 12, 4), V(n3, 1, 12, 4), V(m_, 8, 11), add)
-        cp(V(rq), V(n3))
-        r = remote([(e, first[e], "ar%d" % l, T[rq][:, 4 * e:4 * e + k], T[rl][:, 4 * slot_at[e]:4 * slot_at[e] + k]) for e in range(3)],
-                   [V(rq)], ("rows", 64, 2 * k), after)
-        landed("ar%d" % l, len(eng), [V(rl)], [r])
-        return [r]
-
-    def successors(l, out):
-        a, rl = 32 * l - 32, "rl%d" % l
-        pl, q1, u = new(32, "ti"), new(20), new(12, "ti")
-        tt(V(q1), V("kc", a, a + 20), V(ko, a, a + 20), add)
-        tt(V(pl, 0, 20), V(q1), V(tca, a, a + 20), add)
-        if l == 2:
-            ts(V(pl, 20, 32), V(rl, 0, 12), -2.0, add)
-        else:
-            lo, hi = new(12, "ti"), new(8, "ti")
-            cp(V(u), V(rl, 0, 12))
-            ts(V(lo), V(u), 511, AND)
-            ts(V(hi, 0, 3), V(u, 0, 12, 4), 9, SHR)
-            ts(V(hi, 4, 7), V(u, 1, 12, 4), 2, SHR, 384, AND)
-            tt(V(lo, 3, 12, 4), V(hi, 0, 3), V(hi, 4, 7), add)
-            ts(V(pl, 20, 32), V(lo), -2.0, add)
-        scatter_places("bof", V(pl), a, 32, 4080, V("dmp", 64 + a, 96 + a))
-        sca(V("bw"), V("bof", a, a + 20), V("pb%d" % l, 0, 2 * M))
-        sca(V("bw"), V("bof", a + 20, a + 32), V("pb%d" % l, 2 * M, 512))
-        w0 = 1280 + 640 * (l - 1)
-        for k in range(2):
-            s0 = 320 * (l - 1) + 640 * k
-            trn(V("g2t", w0 + 320 * k, w0 + 320 * k + 320), V("bw", s0, s0 + 320))
-        q2, q3 = new(40), new(20)
-        tt(V(q2), V("g2t", w0, w0 + 640, 16), V("g2t", w0 + 1, w0 + 640, 16), add)
-        tt(V(q3), V(q2, 0, 40, 2), V(q2, 1, 40, 2), add)
-        cp(V(out), V(q3))
-
-    def payload(name, own, far):
-        for a, n, c in ((0, M, own), (M, M, own), (2 * M, NS, far)):
-            if c is None:
-                act(V(name, a, a + n), V("io1", 0, n), V("sel", 0, 1))
-            else:
-                act(V(name, a, a + n), V("io1", 0, n), V("sel", 0, 1), c)
+        o_ = V("tab", 16, 16 + 4 * C, p=(16 * gr, 16 * gr + 1, 1))
+        dma("ys"[gr % 2], "dtab", o_[0], T.td[:, 0:C // 4, :], tdv, [o_])
+    sca(V("sw"), V(hs, 0, 15), V("rj"))
+    a0, sig, aj, sgm = new(11), new(48, "tu"), new(21), new(32, "tu")
+    trn(V("swt", 0, 160), V("sw", 16, 176))
+    trn(V("swt", 160, 352), V("sw", 0, 192))
+    tt(V(a0), V("swt", 1, 352, 32), V("swt", 16, 352, 32), add)
+    ts(V(sig, 0, 16), V(a0), c_j, add, 1.0 / 512, mul, off=c_sig0)
 
     def layer(lq, lp):
         quant("xq", "xp", 0, M, V("xt"))
-        four(0, lq, lp, "xq", "xp", 0, M)
+        four(4, lq, lp, "xq", "xp", 0, M)
 
-    def make(win, pitch, wn, a, n, skip, lst, lq, lp):
-        def w(b):
-            return V(win, pitch * b, pitch * b + wn)
+    def close(l):
+        evac(4, "tl", 0.03125)
+        quant("yq", "yp", M * l, M, V("tl"))
+
+    pick("pq", "pss", 0, "sq", "ss", C, V(sig, 0, 10), M)
+    four(0, "eq", "es", "pq", "pss", 0, M)
+    evac(0, "xt", 1.0)
+    layer("wq", "wp")
+    close(0)
+    send_whole(0)
+    quant("fq", "fp", ZW + M * rank, M, V("tl"))
+    zero("zt", 0, 4 * ZW)
+    quant("fq", "fp", 0, ZW, V("zt"))
+    quant("bq", "bp", 0, ZW, V("zt"))
+    act(V("em", 0, 520), V("et"), column(odd, 0.5, -0.5))
+    act(V("em", 520, 1040), V("et"), column(odd, -0.5))
+    for par in range(2):
         for b in range(4):
-            to_window(win, pitch, a, n, "-" * b + "vsss"[b] + "-" * (3 - b), skip)
-            gat("vsss"[b], V("ab", M * b, M * b + M), w(b), V(lst, 0, 10))
+            quant("eq", "es", 512 * (par + 1) + 128 * b, 128, V("em", 520 * par + 3 - b, 520 * par + 515 - b))
+
+    trn(V("swt", 352, 672), V("sw", 176, 496))
+    trn(V("swt", 672, 1024), V("sw", 160, 512))
+    m1, m2 = new(32, "ti"), new(32, "ti")
+    tt(V(aj), V("swt", 353, 1024, 32), V("swt", 368, 1024, 32), add)
+    ts(V(m1), V(aj), c_m, add, off=c_sig)
+    ts(V(m2, 0, 20), V(m1, 0, 20), 511, AND)
+    cp(V(sgm, 0, 20), V(m2, 0, 20))
+    gs, gst, idx = new(320), new(320), new(40, "tu")
+    gat("v", V(gs), V("rw"), V(sgm, 0, 20))
+    trn(V(gst), V(gs))
+    for l in range(2):
+        for k in range(2):
+            ts(V(idx, 20 * l + 10 * k, 20 * l + 10 * k + 10), V(gst, M * l + 1 + k, M * l + M, 16), 16.0, add)
+    ts(V(sig, 16, 36), V(m1, 0, 20), -(C - 1) / 2.0, add, 1.0 / 512, mul)
+    pick("pq", "pss", M, "sq", "ss", C, V(sig, 16, 26), M)
+    pick("pq", "pss", 2 * M, "sq", "ss", C, V(sig, 26, 36), M)
+
+    ri = ramp([[32, 5], [0, 2], [1, 16]])
+    own_i = column(sel[2], ph)
+    for l, base in ((0, Z1), (1, Z2)):
+        cl = column(sel[3], float(base), own_i)
+        for k in range(2):
+            a = 2 * M * l + M * k
+            act(V("kp", a, a + M), V(ri), sel[2], column(sel[4], M * k - BIG, cl))
+    r10 = ramp([[10, 2]])
+    c_fwd = new(4, "cu")
+    offsets(V(r10), column(odd, 20.0, pr_), 41, 2, V(c_fwd, 0, 4, 2))
+    offsets(V(r10), column(odd, -22.0, column(pr_, 1.0, 22.0)), 41, 2, V(c_fwd, 1, 4, 2))
+    fr = [new(64, "tu"), new(64, "tu")]
+    for a in (0, 336, 688):
+        fill(V("lk", a, a + (32 if a == 336 else 16)), 0.0)
+    for l in range(2):
+        a, w0 = 352 * l, 672 * l
+        ttg(V("lk", a + 16, a + 336), V("tab"), V(idx, 20 * l, 20 * l + 20), V("kp", 2 * M * l, 2 * M * l + 2 * M), add)
+        trn(V("lkt", w0, w0 + 320), V("lk", a + 16, a + 336))
+        trn(V("lkt", w0 + 320, w0 + 672), V("lk", a, a + 352))
+        d1, d2, d3 = new(42), new(42), new(42)
+        tt(V(d1), V("lkt", w0, w0 + 672, 16), V("lkt", w0 + 1, w0 + 672, 16), add)
+        if l == 1:
+            ts(V(d2), V("lkt", w0, w0 + 672, 16), 0.0, GT, float(3 * M), mul)
+            tt(V(d3), V(d1), V(d2), add)
+            d1 = d3
+        ts(V(fr[l]), V(d1), -1.0, add, off=V(c_fwd))
+
+    si, in2, cu2, tb2, tr2, ex2, pr2, p2, pd = new(40, "ti"), new(128, "th"), new(128, "th"), new(32), new(32), new(33), new(32), new(128), new(120)
+    r16 = ramp([[16, 8]])
+    n16, nd = new(8), new(8, "ti")
+    act(V(n16), V(r16), 1.0, pr_)
+    ts(V(nd), V(n16), 0.05, mul, -0.475, add)
+    c_seg = V(new(8, "cu"))
+    ts(c_seg, V(nd), 2.0, mul, p1, add)
+    init = column(p28, 16.0, -1.0 - BIG)
+    ts(V(si), V(idx), -16.0 - (C - 1) / 2.0, add, 1.0 / C, mul)
+    for e in range(3):
+        ts(V(in2, 40 * e, 40 * e + 40), V(si), peers[e], EQ)
+    fill(V(cu2, 120, 128), 0.0)
+    fill(V(tb2), 0.0)
+    act(V(ex2, 0, 1), init)
+    for par in range(2):
+        scan(V(cu2, par, 120, 2), V("keep", 180, 240), V(in2, par, 120, 2))
+        cp(V(tb2, par, 12, 2), V(cu2, 18 + par, 120, 20))
+    trn(V(tr2), V(tb2))
+    scan(V(ex2, 1, 33), V("one", 0, 32), V(tr2), init)
+    trn(V(pr2), V(ex2, 0, 32))
+    ttg(V(p2), V(pr2), c_seg, V(cu2), add)
+    tt(V(pd), V(p2, 0, 120), V(in2, 0, 120), mul)
+    f1, f2, f3, f4, f5, f6, ow, k2 = new(40), new(40, "ti"), new(40, "ti"), new(40), new(40), new(40), new(40), new(40)
+    k1 = ramp([[2 * NS, 2], [0, 10], [16, 2]], int(BIG))
+    kk = new(40, "cf")
+    for l in range(2):
+        iota(V(kk, 20 * l, 20 * l + 20), [[M, 2], [0, 5], [512, 2]], S0 + M - 1)
+    rdm, dm = ramp([[0, 2], [16, 20]], D0), new(40)
+    act(V(dm), V(rdm), 1.0, pr_)
+    tt(V(f1), V(pd, 0, 40), V(pd, 40, 80), add)
+    tt(V(f2), V(f1), V(pd, 80, 120), add)
+    ts(V(f3), V(f2), 1008, AND)
+    tt(V(f4), V(f2), V(k1), add)
+    tt(V(f5), V(f4), V(f3), add)
+    tt(V(f6), V(f5), V(dm), mn_)
+    ts(V(ow), V(si), rank, NE, BIG, mul)
+    tt(V(k2), V(ow), V(kk), add)
+    c1, c2, c3 = new(3), new(3), new(3)
+    ts(V(c1), V(n16, 0, 3), 20.0, GE, 352.0, mul)
+    act(V(c2), V(n16, 0, 3), 16.0, column(flip, 336.0))
+    tt(V(c3), V(c1), V(c2), add)
+    c_own = offsets(V(c3), 0.0, 1343, 3)
+    vo, u1, u2, u3, u4, iof = new(48), new(40), new(40), new(40), new(40), new(40, "tu")
+    gat("v", V(vo), V("lkt"), c_own)
+    ts(V(u1), V(vo, 0, 40), 0.0, GT, 1024.0 - M, mul)
+    tt(V(u2), V(vo, 0, 40), V(k2), add)
+    tt(V(u3), V(u2), V(u1), add)
+    tt(V(u4), V(u3), V(f6), mn_)
+    cp(V(iof), V(u4))
+    zero("ww", 0, S0 + 2 * M + 16)
+    for a in range(1, 4):
+        zero("ww", S0 + 512 * a - 16, 2 * M + 32)
+
+    rq, bs = new(32, "tu"), new(24, "tu")
+    rqq = new(12, "cf")
+    for e in range(3):
+        iota(V(rqq, 4 * e, 4 * e + 4), [[16, 4]], CAP * slot_at[e])
+    dq = [new(12), new(12)]
+    act(V(dq[0]), V(rqq), 1.0, column(pr_, 1.0, 2 * M - (M - 1) - BIG))
+    act(V(dq[1]), V(rqq), 1.0, column(ph, -32.0, column(pr_, 1.0, D0 - S0 - (M - 1) - BIG)))
+    at2, at1 = column(ph, 32.0, S0 + M - 1 + BIG), column(ph, 32.0, float(S0))
+
+    def requests(l, after):
+        w0 = 2 * NS * l
+        sca(V("ww"), V(iof, 20 * l, 20 * l + 20), V("lk", 352 * l + 16, 352 * l + 336))
+        trn(V("slt", w0, w0 + 2 * NS), V("ww", w0, w0 + 2 * NS))
+
+        def row(k, st=16):
+            return V("slt", w0 + k, w0 + 2 * NS, st)
+        n1, n2, n3, n4, n5, n6 = new(24), new(24), new(24), new(12), new(12), new(12)
+        tt(V(n6), row(2, 32), row(18, 32), add)
+        cp(V(bs, 12 * l, 12 * l + 12), V(n6))
+        tt(V(n1), row(0), row(4), add)
+        if l == 1:
+            ts(V(n2), row(0), 0.0, GT, 1024.0 - M, mul)
+            tt(V(n3), V(n1), V(n2), add)
+            n1 = n3
+        tt(V(n4), V(n1, 0, 24, 2), V(n1, 1, 24, 2), add)
+        tt(V(n5), V(n4), V(dq[l]), mn_)
+        if l == 1:
+            ts(V(rq, 16, 28), V(n5), at2, add)
+        else:
+            n7, m_ = new(12, "ti"), new(12, "ti")
+            ts(V(n7), V(n5), M - 1 + BIG, add)
+            ts(V(m_, 0, 3), V(n5, 3, 12, 4), M - 1 + BIG, add, 512.0, mul)
+            ts(V(m_, 4, 7), V(m_, 0, 3), 127 * 512, AND)
+            ts(V(m_, 8, 11), V(m_, 0, 3), 7, SHR, 127 * 512, AND)
+            tt(V(n7, 0, 12, 4), V(n7, 0, 12, 4), V(m_, 4, 7), add)
+            tt(V(n7, 1, 12, 4), V(n7, 1, 12, 4), V(m_, 8, 11), add)
+            cp(V(rq, 0, 12), V(n7))
+        a, k = 16 * l, 3 + l
+        r = remote([([e], first[e], "ar%d" % l, V(rq, a + 4 * e, a + 4 * e + k)[0], T.rl[:, a + 4 * slot_at[e]:a + 4 * slot_at[e] + k])
+                    for e in range(3)], [V(rq, a, a + 12)], after)
+        landed("ar%d" % l, len(eng), [V("rl", a, a + 12)], [r])
+
+    rs, r5k = ramp([[1, NS]]), ramp([[5, 2]])
+    c_su = new(4, "cu")
+    offsets(V(r5k), spread(21), 41, 2, V(c_su, 0, 2))
+    offsets(V(r5k), column(column(odd, -1.0, 22.0), flip, column(half, 1.0, 10.0)), 41, 2, V(c_su, 2, 4))
+    for l, base in ((0, A1), (1, A2)):
+        act(V("pb", NS * l, NS * l + NS), V(rs), sel[2], column(sel[3], float(base)))
+    br = [new(64, "tu"), new(64, "tu")]
+
+    def successors(l):
+        if l == 1:
+            sca(V("ww"), V("rl", 16, 28), V("pb", NS, 2 * NS))
+        else:
+            u, lo, hi, ao = new(24, "ti"), new(12, "ti"), new(8, "ti"), new(12, "tu")
+            cp(V(u, 0, 12), V("rl", 0, 12))
+            ts(V(lo), V(u, 0, 12), 511, AND)
+            ts(V(hi, 0, 3), V(u, 0, 12, 4), 9, SHR)
+            ts(V(hi, 4, 7), V(u, 1, 12, 4), 2, SHR, 384, AND)
+            tt(V(lo, 3, 12, 4), V(hi, 0, 3), V(hi, 4, 7), add)
+            ts(V(ao), V(lo), at1, add)
+            sca(V("ww"), V(ao), V("pb", 0, NS))
+        w0 = 1344 * l
+        for par in range(2):
+            s0 = S0 + 1024 * l + 512 * par
+            trn(V("sut", w0 + 320 * par, w0 + 320 * par + 320), V("ww", s0, s0 + 320))
+            trn(V("sut", w0 + 640 + 352 * par, w0 + 992 + 352 * par), V("ww", s0 - 16, s0 + 336))
+        q2, q3 = new(84), new(42)
+        tt(V(q2), V("sut", w0 + 2, w0 + 1344, 16), V("sut", w0 + 3, w0 + 1344, 16), add)
+        tt(V(q3), V(q2, 0, 84, 2), V(q2, 1, 84, 2), add)
+        gat("v", V(br[l]), V(q3), V(c_su))
+
+    def make(kq, kp_, wq_, wp_, wn, lst, par_of, dq_, dp_, da, lq, lp):
+        for b in (1, 3):
+            mm(4 + b, "eq", "es", b, dq_, dp_, da, M)
+            act(V("dd", M * (b // 2), M * (b // 2) + M), V("ps", 512 * (4 + b), 512 * (4 + b) + M))
+        for i in range(4):
+            pick(kq, kp_, M * i, wq_, wp_, wn, V(lst, 16 * i, 16 * i + 10), M)
+            for b in range(4):
+                mm(b, "eq", "es", 4 * (par_of[i] + 1) + b, kq, kp_, M * i, M, i == 0, i == 3 and b % 2 == 1)
+                if i == 3 and b % 2 == 0:
+                    mm(b, "eq", "es", b, dq_, dp_, da, M, False, True)
         for b in range(4):
-            ttg(V("sm", M * b, M * b + M), w(b), V(lst, 10, 20), V("ab", M * b, M * b + M), add)
-            tt(V("xt", b, 4 * M, 4), V("ps", 512 * (4 + b), 512 * (4 + b) + M), V("sm", M * b, M * b + M), add)
+            o, p_ = V("xt", b, 4 * M, 4), V("ps", 512 * b, 512 * b + M)
+            if b % 2 == 0:
+                act(o, p_)
+            else:
+                tt(o, p_, V("dd", M * (b // 2), M * (b // 2) + M), add)
         layer(lq, lp)
 
-    def arrive(lq, lp, win, pitch, a):
-        four(0, "eq", "es", lq, lp, 0, 2 * CAP)
-        to_window(win, pitch, a, 2 * CAP, "ssss")
-        four(0, "eq", "es", lq, lp, CAP, 2 * CAP)
-
-    def arrive_whole(lq, lp, a):
-        for e in range(3):
-            four(0, "eq", "es", lq, lp, M * e, M)
-            if e < 2:
-                to_window("wf", PF, a + M * peers[e], M, "ssss")
-
-    def pack(c0, sem, sq_, sp_, lq, lp):
+    def pack(l, k, sq_, sp_, a, own):
         for b in range(4):
-            scaled("svsv"[b], V("tp", M * b, M * b + M), V("ps", 512 * b, 512 * b + M), 0.03125)
+            scaled("svsv"[b], V("tp", M * b, M * b + M), V("ps", 512 * (4 + b), 512 * (4 + b) + M), 0.03125)
         for b in range(4):
-            gat("svsv"[b], V("st", b, 8 * CAP, 4), V("tp", M * b, M * b + M), V("bs", c0, c0 + 8))
-        quant(sq_, sp_, 0, 2 * CAP, V("st", 0, 8 * CAP))
-        prev = send_part(sem, sq_, sp_, lq, lp, [0, 1], [])
-        for b in range(4):
-            gat("svss"[b], V("st", 8 * CAP + b, 4 * NS, 4), V("tp", M * b, M * b + M), V("bs", c0 + 8, c0 + 12))
-        quant(sq_, sp_, 2 * CAP, 2 * CAP, V("st", 4 * CAP, 4 * NS))
-        send_part(sem + "2", sq_, sp_, lq, lp, [2], prev)
-        evac(0, "tl", 0.03125, "ssss")
+            gat("svsv"[b], V("st", b, 4 * NS, 4), V("tp", M * b, M * b + M), V(bs, 12 * l, 12 * l + 12))
+        quant(sq_, sp_, 0, NS, V("st"))
+        send_packed(k, sq_, sp_, a)
+        evac(4, "tl", 0.03125, "ssss")
+        quant("bq", "bp", own, M, V("tl"))
 
-    arrive_whole("laq", "lap", 1)
-    four(4, "eq", "es", "pq", "pss", 0, M)
-    dma("y", "dv", T.vq[:].bitcast(dt.uint8), T.vc[:], [V("laq")], [V("vq")], 256)
-    dma("y", "dv", T.vp[:], T.vs[:], [V("laq")], [V("vp")], 64)
-    make("wf", PF, 1 + 4 * M, 1 + M * peers[2], M, 0, "fr1", "wq", "wp")
-    evac(0, "tl", 0.03125)
-    quant("yq", "yp", M, M, V("tl"))
-    last = send_whole(M, "lbq", "lbp", "ab")
-    last = requests(2, last)
-    requests(1, last)
+    arrived = [V("fp", ZW + M * peers[0], ZW + M * peers[0] + M)]
+    dma("y", "dv", T.vq[:].bitcast(dt.uint8), T.vc[:], arrived, [V("vq")])
+    dma("y", "dv", T.vp[:], T.vs[:], arrived, [V("vp")])
+    dma("y", "du", T.us[:], T.u[:], arrived, [V("us")])
+    make("k1q", "k1p", "fq", "fp", ZW + 4 * M, fr[0], (0, 1, 0, 1), "pq", "pss", M, "wq", "wp")
+    close(1)
+    last = send_whole(1)
+    quant("fq", "fp", ZW + 4 * M + M * rank, M, V("tl"))
+    requests(1, [last])
 
-    pick("pq", "pss", M, "sq", "ss", C, "sig", 20, M)
-    four(4, "eq", "es", "pq", "pss", M, M)
-    four(0, "eq", "es", "yq", "yp", M, M)
-    to_window("wf", PF, 1 + 4 * M + M * rank, M, "ssss")
-    arrive_whole("lbq", "lbp", 1 + 4 * M)
-    dma("y", "du", T.us[:], T.u[:], [V("lbq")], [V("us")], 128)
-    for gr in range(8):
-        o_ = V("pij", 0, 30, p=(16 * gr, 16 * gr + 16, 1))
-        dma("y", "dpij", o_[0], T.pdr[0:30, :], [V("pdr"), V("lbq")], [o_])
-    make("wf", PF, 1 + 8 * M, 1 + 4 * M + M * peers[2], M, 0, "fr2", "wq", "wp")
-
-    evac(0, "tl", 0.03125)
-    quant("yq", "yp", 2 * M, M, V("tl"))
-    four(4, "eq", "es", "yq", "yp", 2 * M, M)
-    evac(4, "xt", 1.0)
+    make("k2q", "k2p", "fq", "fp", ZW + 8 * M, fr[1], (0, 1, 0, 1), "pq", "pss", 2 * M, "wq", "wp")
+    close(2)
+    four(0, "eq", "es", "yq", "yp", 2 * M, M)
+    evac(0, "xt", 1.0)
     layer("vq", "vp")
-    pack(12, "ac_", "scq", "scp", "lcq", "lcp")
+    pack(1, 2, "scq", "scp", A2, Z2)
 
-    four(4, "eq", "es", "yq", "yp", M, M)
-    quant("zq", "zp", 2 * M, M, V("tl"))
-    four(0, "eq", "es", "zq", "zp", 2 * M, M)
-    to_window("wb", PB_, 1, M, "ssss")
-    payload("pb2", None, V("col", 5, 6))
-    successors(2, "br1")
-    arrive("lcq", "lcp", "wb", PB_, 1 + M)
-    make("wb", PB_, 1 + M + NS, 1 + M + 2 * CAP, CAP, CAP, "br1", "vq", "vp")
-    pack(0, "ad_", "sdq", "sdp", "ldq", "ldp")
-
-    four(4, "eq", "es", "yq", "yp", 0, M)
-    quant("zq", "zp", M, M, V("tl"))
-    four(0, "eq", "es", "zq", "zp", M, M)
-    to_window("wb", PB_, 1 + M + NS, M, "ssss")
-    payload("pb1", V("col", 6, 7), V("col", 7, 8))
-    successors(1, "br0")
-    arrive("ldq", "ldp", "wb", PB_, 1 + 2 * M + NS)
-    make("wb", PB_, 1 + 2 * M + 2 * NS, 1 + 2 * M + NS + 2 * CAP, CAP, CAP, "br0", "vq", "vp")
+    successors(1)
+    requests(0, [])
+    make("k3q", "k3p", "bq", "bp", Z1, br[1], (0, 0, 1, 1), "yq", "yp", M, "vq", "vp")
+    pack(0, 3, "sdq", "sdp", A1, Z1)
+    successors(0)
+    make("k4q", "k4p", "bq", "bp", Z0, br[0], (0, 0, 1, 1), "yq", "yp", 0, "vq", "vp")
     quant("uq", "up", 0, 128, V("us"))
-    evac(0, "tl", 0.03125)
+    evac(4, "tl", 0.03125)
+    quant("bq", "bp", Z0, M, V("tl"))
 
-    quant("zq", "zp", 0, M, V("tl"))
-    halves = ((0, 256), (256, 224))
-    for i, (a, n) in enumerate(halves):
-        pick("oq", "op", a, "zq", "zp", C, "pij", a // 16, n)
-        mm(4 + i, "uq", "up", 0, "oq", "op", a, n)
-    for i, (a, n) in enumerate(halves):
-        scaled("vs"[i], V("yo", a, a + n), V("ps", 512 * (4 + i), 512 * (4 + i) + n), 1.0)
-    dma("y", "dout", T.oc[:], T.oq[:].bitcast(dt.uint8), [V("oq")], [], 240)
-    dma("s", "dout", T.y[:], T.yo[:], [V("yo")], [], 240)
+    g1, g2, pij = new(30), new(30), new(30, "tu")
+    ts(V(g1), V("lvn", 0, 30), float(Z1 - M - Z0), mul, Z0 - 1024.0, add)
+    tt(V(g2), V(g1), place, add)
+    cp(V(pij), V(g2))
+    for i, (a, n) in enumerate(((0, 256), (256, 224))):
+        pick("oq", "op", a, "bq", "bp", Z0 + M, V(pij, a // 16, (a + n) // 16), n)
+        dma("y", "dout", T.oc[:, 4 * a:4 * a + 4 * n], T.oq[:, a:a + n].bitcast(dt.uint8), [V("oq", a, a + n)], [])
+        mm(i, "uq", "up", 0, "oq", "op", a, n)
+        scaled("vs"[i], V("yo", a, a + n), V("ps", 512 * i, 512 * i + n), 1.0)
+        dma("sy"[i], "dout", T.y[:, a:a + n], T.yo[:, a:a + n], [V("yo", a, a + n)], [])
     for k in range(4):
         dma("y", "dout", T.osc[4 * k:4 * k + 4, :], T.op[32 * k:32 * k + 4, :], [V("op")], [])
 
@@ -617,7 +640,7 @@ def rank_program(g, core, T, topo):
             if ops[j]["kind"] == "d" and j not in o_["soft"]:
                 assert ops[j]["sem"] != o_["sem"]
                 o_["deps"].update(group[ops[j]["sem"]])
-    order = ORDER
+    order = ORDER or list(range(len(ops)))
     assert sorted(order) == list(range(len(ops)))
     total, known, token = {}, {q: {} for q in queues}, {}
     for o_ in ops:
@@ -634,15 +657,15 @@ def rank_program(g, core, T, topo):
             if k.get(s_, 0) < c_:
                 k[s_] = c_
 
-    place = {i: k for k, i in enumerate(order)}
+    at = {i: k for k, i in enumerate(order)}
     for i in order:
         o_ = ops[i]
         q = o_["q"]
-        assert all(place[j] < place[i] for j in o_["deps"])
+        assert all(at[j] < at[i] for j in o_["deps"])
         if o_["kind"] == "l":
             token[i] = (o_["sem"], o_["n"], {})
             continue
-        for j in sorted(o_["deps"], key=lambda j: -place[j]):
+        for j in sorted(o_["deps"], key=lambda j: -at[j]):
             if j not in o_["soft"]:
                 need(q, *token[j])
         if o_["kind"] == "c":

@@ -5,8 +5,9 @@ C, M, CAP = 480, 160, 64
 NS = 3 * CAP
 ZW = 128
 Z2, A2, Z1, A1, Z0 = ZW, ZW + M, ZW + M + NS, ZW + 2 * M + NS, ZW + 2 * M + 2 * NS
-S0 = 4 * NS + 16
-D0 = S0 + 3 * 512 + 2 * M + 16
+S0 = 4 * NS
+PS = 4 * M + NS
+D0 = S0 + PS + 4 * M
 WW = D0 + 2 * M
 BIG = 4096.0
 Q4, U8, BF, F32, I32, U16 = "float8_e4m3fn_x4", "uint8", "bfloat16", "float32", "int32", "uint16"
@@ -35,13 +36,14 @@ SCRATCH = {
     "lvn": _sb(32, I32), "rw": _sb(C, I32), "sw": _sb(512, F32), "swt": _sb(1024, F32),
     "tf": _sb(4096, F32), "ti": _sb(512, I32), "tu": _sb(768, U16), "th": _sb(512, BF),
     "tab": _sb(16 + 4 * C, BF), "lk": _sb(704, BF), "lkt": _sb(1344, BF),
-    "ww": _sb(WW, BF), "slt": _sb(4 * NS, BF), "sut": _sb(2688, BF), "rl": _sb(32, U16), "dd": _sb(2 * M, BF),
+    "ww": _sb(WW, BF), "slt": _sb(4 * NS, BF), "sut": _sb(8 * M, BF), "rl": _sb(32, U16),
+    "dd": _sb(4 * M, BF), "ys": _sb(C, F32),
     "td": ("dram", [4, 128, 4], BF),
 }
-SEMAPHORES = ["cv", "cs", "ct", "cg", "dlv", "dx", "drw", "dw", "dv", "du", "dtd", "dtab", "dout",
+SEMAPHORES = ["cv", "cs", "ct", "cg", "dlv", "dx", "drw", "dw", "dv", "du", "dtd", "dtab", "dout", "dk0", "dk1",
               "sent", "atab", "ac0", "as0", "ac1", "as1", "ar0", "ar1", "ac2", "as2", "ac3", "as3"]
 ORDER = [
-    20, 5, 4, 11, 0, 1, 54, 6, 7, 180, 195, 2, 3, 8, 25, 32, 30, 27, 37, 29, 26, 17, 28, 21, 31, 9, 22, 50, 55, 35, 23, 36, 33, 177, 10, 251, 196, 47, 88, 182, 86, 73, 81, 175, 135, 12, 41, 18, 34, 19, 199, 58, 38, 57, 82, 56, 44, 61, 49, 42, 60, 163, 59, 39, 64, 230, 90, 62, 84, 63, 48, 65, 51, 66, 45, 52, 257, 67, 248, 40, 69, 256, 70, 68, 181, 169, 71, 89, 15, 218, 74, 72, 75, 219, 229, 243, 43, 76, 100, 162, 77, 78, 164, 262, 165, 174, 178, 167, 216, 85, 217, 179, 247, 46, 166, 101, 91, 53, 79, 170, 102, 83, 246, 133, 87, 16, 103, 14, 104, 172, 13, 106, 105, 136, 548, 197, 110, 205, 145, 109, 107, 108, 113, 114, 111, 112, 168, 176, 24, 115, 249, 134, 146, 119, 118, 117, 80, 204, 96, 99, 198, 116, 92, 93, 147, 98, 95, 549, 97, 94, 122, 123, 120, 121, 171, 148, 124, 245, 157, 149, 125, 144, 173, 137, 126, 130, 150, 140, 129, 151, 265, 254, 267, 261, 161, 138, 206, 152, 263, 258, 220, 242, 244, 131, 153, 154, 139, 231, 259, 156, 159, 183, 241, 142, 184, 185, 143, 186, 127, 158, 187, 274, 155, 272, 141, 276, 232, 282, 128, 271, 277, 288, 270, 269, 283, 294, 279, 278, 281, 289, 188, 280, 284, 295, 285, 291, 287, 255, 293, 273, 298, 250, 301, 252, 303, 290, 275, 296, 190, 297, 286, 200, 305, 302, 292, 299, 203, 201, 300, 202, 189, 304, 306, 209, 192, 308, 207, 191, 309, 210, 310, 193, 313, 307, 312, 314, 311, 208, 315, 211, 260, 316, 233, 542, 317, 212, 234, 227, 160, 213, 228, 333, 235, 335, 214, 336, 215, 334, 240, 221, 222, 320, 236, 224, 223, 225, 237, 226, 194, 238, 239, 318, 337, 343, 349, 355, 319, 321, 338, 344, 339, 341, 342, 350, 340, 346, 268, 345, 347, 356, 353, 550, 352, 322, 348, 253, 354, 351, 360, 359, 362, 364, 361, 357, 366, 365, 358, 326, 325, 363, 367, 327, 371, 328, 368, 132, 370, 375, 372, 369, 374, 373, 329, 376, 330, 264, 378, 331, 377, 382, 380, 381, 379, 323, 384, 383, 324, 385, 388, 389, 392, 386, 393, 387, 390, 391, 396, 397, 394, 395, 406, 266, 398, 434, 332, 403, 408, 399, 404, 405, 401, 432, 433, 407, 409, 412, 411, 410, 413, 414, 415, 416, 400, 436, 417, 402, 442, 437, 420, 443, 448, 441, 438, 440, 449, 421, 454, 439, 444, 455, 445, 422, 447, 446, 424, 435, 452, 425, 450, 423, 426, 453, 418, 427, 451, 428, 461, 459, 465, 460, 458, 429, 464, 456, 430, 463, 457, 462, 466, 419, 467, 468, 471, 469, 472, 470, 473, 474, 475, 476, 477, 478, 486, 485, 479, 487, 503, 484, 480, 431, 505, 504, 489, 482, 490, 491, 492, 488, 493, 494, 495, 497, 498, 499, 496, 500, 501, 502, 481, 507, 513, 483, 519, 508, 525, 514, 509, 512, 511, 520, 510, 515, 526, 517, 518, 516, 506, 521, 522, 529, 524, 534, 532, 527, 536, 528, 523, 533, 530, 531, 535, 537, 540, 539, 545, 538, 544, 541, 543, 546, 547, 558, 557, 551, 552, 559, 560, 561, 553, 554, 563, 562, 555, 565, 566, 564, 556,
+    10, 2, 7, 4, 3, 9, 5, 6, 1, 0, 11, 172, 8, 137, 31, 25, 28, 29, 24, 26, 12, 27, 30, 20, 187, 13, 21, 35, 52, 37, 71, 188, 32, 38, 196, 55, 53, 54, 22, 124, 44, 56, 58, 79, 34, 57, 45, 59, 62, 157, 211, 60, 61, 48, 197, 63, 64, 210, 65, 68, 66, 67, 69, 46, 221, 72, 245, 39, 70, 73, 49, 33, 158, 74, 75, 92, 42, 159, 40, 81, 156, 17, 50, 41, 19, 76, 18, 94, 93, 77, 166, 125, 222, 126, 136, 191, 83, 170, 209, 36, 47, 95, 80, 51, 121, 23, 96, 15, 97, 98, 14, 161, 138, 223, 99, 16, 100, 140, 101, 139, 553, 102, 104, 103, 105, 212, 106, 82, 141, 43, 107, 171, 108, 129, 122, 111, 142, 112, 110, 78, 115, 109, 86, 91, 114, 84, 87, 143, 89, 113, 244, 236, 165, 237, 238, 127, 90, 88, 144, 85, 116, 145, 117, 247, 198, 241, 167, 239, 240, 168, 118, 208, 151, 146, 135, 153, 498, 149, 133, 234, 148, 160, 163, 147, 189, 134, 173, 150, 152, 254, 230, 231, 256, 132, 179, 162, 243, 260, 192, 131, 258, 195, 130, 249, 176, 255, 259, 257, 219, 224, 175, 190, 193, 169, 177, 119, 194, 128, 178, 232, 182, 199, 262, 120, 263, 251, 201, 200, 253, 252, 268, 418, 269, 233, 267, 202, 274, 275, 280, 264, 265, 266, 273, 272, 281, 235, 271, 278, 270, 203, 225, 276, 181, 261, 204, 220, 284, 155, 282, 288, 279, 285, 286, 164, 277, 289, 283, 287, 250, 180, 174, 205, 290, 184, 206, 291, 292, 295, 226, 293, 294, 296, 297, 298, 246, 299, 207, 300, 554, 213, 227, 301, 214, 183, 215, 216, 185, 217, 218, 154, 228, 555, 333, 229, 335, 186, 339, 304, 336, 337, 302, 341, 347, 305, 303, 342, 353, 348, 346, 343, 344, 306, 354, 345, 352, 359, 350, 351, 360, 315, 357, 334, 349, 356, 362, 338, 363, 340, 366, 355, 367, 361, 358, 365, 364, 368, 369, 370, 248, 242, 309, 123, 371, 310, 307, 374, 372, 311, 373, 375, 376, 377, 312, 378, 313, 316, 381, 380, 385, 379, 382, 383, 384, 386, 387, 388, 392, 308, 317, 389, 390, 320, 393, 391, 394, 395, 396, 397, 314, 398, 399, 405, 321, 400, 406, 425, 412, 407, 401, 427, 408, 322, 403, 413, 428, 426, 431, 429, 414, 324, 318, 417, 323, 415, 416, 325, 409, 419, 326, 332, 410, 411, 420, 421, 327, 422, 430, 328, 423, 329, 424, 330, 319, 402, 433, 439, 404, 434, 445, 440, 451, 435, 446, 438, 436, 437, 442, 452, 444, 441, 447, 448, 450, 432, 331, 456, 454, 460, 453, 443, 458, 449, 457, 455, 459, 486, 461, 487, 488, 462, 489, 465, 490, 466, 464, 469, 463, 468, 467, 470, 473, 472, 471, 474, 480, 482, 475, 481, 479, 491, 492, 493, 505, 509, 511, 507, 508, 510, 512, 495, 496, 483, 506, 494, 497, 484, 499, 500, 501, 485, 502, 556, 476, 477, 478, 503, 504, 513, 519, 525, 531, 514, 520, 526, 515, 518, 517, 516, 521, 532, 524, 523, 527, 530, 529, 535, 533, 539, 536, 522, 537, 528, 540, 534, 538, 541, 544, 548, 545, 542, 549, 543, 546, 547, 550, 557, 551, 552, 562, 565, 559, 564, 566, 560, 561, 563, 558, 568, 567, 569, 570,
 ]
 
 
@@ -183,6 +185,24 @@ def rank_program(g, core, T, topo):
             k = min(512, a + n - c)
             act(V(name, c, c + k), V("et", 0, k), 0.0, bias)
 
+    def iota(o, pat, base=0, cm=0, fl=True, after=()):
+        if fl:
+            note("g", "c", lambda: g.iota(o[0], pat, base, cm, allow_small_or_imprecise_dtypes=True), [], [o], after=after)
+        else:
+            op("g", lambda: g.iota(o[0], pat, base, cm), [], [o])
+
+    def clear(o, q="g"):
+        if q == "g":
+            iota(o, [[0, o[4]]])
+        else:
+            act(o, V("one", 0, o[4]), 0.0)
+
+    def both(x):
+        y_ = new(64)
+        trn(V(y_, 0, 32), V(x, 0, 32))
+        trn(V(y_, 32, 64), V(x, 0, 32))
+        trn(V(x, 32, 64), V(y_, 16, 48))
+
     def scaled(q, o, i, c):
         if q == "s":
             act(o, i, c)
@@ -190,12 +210,6 @@ def rank_program(g, core, T, topo):
             cp(o, i)
         else:
             ts(o, i, c, mul)
-
-    def iota(o, pat, base=0, cm=0, fl=True):
-        if fl:
-            op("g", lambda: g.iota(o[0], pat, base, cm, allow_small_or_imprecise_dtypes=True), [], [o])
-        else:
-            op("g", lambda: g.iota(o[0], pat, base, cm), [], [o])
 
     def ramp(pat, base=0):
         n = 1
@@ -247,8 +261,8 @@ def rank_program(g, core, T, topo):
     second = [eng[2 * h:4 * h], eng[0:h], eng[h:2 * h]]
 
     def send_whole(l):
-        a, b = M * l, ZW + 4 * M * l + M * rank
-        vq_, vp_ = V("yq", a, a + M), V("yp", a, a + M)
+        b = ZW + 4 * M * l + M * rank
+        vq_, vp_ = V("fq", b, b + M), V("fp", b, b + M)
         r1 = remote([([0, 1, 2], eng, "ac%d" % l, vq_[0].bitcast(dt.uint8), T.fq[:, b:b + M].bitcast(dt.uint8))], [vq_])
         r2 = remote([([0, 1, 2], eng, "as%d" % l, vp_[0], T.fp[:, b:b + M])], [vp_, V("rl", 0, 16)], [r1])
         for nm, sem, r in (("fq", "ac%d" % l, r1), ("fp", "as%d" % l, r2)):
@@ -258,13 +272,14 @@ def rank_program(g, core, T, topo):
     def send_packed(k, sq_, sp_, a):
         prev = []
         for src, dst, sem, en in ((sq_, "bq", "ac%d" % k, first), (sp_, "bp", "as%d" % k, second)):
-            trs = []
+            trs, rd = [], []
             for e in range(3):
-                v, o = T[src][:, CAP * e:CAP * e + CAP], T[dst][:, a + CAP * slot_at[e]:a + CAP * slot_at[e] + CAP]
+                rd.append(V(src, CAP * e, CAP * e + CAP))
+                v, o = rd[-1][0], T[dst][:, a + CAP * slot_at[e]:a + CAP * slot_at[e] + CAP]
                 if dst == "bq":
                     v, o = v.bitcast(dt.uint8), o.bitcast(dt.uint8)
                 trs.append(([e], en[e], sem, v, o))
-            prev = [remote(trs, [V(src)], prev)]
+            prev = prev + [remote(trs, rd, prev[-1:])]
             landed(sem, len(eng), [V(dst, a, a + NS)], prev)
 
     last = []
@@ -286,10 +301,13 @@ def rank_program(g, core, T, topo):
         o_ = V("rw", p=(k, 128, 16))
         dma("y", "drw", o_[0], src[:], [], [o_], last)
     fill(V("rl", 0, 16), 0)
-    fill(V("keep"), 1.0)
-    fill(V("keep", 0, 90, 30), 0.0)
-    fill(V("keep", 90, 180, 3), 0.0)
-    fill(V("keep", 180, 240, 10), 0.0)
+
+    def resets(a, n, k):
+        o = V("keep", a, a + n)
+        op("g", lambda: g.affine_select(o[0], T.one[:, 0:n], [[0, n // k], [1, k]], NE, 0.0, 0, 0), [V("one")], [o])
+    resets(0, 90, 30)
+    resets(90, 90, 3)
+    resets(180, 60, 10)
     for i, m in enumerate((15, 16, 14, 1, 28, 96)):
         ts(V("pt", i, i + 1), V("pid", 0, 1), m, AND)
     pf = new(6, "col")
@@ -303,33 +321,34 @@ def rank_program(g, core, T, topo):
     half = column(p14, 0.5)
     odd = column(ph, 1.0 / 16)
 
-    def spread(b):
-        return column(column(odd, -1.0, float(b)), flip, half)
-
     def offsets(src, c, top, n, o=None):
         o = o or V(new(n, "cu"))
         ts(o, src, c, add, float(top), mn_)
         return o
 
     r8 = ramp([[8, 2]])
-    c_half = offsets(column(pr_, 3.0, column(odd, 45.0)), 2.0, 89, 1)
-    c_sig0 = offsets(spread(6), 0.0, 10, 1)
-    c_sig = offsets(V(r8), spread(11), 20, 2)
+    c_half = V(new(1, "cu"))
+    ts(c_half, column(odd, 15.0, pr_), 3.0, mul, 2.0, add)
+    c_sig0 = offsets(column(column(odd, -1.0, 6.0), flip, half), 0.0, 10, 1)
+    swap = column(flip, 32.0, half)
+    c_sig = offsets(V(r8), swap, 63, 2)
     cst = new(3, "col")
     act(V(cst), V(r5, 0, 3), float(M), column(odd, -float(M), -1.0))
-    iota(V("rj"), [[16 * 512 + 1, 15], [512 + 30, 16]], 0, 16 * 512 + 1)
+    iota(V("rj"), [[16 * 512 + 1, 15], [512 + 30, 16]], -C // 2, 16 * 512 + 1)
     c_m = column(p96, -(16 * 512 + 1.0), -(16 * 512 + 1.0))
-    c_j = column(p96, -(16 * 512 + 1.0), -(16 * 512 + 1.0) - (C - 1) / 2.0)
     zero("sw", 0, 512)
 
     def evac(bank0, tile, c, who="svsv", n=M):
         for b in range(4):
             scaled(who[b], V(tile, b, 4 * n, 4), V("ps", 512 * (bank0 + b), 512 * (bank0 + b) + n), c)
 
-    quant("sq", "ss", 0, C, V("xs"))
-    ind, cum, ib, cb, tot, tr1, ex, pre, pi, pl = [new(n) for n in (90, 90, 90, 90, 32, 32, 33, 32, 90, 90)]
-    fill(V(tot), 0.0)
-    fill(V(ex, 0, 1), 0.0)
+    for a in range(0, C, M):
+        quant("sq", "ss", a, M, V("xs", 4 * a, 4 * a + 4 * M))
+    ind, cum, ib, cb, tot, tr1, pre, pi, pl = [new(n) for n in (90, 90, 90, 90, 80, 32, 32, 90, 96)]
+    ex = (tot[0], tot[1] + 32, 33)
+    clear(V(tot, 0, 33), "s")
+    clear(V(pl, 90, 96), "s")
+    tot = (tot[0], tot[1], 32)
     for l in range(3):
         ts(V(ind, 30 * l, 30 * l + 30), V("lvn", 0, 30), l, EQ)
     for l in range(3):
@@ -342,12 +361,12 @@ def rank_program(g, core, T, topo):
     trn(V(pre), V(ex, 0, 32))
     for l in range(3):
         ts(V(pi, l, 90, 3), V(cb, 30 * l, 30 * l + 30), V(pre, l, l + 1), add, V(cst, l, l + 1), add)
-    scan(V(pl), V("keep", 90, 180), V(pi), 0.0, mx_)
+    scan(V(pl, 0, 90), V("keep", 90, 180), V(pi), 0.0, mx_)
     place = V(pl, 2, 90, 3)
     hs = new(16, "tu")
     ts(V(hs), V(pl), 16.0 - 1024.0, add, off=c_half)
     tb, tbt = new(32, "th"), new(32, "th")
-    fill(V(tb, 30, 32), 0.0)
+    clear(V(tb, 30, 32), "s")
     ts(V(tb, 0, 30), place, -1024.0 - (M - 1), add)
     trn(V(tbt), V(tb))
     v = V(tbt, 0, 16, p=(0, 32, 1))
@@ -357,18 +376,18 @@ def rank_program(g, core, T, topo):
     last = dma("y", "dw", T.wp[:], T.ws[:], [], [V("wp")], [last])
     r_ = remote([([e], first[e], "atab", T.td[rank], T.td[rank]) for e in range(3)], [tdv[rank]])
     landed("atab", len(eng), [tdv[s] for s in peers], [r_])
-    zero("tab", 0, 16, column(sel[0], -199.0, column(sel[1], 200.0)))
+    zero("tab", 0, 16, 0.5)
     for s in range(4):
-        zero("tab", 16 + C * s, C, column(sel[1], float(ZW + M + M * s)))
+        zero("tab", 16 + C * s, C, float(ZW + M + M * s))
     for gr in range(8):
         o_ = V("tab", 16, 16 + 4 * C, p=(16 * gr, 16 * gr + 1, 1))
-        dma("ys"[gr % 2], "dtab", o_[0], T.td[:, 0:C // 4, :], tdv, [o_])
+        dma("y", "dtab", o_[0], T.td[:, 0:C // 4, :], tdv, [o_])
     sca(V("sw"), V(hs, 0, 15), V("rj"))
-    a0, sig, aj, sgm = new(11), new(48, "tu"), new(21), new(32, "tu")
+    a0, sig, aj, sgm = new(11), new(48, "tu"), new(64), new(32, "tu")
     trn(V("swt", 0, 160), V("sw", 16, 176))
     trn(V("swt", 160, 352), V("sw", 0, 192))
     tt(V(a0), V("swt", 1, 352, 32), V("swt", 16, 352, 32), add)
-    ts(V(sig, 0, 16), V(a0), c_j, add, 1.0 / 512, mul, off=c_sig0)
+    ts(V(sig, 0, 16), V(a0), c_m, add, 1.0 / 512, mul, off=c_sig0)
 
     def layer(lq, lp):
         quant("xq", "xp", 0, M, V("xt"))
@@ -376,16 +395,18 @@ def rank_program(g, core, T, topo):
 
     def close(l):
         evac(4, "tl", 0.03125)
-        quant("yq", "yp", M * l, M, V("tl"))
+        if l == 2:
+            quant("yq", "yp", 2 * M, M, V("tl"))
+        else:
+            quant("fq", "fp", ZW + 4 * M * l + M * rank, M, V("tl"))
 
     pick("pq", "pss", 0, "sq", "ss", C, V(sig, 0, 10), M)
     four(0, "eq", "es", "pq", "pss", 0, M)
     evac(0, "xt", 1.0)
     layer("wq", "wp")
     close(0)
-    send_whole(0)
-    quant("fq", "fp", ZW + M * rank, M, V("tl"))
-    zero("zt", 0, 4 * ZW)
+    sent0 = send_whole(0)
+    clear(V("zt"))
     quant("fq", "fp", 0, ZW, V("zt"))
     quant("bq", "bp", 0, ZW, V("zt"))
     act(V("em", 0, 520), V("et"), column(odd, 0.5, -0.5))
@@ -395,10 +416,11 @@ def rank_program(g, core, T, topo):
             quant("eq", "es", 512 * (par + 1) + 128 * b, 128, V("em", 520 * par + 3 - b, 520 * par + 515 - b))
 
     trn(V("swt", 352, 672), V("sw", 176, 496))
-    trn(V("swt", 672, 1024), V("sw", 160, 512))
     m1, m2 = new(32, "ti"), new(32, "ti")
-    tt(V(aj), V("swt", 353, 1024, 32), V("swt", 368, 1024, 32), add)
-    ts(V(m1), V(aj), c_m, add, off=c_sig)
+    clear(V(aj, 10, 32))
+    tt(V(aj, 0, 10), V("swt", 353, 672, 32), V("swt", 368, 672, 32), add)
+    both(aj)
+    ts(V(m1), V(aj), c_m, add, C / 2.0, add, off=c_sig)
     ts(V(m2, 0, 20), V(m1, 0, 20), 511, AND)
     cp(V(sgm, 0, 20), V(m2, 0, 20))
     gs, gst, idx = new(320), new(320), new(40, "tu")
@@ -413,27 +435,28 @@ def rank_program(g, core, T, topo):
 
     ri = ramp([[32, 5], [0, 2], [1, 16]])
     own_i = column(sel[2], ph)
-    for l, base in ((0, Z1), (1, Z2)):
-        cl = column(sel[3], float(base), own_i)
-        for k in range(2):
-            a = 2 * M * l + M * k
-            act(V("kp", a, a + M), V(ri), sel[2], column(sel[4], M * k - BIG, cl))
-    r10 = ramp([[10, 2]])
+    cl = column(sel[3], float(Z1), own_i)
+    for k in range(2):
+        act(V("kp", M * k, M * k + M), V(ri), sel[2], column(sel[4], 2 * M * k - BIG, cl))
+    act(V("kp", 2 * M, 4 * M), V("kp", 0, 2 * M), 1.0, column(sel[3], float(Z2 - Z1)))
+    r10 = ramp([[22, 2], [10, 2]])
     c_fwd = new(4, "cu")
-    offsets(V(r10), column(odd, 20.0, pr_), 41, 2, V(c_fwd, 0, 4, 2))
-    offsets(V(r10), column(odd, -22.0, column(pr_, 1.0, 22.0)), 41, 2, V(c_fwd, 1, 4, 2))
+    offsets(V(r10, 0, 2), column(odd, 20.0, pr_), 41, 2, V(c_fwd, 0, 4, 2))
+    offsets(V(r10, 2, 4), column(odd, -22.0, pr_), 41, 2, V(c_fwd, 1, 4, 2))
     fr = [new(64, "tu"), new(64, "tu")]
     for a in (0, 336, 688):
-        fill(V("lk", a, a + (32 if a == 336 else 16)), 0.0)
+        clear(V("lk", a, a + (32 if a == 336 else 16)))
     for l in range(2):
         a, w0 = 352 * l, 672 * l
-        ttg(V("lk", a + 16, a + 336), V("tab"), V(idx, 20 * l, 20 * l + 20), V("kp", 2 * M * l, 2 * M * l + 2 * M), add)
+        gat("s", V("lk", a + 16, a + 336), V("tab"), V(idx, 20 * l, 20 * l + 20))
+        o_, i_ = V("kp", 2 * M * l, 2 * M * l + 2 * M, p=(0, 128, 16)), V("lk", a + 16, a + 336, p=(0, 128, 16))
+        dma("y", "dk%d" % l, o_[0], i_[0], [i_], [o_])
         trn(V("lkt", w0, w0 + 320), V("lk", a + 16, a + 336))
         trn(V("lkt", w0 + 320, w0 + 672), V("lk", a, a + 352))
         d1, d2, d3 = new(42), new(42), new(42)
         tt(V(d1), V("lkt", w0, w0 + 672, 16), V("lkt", w0 + 1, w0 + 672, 16), add)
         if l == 1:
-            ts(V(d2), V("lkt", w0, w0 + 672, 16), 0.0, GT, float(3 * M), mul)
+            ts(V(d2), V("lkt", w0, w0 + 672, 16), 0.75, GT, float(3 * M), mul)
             tt(V(d3), V(d1), V(d2), add)
             d1 = d3
         ts(V(fr[l]), V(d1), -1.0, add, off=V(c_fwd))
@@ -449,8 +472,8 @@ def rank_program(g, core, T, topo):
     ts(V(si), V(idx), -16.0 - (C - 1) / 2.0, add, 1.0 / C, mul)
     for e in range(3):
         ts(V(in2, 40 * e, 40 * e + 40), V(si), peers[e], EQ)
-    fill(V(cu2, 120, 128), 0.0)
-    fill(V(tb2), 0.0)
+    clear(V(cu2, 120, 128))
+    clear(V(tb2))
     act(V(ex2, 0, 1), init)
     for par in range(2):
         scan(V(cu2, par, 120, 2), V("keep", 180, 240), V(in2, par, 120, 2))
@@ -464,7 +487,7 @@ def rank_program(g, core, T, topo):
     k1 = ramp([[2 * NS, 2], [0, 10], [16, 2]], int(BIG))
     kk = new(40, "cf")
     for l in range(2):
-        iota(V(kk, 20 * l, 20 * l + 20), [[M, 2], [0, 5], [512, 2]], S0 + M - 1)
+        iota(V(kk, 20 * l, 20 * l + 20), [[2 * M, 2], [0, 5], [PS, 2]], S0 + M - 1)
     rdm, dm = ramp([[0, 2], [16, 20]], D0), new(40)
     act(V(dm), V(rdm), 1.0, pr_)
     tt(V(f1), V(pd, 0, 40), V(pd, 40, 80), add)
@@ -480,51 +503,45 @@ def rank_program(g, core, T, topo):
     act(V(c2), V(n16, 0, 3), 16.0, column(flip, 336.0))
     tt(V(c3), V(c1), V(c2), add)
     c_own = offsets(V(c3), 0.0, 1343, 3)
-    vo, u1, u2, u3, u4, iof = new(48), new(40), new(40), new(40), new(40), new(40, "tu")
+    vo, u3, u4, iof = new(48), new(40), new(40), new(40, "tu")
     gat("v", V(vo), V("lkt"), c_own)
-    ts(V(u1), V(vo, 0, 40), 0.0, GT, 1024.0 - M, mul)
-    tt(V(u2), V(vo, 0, 40), V(k2), add)
-    tt(V(u3), V(u2), V(u1), add)
+    tt(V(u3), V(vo, 0, 40), V(k2), add)
     tt(V(u4), V(u3), V(f6), mn_)
     cp(V(iof), V(u4))
-    zero("ww", 0, S0 + 2 * M + 16)
-    for a in range(1, 4):
-        zero("ww", S0 + 512 * a - 16, 2 * M + 32)
+    for a, n in ((0, 2 * NS), (2 * NS, 2 * NS), (S0, 2 * M), (S0 + 2 * M, 2 * M), (S0 + PS, 2 * M), (S0 + PS + 2 * M, 2 * M)):
+        iota(V("ww", a, a + n), [[0, n]], after=[sent0])
 
     rq, bs = new(32, "tu"), new(24, "tu")
     rqq = new(12, "cf")
     for e in range(3):
         iota(V(rqq, 4 * e, 4 * e + 4), [[16, 4]], CAP * slot_at[e])
     dq = [new(12), new(12)]
-    act(V(dq[0]), V(rqq), 1.0, column(pr_, 1.0, 2 * M - (M - 1) - BIG))
-    act(V(dq[1]), V(rqq), 1.0, column(ph, -32.0, column(pr_, 1.0, D0 - S0 - (M - 1) - BIG)))
-    at2, at1 = column(ph, 32.0, S0 + M - 1 + BIG), column(ph, 32.0, float(S0))
+    act(V(dq[0]), V(rqq), 1.0, column(pr_, 1.0, 4 * M - (M - 1) - BIG))
+    act(V(dq[1]), V(dq[0]), 1.0, column(ph, -PS / 16.0, float(D0 - S0 - 4 * M)))
+    at1 = column(ph, PS / 16.0, float(S0))
 
     def requests(l, after):
         w0 = 2 * NS * l
-        sca(V("ww"), V(iof, 20 * l, 20 * l + 20), V("lk", 352 * l + 16, 352 * l + 336))
+        for k in range(2):
+            sca(V("ww"), V(iof, 20 * l + 10 * k, 20 * l + 10 * k + 10), V("kp", 2 * M * l + M * k, 2 * M * l + M * k + M))
         trn(V("slt", w0, w0 + 2 * NS), V("ww", w0, w0 + 2 * NS))
 
         def row(k, st=16):
             return V("slt", w0 + k, w0 + 2 * NS, st)
-        n1, n2, n3, n4, n5, n6 = new(24), new(24), new(24), new(12), new(12), new(12)
+        n1, n4, n5, n6 = new(24), new(12), new(12), new(12)
         tt(V(n6), row(2, 32), row(18, 32), add)
         cp(V(bs, 12 * l, 12 * l + 12), V(n6))
         tt(V(n1), row(0), row(4), add)
-        if l == 1:
-            ts(V(n2), row(0), 0.0, GT, 1024.0 - M, mul)
-            tt(V(n3), V(n1), V(n2), add)
-            n1 = n3
         tt(V(n4), V(n1, 0, 24, 2), V(n1, 1, 24, 2), add)
         tt(V(n5), V(n4), V(dq[l]), mn_)
         if l == 1:
-            ts(V(rq, 16, 28), V(n5), at2, add)
+            ts(V(rq, 16, 28), V(n5), at1, add, M - 1 + BIG, add)
         else:
             n7, m_ = new(12, "ti"), new(12, "ti")
             ts(V(n7), V(n5), M - 1 + BIG, add)
-            ts(V(m_, 0, 3), V(n5, 3, 12, 4), M - 1 + BIG, add, 512.0, mul)
-            ts(V(m_, 4, 7), V(m_, 0, 3), 127 * 512, AND)
-            ts(V(m_, 8, 11), V(m_, 0, 3), 7, SHR, 127 * 512, AND)
+            ts(V(m_, 0, 3), V(n5, 3, 12, 4), M - 1 + BIG, add, 1024.0, mul)
+            ts(V(m_, 4, 7), V(m_, 0, 3), 63 * 1024, AND)
+            ts(V(m_, 8, 11), V(m_, 0, 3), 6, SHR, 63 * 1024, AND)
             tt(V(n7, 0, 12, 4), V(n7, 0, 12, 4), V(m_, 4, 7), add)
             tt(V(n7, 1, 12, 4), V(n7, 1, 12, 4), V(m_, 8, 11), add)
             cp(V(rq, 0, 12), V(n7))
@@ -533,52 +550,48 @@ def rank_program(g, core, T, topo):
                     for e in range(3)], [V(rq, a, a + 12)], after)
         landed("ar%d" % l, len(eng), [V("rl", a, a + 12)], [r])
 
-    rs, r5k = ramp([[1, NS]]), ramp([[5, 2]])
-    c_su = new(4, "cu")
-    offsets(V(r5k), spread(21), 41, 2, V(c_su, 0, 2))
-    offsets(V(r5k), column(column(odd, -1.0, 22.0), flip, column(half, 1.0, 10.0)), 41, 2, V(c_su, 2, 4))
+    rs, r5k = ramp([[1, NS]]), ramp([[5, 4]])
+    c_su = offsets(V(r5k), swap, 63, 4)
     for l, base in ((0, A1), (1, A2)):
         act(V("pb", NS * l, NS * l + NS), V(rs), sel[2], column(sel[3], float(base)))
     br = [new(64, "tu"), new(64, "tu")]
 
     def successors(l):
         if l == 1:
-            sca(V("ww"), V("rl", 16, 28), V("pb", NS, 2 * NS))
+            for a in (0, 6):
+                sca(V("ww"), V("rl", 16 + a, 22 + a), V("pb", NS + 16 * a, NS + 16 * a + 96))
         else:
             u, lo, hi, ao = new(24, "ti"), new(12, "ti"), new(8, "ti"), new(12, "tu")
             cp(V(u, 0, 12), V("rl", 0, 12))
-            ts(V(lo), V(u, 0, 12), 511, AND)
-            ts(V(hi, 0, 3), V(u, 0, 12, 4), 9, SHR)
-            ts(V(hi, 4, 7), V(u, 1, 12, 4), 2, SHR, 384, AND)
+            ts(V(lo), V(u, 0, 12), 1023, AND)
+            ts(V(hi, 0, 3), V(u, 0, 12, 4), 10, SHR)
+            ts(V(hi, 4, 7), V(u, 1, 12, 4), 4, SHR, 63 * 64, AND)
             tt(V(lo, 3, 12, 4), V(hi, 0, 3), V(hi, 4, 7), add)
             ts(V(ao), V(lo), at1, add)
-            sca(V("ww"), V(ao), V("pb", 0, NS))
-        w0 = 1344 * l
-        for par in range(2):
-            s0 = S0 + 1024 * l + 512 * par
-            trn(V("sut", w0 + 320 * par, w0 + 320 * par + 320), V("ww", s0, s0 + 320))
-            trn(V("sut", w0 + 640 + 352 * par, w0 + 992 + 352 * par), V("ww", s0 - 16, s0 + 336))
-        q2, q3 = new(84), new(42)
-        tt(V(q2), V("sut", w0 + 2, w0 + 1344, 16), V("sut", w0 + 3, w0 + 1344, 16), add)
-        tt(V(q3), V(q2, 0, 84, 2), V(q2, 1, 84, 2), add)
-        gat("v", V(br[l]), V(q3), V(c_su))
-
-    def make(kq, kp_, wq_, wp_, wn, lst, par_of, dq_, dp_, da, lq, lp):
-        for b in (1, 3):
-            mm(4 + b, "eq", "es", b, dq_, dp_, da, M)
-            act(V("dd", M * (b // 2), M * (b // 2) + M), V("ps", 512 * (4 + b), 512 * (4 + b) + M))
+            for a in (0, 6):
+                sca(V("ww"), V(ao, a, a + 6), V("pb", 16 * a, 16 * a + 96))
+        w0 = 4 * M * l
         for i in range(4):
-            pick(kq, kp_, M * i, wq_, wp_, wn, V(lst, 16 * i, 16 * i + 10), M)
-            for b in range(4):
-                mm(b, "eq", "es", 4 * (par_of[i] + 1) + b, kq, kp_, M * i, M, i == 0, i == 3 and b % 2 == 1)
-                if i == 3 and b % 2 == 0:
-                    mm(b, "eq", "es", b, dq_, dp_, da, M, False, True)
+            s0 = S0 + PS * (i // 2) + 2 * M * (i % 2) + M * l
+            trn(V("sut", w0 + M * i, w0 + M * i + M), V("ww", s0, s0 + M))
+        q2, q3 = new(40), new(64)
+        clear(V(q3, 20, 32))
+        tt(V(q2), V("sut", w0 + 2, w0 + 4 * M, 16), V("sut", w0 + 3, w0 + 4 * M, 16), add)
+        tt(V(q3, 0, 20), V(q2, 0, 40, 2), V(q2, 1, 40, 2), add)
+        both(q3)
+        gat("v", V(br[l]), V(q3), c_su)
+
+    def make(kq, kp_, wq_, wp_, wn, lst, lists, dq_, dp_, da, lq, lp):
         for b in range(4):
-            o, p_ = V("xt", b, 4 * M, 4), V("ps", 512 * b, 512 * b + M)
-            if b % 2 == 0:
-                act(o, p_)
-            else:
-                tt(o, p_, V("dd", M * (b // 2), M * (b // 2) + M), add)
+            mm(4 + b, "eq", "es", b, dq_, dp_, da, M)
+            act(V("dd", M * b, M * b + M), V("ps", 512 * (4 + b), 512 * (4 + b) + M))
+        for i in range(4):
+            j = lists[i]
+            pick(kq, kp_, M * i, wq_, wp_, wn, V(lst, 16 * j, 16 * j + 10), M)
+            for b in range(4):
+                mm(b, "eq", "es", 4 * (i // 2 + 1) + b, kq, kp_, M * i, M, i == 0, i == 3)
+        for b in range(4):
+            tt(V("xt", b, 4 * M, 4), V("ps", 512 * b, 512 * b + M), V("dd", M * b, M * b + M), add)
         layer(lq, lp)
 
     def pack(l, k, sq_, sp_, a, own):
@@ -595,41 +608,49 @@ def rank_program(g, core, T, topo):
     dma("y", "dv", T.vq[:].bitcast(dt.uint8), T.vc[:], arrived, [V("vq")])
     dma("y", "dv", T.vp[:], T.vs[:], arrived, [V("vp")])
     dma("y", "du", T.us[:], T.u[:], arrived, [V("us")])
-    make("k1q", "k1p", "fq", "fp", ZW + 4 * M, fr[0], (0, 1, 0, 1), "pq", "pss", M, "wq", "wp")
+    make("k1q", "k1p", "fq", "fp", ZW + 4 * M, fr[0], (0, 2, 1, 3), "pq", "pss", M, "wq", "wp")
     close(1)
     last = send_whole(1)
-    quant("fq", "fp", ZW + 4 * M + M * rank, M, V("tl"))
     requests(1, [last])
+    requests(0, [last])
 
-    make("k2q", "k2p", "fq", "fp", ZW + 8 * M, fr[1], (0, 1, 0, 1), "pq", "pss", 2 * M, "wq", "wp")
+    quant("uq", "up", 0, 128, V("us"))
+
+    def result(l, a):
+        mm(l, "uq", "up", 0, "bq", "bp", a, M)
+        act(V("ys", M * l, M * l + M), V("ps", 512 * l, 512 * l + M))
+
+    make("k2q", "k2p", "fq", "fp", ZW + 8 * M, fr[1], (0, 2, 1, 3), "pq", "pss", 2 * M, "wq", "wp")
     close(2)
     four(0, "eq", "es", "yq", "yp", 2 * M, M)
     evac(0, "xt", 1.0)
     layer("vq", "vp")
     pack(1, 2, "scq", "scp", A2, Z2)
+    result(2, Z2)
 
     successors(1)
-    requests(0, [])
-    make("k3q", "k3p", "bq", "bp", Z1, br[1], (0, 0, 1, 1), "yq", "yp", M, "vq", "vp")
+    make("k3q", "k3p", "bq", "bp", Z1, br[1], (0, 1, 2, 3), "fq", "fp", ZW + 4 * M + M * rank, "vq", "vp")
     pack(0, 3, "sdq", "sdp", A1, Z1)
+    result(1, Z1)
     successors(0)
-    make("k4q", "k4p", "bq", "bp", Z0, br[0], (0, 0, 1, 1), "yq", "yp", 0, "vq", "vp")
-    quant("uq", "up", 0, 128, V("us"))
+    make("k4q", "k4p", "bq", "bp", Z0, br[0], (0, 1, 2, 3), "fq", "fp", ZW + M * rank, "vq", "vp")
     evac(4, "tl", 0.03125)
     quant("bq", "bp", Z0, M, V("tl"))
+    result(0, Z0)
 
     g1, g2, pij = new(30), new(30), new(30, "tu")
     ts(V(g1), V("lvn", 0, 30), float(Z1 - M - Z0), mul, Z0 - 1024.0, add)
     tt(V(g2), V(g1), place, add)
     cp(V(pij), V(g2))
+    plc = new(30, "tu")
+    ts(V(plc), place, -1024.0, add)
     for i, (a, n) in enumerate(((0, 256), (256, 224))):
-        pick("oq", "op", a, "bq", "bp", Z0 + M, V(pij, a // 16, (a + n) // 16), n)
+        pick("oq", "op", a, "bq", "bp", Z0 + M, V(pij, a // 16, (a + n) // 16), n, "v")
         dma("y", "dout", T.oc[:, 4 * a:4 * a + 4 * n], T.oq[:, a:a + n].bitcast(dt.uint8), [V("oq", a, a + n)], [])
-        mm(i, "uq", "up", 0, "oq", "op", a, n)
-        scaled("vs"[i], V("yo", a, a + n), V("ps", 512 * i, 512 * i + n), 1.0)
+        gat("s", V("yo", a, a + n), V("ys"), V(plc, a // 16, (a + n) // 16))
         dma("sy"[i], "dout", T.y[:, a:a + n], T.yo[:, a:a + n], [V("yo", a, a + n)], [])
     for k in range(4):
-        dma("y", "dout", T.osc[4 * k:4 * k + 4, :], T.op[32 * k:32 * k + 4, :], [V("op")], [])
+        dma("ys"[k % 2], "dout", T.osc[4 * k:4 * k + 4, :], T.op[32 * k:32 * k + 4, :], [V("op")], [])
 
     group = {}
     for i, o_ in enumerate(ops):

from concourse.bass import DstId, RemoteDMATransfer
from concourse.mybir import dt, AluOpType, ActivationFunctionType, AxisListType

C, M, CAP = 480, 160, 64
NS = 3 * CAP
ZW = 128
Z2, A2, Z1, A1, Z0 = ZW, ZW + M, ZW + M + NS, ZW + 2 * M + NS, ZW + 2 * M + 2 * NS
S0 = 4 * NS
PS = 4 * M + NS
D0 = S0 + PS + 4 * M
WW = D0 + 2 * M
BIG = 4096.0
Q4, U8, BF, F32, I32, U16 = "float8_e4m3fn_x4", "uint8", "bfloat16", "float32", "int32", "uint16"


def _sb(n, d):
    return ("sbuf", [128, n], d)


SCRATCH = {
    "ps": ("psum", [128, 4096], F32),
    "xs": _sb(4 * C, BF), "sq": _sb(C, Q4), "ss": _sb(C, U8), "pq": _sb(C, Q4), "pss": _sb(C, U8),
    "et": _sb(520, BF), "em": _sb(2 * 520, BF), "eq": _sb(1536, Q4), "es": _sb(1536, U8), "one": _sb(128, BF),
    "zt": _sb(4 * ZW, BF),
    "wq": _sb(512, Q4), "wp": _sb(512, U8), "vq": _sb(512, Q4), "vp": _sb(512, U8),
    "us": _sb(512, BF), "uq": _sb(128, Q4), "up": _sb(128, U8),
    "xt": _sb(4 * M, BF), "xq": _sb(M, Q4), "xp": _sb(M, U8), "tl": _sb(4 * M, BF),
    "yq": _sb(C, Q4), "yp": _sb(C, U8), "oq": _sb(C, Q4), "op": _sb(C, U8),
    "fq": _sb(ZW + 8 * M, Q4), "fp": _sb(ZW + 8 * M, U8), "bq": _sb(Z0 + M, Q4), "bp": _sb(Z0 + M, U8),
    "k1q": _sb(4 * M, Q4), "k1p": _sb(4 * M, U8), "k2q": _sb(4 * M, Q4), "k2p": _sb(4 * M, U8),
    "k3q": _sb(4 * M, Q4), "k3p": _sb(4 * M, U8), "k4q": _sb(4 * M, Q4), "k4p": _sb(4 * M, U8),
    "tp": _sb(4 * M, BF), "st": _sb(4 * NS, BF), "yo": _sb(C, F32),
    "scq": _sb(NS, Q4), "scp": _sb(NS, U8), "sdq": _sb(NS, Q4), "sdp": _sb(NS, U8),
    "pid": _sb(2, I32), "pt": _sb(8, I32), "col": _sb(96, F32), "cf": _sb(2048, F32), "cu": _sb(160, U16),
    "keep": _sb(240, BF), "rj": _sb(240, F32), "kp": _sb(4 * M, BF), "pb": _sb(2 * NS, BF),
    "lvn": _sb(32, I32), "rw": _sb(C, I32), "sw": _sb(512, F32), "swt": _sb(1024, F32),
    "tf": _sb(4096, F32), "ti": _sb(512, I32), "tu": _sb(768, U16), "th": _sb(512, BF),
    "tab": _sb(16 + 4 * C, BF), "lk": _sb(704, BF), "lkt": _sb(1344, BF),
    "ww": _sb(WW, BF), "slt": _sb(4 * NS, BF), "sut": _sb(8 * M, BF), "rl": _sb(32, U16),
    "dd": _sb(4 * M, BF), "ys": _sb(C, F32),
    "td": ("dram", [4, 128, 4], BF),
}
SEMAPHORES = ["cv", "cs", "ct", "cg", "dlv", "dx", "drw", "dw", "dv", "du", "dtd", "dtab", "dout", "dk0", "dk1",
              "sent", "atab", "ac0", "as0", "ac1", "as1", "ar0", "ar1", "ac2", "as2", "ac3", "as3"]
ORDER = [
    10, 2, 7, 4, 3, 9, 5, 6, 1, 0, 11, 172, 8, 137, 31, 25, 28, 29, 24, 26, 12, 27, 30, 20, 187, 13, 21, 35, 52, 37, 71, 188, 32, 38, 196, 55, 53, 54, 22, 124, 44, 56, 58, 79, 34, 57, 45, 59, 62, 157, 211, 60, 61, 48, 197, 63, 64, 210, 65, 68, 66, 67, 69, 46, 221, 72, 245, 39, 70, 73, 49, 33, 158, 74, 75, 92, 42, 159, 40, 81, 156, 17, 50, 41, 19, 76, 18, 94, 93, 77, 166, 125, 222, 126, 136, 191, 83, 170, 209, 36, 47, 95, 80, 51, 121, 23, 96, 15, 97, 98, 14, 161, 138, 223, 99, 16, 100, 140, 101, 139, 553, 102, 104, 103, 105, 212, 106, 82, 141, 43, 107, 171, 108, 129, 122, 111, 142, 112, 110, 78, 115, 109, 86, 91, 114, 84, 87, 143, 89, 113, 244, 236, 165, 237, 238, 127, 90, 88, 144, 85, 116, 145, 117, 247, 198, 241, 167, 239, 240, 168, 118, 208, 151, 146, 135, 153, 498, 149, 133, 234, 148, 160, 163, 147, 189, 134, 173, 150, 152, 254, 230, 231, 256, 132, 179, 162, 243, 260, 192, 131, 258, 195, 130, 249, 176, 255, 259, 257, 219, 224, 175, 190, 193, 169, 177, 119, 194, 128, 178, 232, 182, 199, 262, 120, 263, 251, 201, 200, 253, 252, 268, 418, 269, 233, 267, 202, 274, 275, 280, 264, 265, 266, 273, 272, 281, 235, 271, 278, 270, 203, 225, 276, 181, 261, 204, 220, 284, 155, 282, 288, 279, 285, 286, 164, 277, 289, 283, 287, 250, 180, 174, 205, 290, 184, 206, 291, 292, 295, 226, 293, 294, 296, 297, 298, 246, 299, 207, 300, 554, 213, 227, 301, 214, 183, 215, 216, 185, 217, 218, 154, 228, 555, 333, 229, 335, 186, 339, 304, 336, 337, 302, 341, 347, 305, 303, 342, 353, 348, 346, 343, 344, 306, 354, 345, 352, 359, 350, 351, 360, 315, 357, 334, 349, 356, 362, 338, 363, 340, 366, 355, 367, 361, 358, 365, 364, 368, 369, 370, 248, 242, 309, 123, 371, 310, 307, 374, 372, 311, 373, 375, 376, 377, 312, 378, 313, 316, 381, 380, 385, 379, 382, 383, 384, 386, 387, 388, 392, 308, 317, 389, 390, 320, 393, 391, 394, 395, 396, 397, 314, 398, 399, 405, 321, 400, 406, 425, 412, 407, 401, 427, 408, 322, 403, 413, 428, 426, 431, 429, 414, 324, 318, 417, 323, 415, 416, 325, 409, 419, 326, 332, 410, 411, 420, 421, 327, 422, 430, 328, 423, 329, 424, 330, 319, 402, 433, 439, 404, 434, 445, 440, 451, 435, 446, 438, 436, 437, 442, 452, 444, 441, 447, 448, 450, 432, 331, 456, 454, 460, 453, 443, 458, 449, 457, 455, 459, 486, 461, 487, 488, 462, 489, 465, 490, 466, 464, 469, 463, 468, 467, 470, 473, 472, 471, 474, 480, 482, 475, 481, 479, 491, 492, 493, 505, 509, 511, 507, 508, 510, 512, 495, 496, 483, 506, 494, 497, 484, 499, 500, 501, 485, 502, 556, 476, 477, 478, 503, 504, 513, 519, 525, 531, 514, 520, 526, 515, 518, 517, 516, 521, 532, 524, 523, 527, 530, 529, 535, 533, 539, 536, 522, 537, 528, 540, 534, 538, 541, 544, 548, 545, 542, 549, 543, 546, 547, 550, 557, 551, 552, 562, 565, 559, 564, 566, 560, 561, 563, 558, 568, 567, 569, 570,
]


def rank_program(g, core, T, topo):
    rank = T.rank_of(core)
    if rank is None:
        return
    cores = list(T.cores)
    add, mul, mx_, mn_ = AluOpType.add, AluOpType.mult, AluOpType.max, AluOpType.min
    EQ, NE, GT, GE = AluOpType.is_equal, AluOpType.not_equal, AluOpType.is_gt, AluOpType.is_ge
    AND, SHR = AluOpType.bitwise_and, AluOpType.arith_shift_right
    COPY, IDENT = ActivationFunctionType.Copy, ActivationFunctionType.Identity

    def peers_of(r):
        def near(s):
            a, b = topo.chip(cores[r]), topo.chip(cores[s])
            return 2 if topo.mates(a, b) else (1 if topo.same_plane(a, b) else 0)
        return sorted([s for s in range(len(cores)) if s != r], key=lambda s: (near(s), s))

    peers = peers_of(rank)
    slot_at = [peers_of(s).index(rank) for s in peers]

    queues = {"v": g.vector, "s": g.scalar, "t": g.tensor, "g": g, "y": g.sync}
    csem = {"v": "cv", "s": "cs", "t": "ct", "g": "cg"}
    ops = []
    hist = {}
    used = {"tf": 0, "ti": 0, "tu": 0, "th": 0, "cf": 0, "cu": 0, "col": 0}

    def bits(a, b, st):
        if st == 1:
            return ((1 << (b - a)) - 1) << a
        m = 0
        for i in range(a, b, st):
            m |= 1 << i
        return m

    def V(name, a=0, b=None, st=1, p=(0, 128, 1)):
        if isinstance(name, tuple):
            name, base, n = name
            a, b = base + a, base + (n if b is None else b)
        if b is None:
            b = SCRATCH[name][1][-1]
        t = T[name]
        ap = t[p[0]:p[1]:p[2], a:b:st] if (st != 1 or p[2] != 1) else t[p[0]:p[1], a:b]
        cm = bits(a, b, st)
        if name == "ps":
            cm = bits(512 * (a // 512), 512 * ((b - 1) // 512 + 1), 1)
        return (ap, name, bits(p[0], p[1], p[2]), cm, len(range(a, b, st)))

    def new(n, pool="tf"):
        a = used[pool]
        used[pool] += n if pool == "col" else -(-n // 16) * 16
        assert used[pool] <= SCRATCH[pool][1][1]
        return (pool, a, n)

    def note(q, kind, fn, reads, writes, sem=None, n=0, after=()):
        deps, soft = set(after), set(after)
        for views, w in ((reads, False), (writes, True)):
            for v_ in views:
                for (j, pm2, cm2, w2) in hist.get(v_[1], []):
                    if (w or w2 or v_[1] == "ps") and (v_[2] & pm2) and (v_[3] & cm2):
                        deps.add(j)
                        if q == "t" and ops[j]["q"] == "t":
                            soft.add(j)
        i = len(ops)
        ops.append({"q": q, "kind": kind, "fn": fn, "sem": sem, "n": n, "deps": deps, "soft": soft})
        for views, w in ((reads, False), (writes, True)):
            for v_ in views:
                hist.setdefault(v_[1], []).append((i, v_[2], v_[3], w))
        return i

    def op(q, fn, reads, writes):
        return note(q, "c", fn, reads, writes)

    def dma(q, sem, out, in_, reads, writes, after=()):
        return note(q, "d", lambda: queues[q].dma_start(out, in_), reads, writes, sem, 16, after)

    def landed(sem, n, views, after):
        return note(None, "l", None, [], views, sem, n, after)

    def cp(o, i):
        op("v", lambda: g.vector.tensor_copy(o[0], i[0]), [i], [o])

    def fill(o, c):
        op("v", lambda: g.vector.memset(o[0], c), [], [o])

    def tt(o, a, b, f):
        op("v", lambda: g.vector.tensor_tensor(o[0], a[0], b[0], f), [a, b], [o])

    def ts(o, a, s1, f1, s2=None, f2=None, off=None):
        rd = [a] + [s for s in (s1, s2, off) if isinstance(s, tuple)]
        x1 = s1[0] if isinstance(s1, tuple) else s1
        x2 = s2[0] if isinstance(s2, tuple) else s2
        src = a[0] if off is None else a[0].indirect(off[0])
        if f2 is None:
            op("v", lambda: g.vector.tensor_scalar(o[0], src, x1, None, f1), rd, [o])
        else:
            op("v", lambda: g.vector.tensor_scalar(o[0], src, x1, x2, f1, f2), rd, [o])

    def ttg(o, w, off, b, f):
        op("v", lambda: g.vector.tensor_tensor(o[0], w[0].indirect(off[0]), b[0], f), [w, off, b], [o])

    def gat(q, o, w, off):
        if q == "v":
            op("v", lambda: g.vector.tensor_copy(o[0], w[0].indirect(off[0])), [w, off], [o])
        else:
            op("s", lambda: g.scalar.activation(o[0], w[0].indirect(off[0]), COPY), [w, off], [o])

    def sca(w, off, i):
        op("v", lambda: g.vector.tensor_copy(w[0].indirect(off[0]), i[0]), [i, off], [w])

    def scan(o, k, d, init=0.0, f=add):
        x = init[0] if isinstance(init, tuple) else init
        op("v", lambda: g.vector.tensor_tensor_scan(o[0], k[0], d[0], x, mul, f), [k, d] + ([init] if isinstance(init, tuple) else []), [o])

    def trn(o, i):
        op("v", lambda: g.vector.transpose(o[0], i[0]), [i], [o])

    def total_of(o, i):
        op("v", lambda: g.vector.tensor_reduce(o[0], i[0], AxisListType.X, add), [i], [o])

    def act(o, i, scale=1.0, bias=None, f=None):
        rd = [i] + [s for s in (scale, bias) if isinstance(s, tuple)]
        sc_ = scale[0] if isinstance(scale, tuple) else scale
        if bias is None:
            f = f or (IDENT if isinstance(scale, tuple) else COPY)
            op("s", lambda: g.scalar.activation(o[0], i[0], f, scale=sc_), rd, [o])
        else:
            b_ = bias[0] if isinstance(bias, tuple) else bias
            op("s", lambda: g.scalar.activation(o[0], i[0], f or IDENT, bias=b_, scale=sc_), rd, [o])

    def column(i, scale=1.0, bias=None, f=None):
        o = V(new(1, "col"))
        act(o, i, scale, bias, f)
        return o

    def zero(name, a, n, bias=None):
        for c in range(a, a + n, 512):
            k = min(512, a + n - c)
            act(V(name, c, c + k), V("et", 0, k), 0.0, bias)

    def iota(o, pat, base=0, cm=0, fl=True, after=()):
        if fl:
            note("g", "c", lambda: g.iota(o[0], pat, base, cm, allow_small_or_imprecise_dtypes=True), [], [o], after=after)
        else:
            op("g", lambda: g.iota(o[0], pat, base, cm), [], [o])

    def clear(o, q="g"):
        if q == "g":
            iota(o, [[0, o[4]]])
        else:
            act(o, V("one", 0, o[4]), 0.0)

    def both(x):
        y_ = new(64)
        trn(V(y_, 0, 32), V(x, 0, 32))
        trn(V(y_, 32, 64), V(x, 0, 32))
        trn(V(x, 32, 64), V(y_, 16, 48))

    def scaled(q, o, i, c):
        if q == "s":
            act(o, i, c)
        elif c == 1.0:
            cp(o, i)
        else:
            ts(o, i, c, mul)

    def ramp(pat, base=0):
        n = 1
        for _, k in pat:
            n *= k
        o = new(n, "cf")
        iota(V(o), pat, base)
        return o

    def quant(qn, pn, a, n, i):
        o, s_ = V(qn, a, a + n), V(pn, a, a + n)
        op("v", lambda: g.vector.quantize_mx(o[0], s_[0], i[0]), [i], [o, s_])

    def mm(bank, lq, lp, b, rq, rp, a, n, start=True, stop=True):
        o, l1, l2 = V("ps", 512 * bank, 512 * bank + n), V(lq, 128 * b, 128 * b + 128), V(lp, 128 * b, 128 * b + 128)
        r1, r2 = V(rq, a, a + n), V(rp, a, a + n)
        op("t", lambda: g.tensor.matmul_mx(o[0], l1[0], l2[0], r1[0], r2[0], start, stop), [l1, l2, r1, r2], [o])

    def four(bank0, lq, lp, rq, rp, a, n):
        for b in range(4):
            mm(bank0 + b, lq, lp, b, rq, rp, a, n)

    def pick(oq, op_, a, sq_, sp_, n, f, k, who="s"):
        o, w = V(oq, a, a + k), V(sq_, 0, n)
        op("v", lambda: g.vector.tensor_copy(o[0].bitcast(dt.uint32), w[0].bitcast(dt.uint32).indirect(f[0])), [w, f], [o])
        gat(who, V(op_, a, a + k), V(sp_, 0, n), f)

    eng = topo.engines(core, cores[peers[0]])
    for s in peers:
        eng = [e for e in eng if e in topo.engines(core, cores[s])]
    h = len(eng) // 4

    def emask(es):
        m = 0
        for e in es:
            m |= 1 << e
        return m

    def remote(trs, reads, after=()):
        def fn():
            out = []
            for es_, en, sem, src, dst in trs:
                ids = [DstId(rid=topo.addr(cores[peers[e]])[0], pnc=topo.addr(cores[peers[e]])[1]) for e in es_]
                out.append(RemoteDMATransfer(dst_ids=ids, dma_engine_mask=emask(en), remote_sem=T.sem[sem], srcs=[src], dsts=[dst] * len(ids)))
            return g.remote_dma_fused(out, local_sem=T.sem.sent)
        return note("g", "r", fn, reads, [], "sent", sum(len(t_[1]) for t_ in trs), after)

    first = [eng[0:2 * h], eng[2 * h:3 * h], eng[3 * h:4 * h]]
    second = [eng[2 * h:4 * h], eng[0:h], eng[h:2 * h]]

    def send_whole(l):
        b = ZW + 4 * M * l + M * rank
        vq_, vp_ = V("fq", b, b + M), V("fp", b, b + M)
        r1 = remote([([0, 1, 2], eng, "ac%d" % l, vq_[0].bitcast(dt.uint8), T.fq[:, b:b + M].bitcast(dt.uint8))], [vq_])
        r2 = remote([([0, 1, 2], eng, "as%d" % l, vp_[0], T.fp[:, b:b + M])], [vp_, V("rl", 0, 16)], [r1])
        for nm, sem, r in (("fq", "ac%d" % l, r1), ("fp", "as%d" % l, r2)):
            landed(sem, 3 * len(eng), [V(nm, ZW + 4 * M * l + M * s, ZW + 4 * M * l + M * s + M) for s in peers], [r])
        return r2

    def send_packed(k, sq_, sp_, a):
        prev = []
        for src, dst, sem, en in ((sq_, "bq", "ac%d" % k, first), (sp_, "bp", "as%d" % k, second)):
            trs, rd = [], []
            for e in range(3):
                rd.append(V(src, CAP * e, CAP * e + CAP))
                v, o = rd[-1][0], T[dst][:, a + CAP * slot_at[e]:a + CAP * slot_at[e] + CAP]
                if dst == "bq":
                    v, o = v.bitcast(dt.uint8), o.bitcast(dt.uint8)
                trs.append(([e], en[e], sem, v, o))
            prev = prev + [remote(trs, rd, prev[-1:])]
            landed(sem, len(eng), [V(dst, a, a + NS)], prev)

    last = []
    for gr in range(8):
        o = V("lvn", 0, 30, p=(16 * gr, 16 * gr + 16, 1))
        i_ = dma("ys"[gr % 2], "dlv", o[0], T.lv[:], [], [o])
        if gr % 2 == 0:
            last = [i_]
    last = [dma("y", "dx", T.xs[:], T.x[:], [], [V("xs")], last)]
    fill(V("one"), 1.0)
    fill(V("et"), 0.0)
    iota(V("pid"), [[0, 2]], 0, 1, False)
    o = V("et", 3, 515, 4)
    op("g", lambda: g.affine_select(o[0], T.one[:], [[-1, 128]], EQ, 0.0, 0, 1), [V("one")], [o])
    for b in range(4):
        quant("eq", "es", 128 * b, 128, V("et", 3 - b, 515 - b))
    iota(V("rw"), [[0, C]], 0, 0, False)
    for k, src in ((1, T.pr0), (2, T.pr1)):
        o_ = V("rw", p=(k, 128, 16))
        dma("y", "drw", o_[0], src[:], [], [o_], last)
    fill(V("rl", 0, 16), 0)

    def resets(a, n, k):
        o = V("keep", a, a + n)
        op("g", lambda: g.affine_select(o[0], T.one[:, 0:n], [[0, n // k], [1, k]], NE, 0.0, 0, 0), [V("one")], [o])
    resets(0, 90, 30)
    resets(90, 90, 3)
    resets(180, 60, 10)
    for i, m in enumerate((15, 16, 14, 1, 28, 96)):
        ts(V("pt", i, i + 1), V("pid", 0, 1), m, AND)
    pf = new(6, "col")
    cp(V(pf), V("pt", 0, 6))
    pr_, ph, p14, p1, p28, p96 = [V(pf, i, i + 1) for i in range(6)]
    r5 = ramp([[1, 5]])
    sel = new(5, "col")
    ts(V(sel), V(r5), pr_, EQ)
    sel = [V(sel, i, i + 1) for i in range(5)]
    flip = column(ph, -1.0 / 16, p1, ActivationFunctionType.Abs)
    half = column(p14, 0.5)
    odd = column(ph, 1.0 / 16)

    def offsets(src, c, top, n, o=None):
        o = o or V(new(n, "cu"))
        ts(o, src, c, add, float(top), mn_)
        return o

    r8 = ramp([[8, 2]])
    c_half = V(new(1, "cu"))
    ts(c_half, column(odd, 15.0, pr_), 3.0, mul, 2.0, add)
    c_sig0 = offsets(column(column(odd, -1.0, 6.0), flip, half), 0.0, 10, 1)
    swap = column(flip, 32.0, half)
    c_sig = offsets(V(r8), swap, 63, 2)
    cst = new(3, "col")
    act(V(cst), V(r5, 0, 3), float(M), column(odd, -float(M), -1.0))
    iota(V("rj"), [[16 * 512 + 1, 15], [512 + 30, 16]], -C // 2, 16 * 512 + 1)
    c_m = column(p96, -(16 * 512 + 1.0), -(16 * 512 + 1.0))
    zero("sw", 0, 512)

    def evac(bank0, tile, c, who="svsv", n=M):
        for b in range(4):
            scaled(who[b], V(tile, b, 4 * n, 4), V("ps", 512 * (bank0 + b), 512 * (bank0 + b) + n), c)

    for a in range(0, C, M):
        quant("sq", "ss", a, M, V("xs", 4 * a, 4 * a + 4 * M))
    ind, cum, ib, cb, tot, tr1, pre, pi, pl = [new(n) for n in (90, 90, 90, 90, 80, 32, 32, 90, 96)]
    ex = (tot[0], tot[1] + 32, 33)
    clear(V(tot, 0, 33), "s")
    clear(V(pl, 90, 96), "s")
    tot = (tot[0], tot[1], 32)
    for l in range(3):
        ts(V(ind, 30 * l, 30 * l + 30), V("lvn", 0, 30), l, EQ)
    for l in range(3):
        total_of(V(tot, l, l + 1), V(ind, 30 * l, 30 * l + 30))
    trn(V(tr1), V(tot))
    scan(V(cum), V("keep", 0, 90), V(ind))
    ts(V(ib), V(ind), 1024.0, mul)
    scan(V(ex, 1, 33), V("one", 0, 32), V(tr1))
    tt(V(cb), V(cum), V(ib), add)
    trn(V(pre), V(ex, 0, 32))
    for l in range(3):
        ts(V(pi, l, 90, 3), V(cb, 30 * l, 30 * l + 30), V(pre, l, l + 1), add, V(cst, l, l + 1), add)
    scan(V(pl, 0, 90), V("keep", 90, 180), V(pi), 0.0, mx_)
    place = V(pl, 2, 90, 3)
    hs = new(16, "tu")
    ts(V(hs), V(pl), 16.0 - 1024.0, add, off=c_half)
    tb, tbt = new(32, "th"), new(32, "th")
    clear(V(tb, 30, 32), "s")
    ts(V(tb, 0, 30), place, -1024.0 - (M - 1), add)
    trn(V(tbt), V(tb))
    v = V(tbt, 0, 16, p=(0, 32, 1))
    tdv = [(None, "td", 1, 1 << r, 0) for r in range(4)]
    last = dma("y", "dtd", T.td[rank], v[0], [v], [tdv[rank]])
    last = dma("y", "dw", T.wq[:].bitcast(dt.uint8), T.wc[:], [], [V("wq")], [last])
    last = dma("y", "dw", T.wp[:], T.ws[:], [], [V("wp")], [last])
    r_ = remote([([e], first[e], "atab", T.td[rank], T.td[rank]) for e in range(3)], [tdv[rank]])
    landed("atab", len(eng), [tdv[s] for s in peers], [r_])
    zero("tab", 0, 16, 0.5)
    for s in range(4):
        zero("tab", 16 + C * s, C, float(ZW + M + M * s))
    for gr in range(8):
        o_ = V("tab", 16, 16 + 4 * C, p=(16 * gr, 16 * gr + 1, 1))
        dma("y", "dtab", o_[0], T.td[:, 0:C // 4, :], tdv, [o_])
    sca(V("sw"), V(hs, 0, 15), V("rj"))
    a0, sig, aj, sgm = new(11), new(48, "tu"), new(64), new(32, "tu")
    trn(V("swt", 0, 160), V("sw", 16, 176))
    trn(V("swt", 160, 352), V("sw", 0, 192))
    tt(V(a0), V("swt", 1, 352, 32), V("swt", 16, 352, 32), add)
    ts(V(sig, 0, 16), V(a0), c_m, add, 1.0 / 512, mul, off=c_sig0)

    def layer(lq, lp):
        quant("xq", "xp", 0, M, V("xt"))
        four(4, lq, lp, "xq", "xp", 0, M)

    def close(l):
        evac(4, "tl", 0.03125)
        if l == 2:
            quant("yq", "yp", 2 * M, M, V("tl"))
        else:
            quant("fq", "fp", ZW + 4 * M * l + M * rank, M, V("tl"))

    pick("pq", "pss", 0, "sq", "ss", C, V(sig, 0, 10), M)
    four(0, "eq", "es", "pq", "pss", 0, M)
    evac(0, "xt", 1.0)
    layer("wq", "wp")
    close(0)
    sent0 = send_whole(0)
    clear(V("zt"))
    quant("fq", "fp", 0, ZW, V("zt"))
    quant("bq", "bp", 0, ZW, V("zt"))
    act(V("em", 0, 520), V("et"), column(odd, 0.5, -0.5))
    act(V("em", 520, 1040), V("et"), column(odd, -0.5))
    for par in range(2):
        for b in range(4):
            quant("eq", "es", 512 * (par + 1) + 128 * b, 128, V("em", 520 * par + 3 - b, 520 * par + 515 - b))

    trn(V("swt", 352, 672), V("sw", 176, 496))
    m1, m2 = new(32, "ti"), new(32, "ti")
    clear(V(aj, 10, 32))
    tt(V(aj, 0, 10), V("swt", 353, 672, 32), V("swt", 368, 672, 32), add)
    both(aj)
    ts(V(m1), V(aj), c_m, add, C / 2.0, add, off=c_sig)
    ts(V(m2, 0, 20), V(m1, 0, 20), 511, AND)
    cp(V(sgm, 0, 20), V(m2, 0, 20))
    gs, gst, idx = new(320), new(320), new(40, "tu")
    gat("v", V(gs), V("rw"), V(sgm, 0, 20))
    trn(V(gst), V(gs))
    for l in range(2):
        for k in range(2):
            ts(V(idx, 20 * l + 10 * k, 20 * l + 10 * k + 10), V(gst, M * l + 1 + k, M * l + M, 16), 16.0, add)
    ts(V(sig, 16, 36), V(m1, 0, 20), -(C - 1) / 2.0, add, 1.0 / 512, mul)
    pick("pq", "pss", M, "sq", "ss", C, V(sig, 16, 26), M)
    pick("pq", "pss", 2 * M, "sq", "ss", C, V(sig, 26, 36), M)

    ri = ramp([[32, 5], [0, 2], [1, 16]])
    own_i = column(sel[2], ph)
    cl = column(sel[3], float(Z1), own_i)
    for k in range(2):
        act(V("kp", M * k, M * k + M), V(ri), sel[2], column(sel[4], 2 * M * k - BIG, cl))
    act(V("kp", 2 * M, 4 * M), V("kp", 0, 2 * M), 1.0, column(sel[3], float(Z2 - Z1)))
    r10 = ramp([[22, 2], [10, 2]])
    c_fwd = new(4, "cu")
    offsets(V(r10, 0, 2), column(odd, 20.0, pr_), 41, 2, V(c_fwd, 0, 4, 2))
    offsets(V(r10, 2, 4), column(odd, -22.0, pr_), 41, 2, V(c_fwd, 1, 4, 2))
    fr = [new(64, "tu"), new(64, "tu")]
    for a in (0, 336, 688):
        clear(V("lk", a, a + (32 if a == 336 else 16)))
    for l in range(2):
        a, w0 = 352 * l, 672 * l
        gat("s", V("lk", a + 16, a + 336), V("tab"), V(idx, 20 * l, 20 * l + 20))
        o_, i_ = V("kp", 2 * M * l, 2 * M * l + 2 * M, p=(0, 128, 16)), V("lk", a + 16, a + 336, p=(0, 128, 16))
        dma("y", "dk%d" % l, o_[0], i_[0], [i_], [o_])
        trn(V("lkt", w0, w0 + 320), V("lk", a + 16, a + 336))
        trn(V("lkt", w0 + 320, w0 + 672), V("lk", a, a + 352))
        d1, d2, d3 = new(42), new(42), new(42)
        tt(V(d1), V("lkt", w0, w0 + 672, 16), V("lkt", w0 + 1, w0 + 672, 16), add)
        if l == 1:
            ts(V(d2), V("lkt", w0, w0 + 672, 16), 0.75, GT, float(3 * M), mul)
            tt(V(d3), V(d1), V(d2), add)
            d1 = d3
        ts(V(fr[l]), V(d1), -1.0, add, off=V(c_fwd))

    si, in2, cu2, tb2, tr2, ex2, pr2, p2, pd = new(40, "ti"), new(128, "th"), new(128, "th"), new(32), new(32), new(33), new(32), new(128), new(120)
    r16 = ramp([[16, 8]])
    n16, nd = new(8), new(8, "ti")
    act(V(n16), V(r16), 1.0, pr_)
    ts(V(nd), V(n16), 0.05, mul, -0.475, add)
    c_seg = V(new(8, "cu"))
    ts(c_seg, V(nd), 2.0, mul, p1, add)
    init = column(p28, 16.0, -1.0 - BIG)
    ts(V(si), V(idx), -16.0 - (C - 1) / 2.0, add, 1.0 / C, mul)
    for e in range(3):
        ts(V(in2, 40 * e, 40 * e + 40), V(si), peers[e], EQ)
    clear(V(cu2, 120, 128))
    clear(V(tb2))
    act(V(ex2, 0, 1), init)
    for par in range(2):
        scan(V(cu2, par, 120, 2), V("keep", 180, 240), V(in2, par, 120, 2))
        cp(V(tb2, par, 12, 2), V(cu2, 18 + par, 120, 20))
    trn(V(tr2), V(tb2))
    scan(V(ex2, 1, 33), V("one", 0, 32), V(tr2), init)
    trn(V(pr2), V(ex2, 0, 32))
    ttg(V(p2), V(pr2), c_seg, V(cu2), add)
    tt(V(pd), V(p2, 0, 120), V(in2, 0, 120), mul)
    f1, f2, f3, f4, f5, f6, ow, k2 = new(40), new(40, "ti"), new(40, "ti"), new(40), new(40), new(40), new(40), new(40)
    k1 = ramp([[2 * NS, 2], [0, 10], [16, 2]], int(BIG))
    kk = new(40, "cf")
    for l in range(2):
        iota(V(kk, 20 * l, 20 * l + 20), [[2 * M, 2], [0, 5], [PS, 2]], S0 + M - 1)
    rdm, dm = ramp([[0, 2], [16, 20]], D0), new(40)
    act(V(dm), V(rdm), 1.0, pr_)
    tt(V(f1), V(pd, 0, 40), V(pd, 40, 80), add)
    tt(V(f2), V(f1), V(pd, 80, 120), add)
    ts(V(f3), V(f2), 1008, AND)
    tt(V(f4), V(f2), V(k1), add)
    tt(V(f5), V(f4), V(f3), add)
    tt(V(f6), V(f5), V(dm), mn_)
    ts(V(ow), V(si), rank, NE, BIG, mul)
    tt(V(k2), V(ow), V(kk), add)
    c1, c2, c3 = new(3), new(3), new(3)
    ts(V(c1), V(n16, 0, 3), 20.0, GE, 352.0, mul)
    act(V(c2), V(n16, 0, 3), 16.0, column(flip, 336.0))
    tt(V(c3), V(c1), V(c2), add)
    c_own = offsets(V(c3), 0.0, 1343, 3)
    vo, u3, u4, iof = new(48), new(40), new(40), new(40, "tu")
    gat("v", V(vo), V("lkt"), c_own)
    tt(V(u3), V(vo, 0, 40), V(k2), add)
    tt(V(u4), V(u3), V(f6), mn_)
    cp(V(iof), V(u4))
    for a, n in ((0, 2 * NS), (2 * NS, 2 * NS), (S0, 2 * M), (S0 + 2 * M, 2 * M), (S0 + PS, 2 * M), (S0 + PS + 2 * M, 2 * M)):
        iota(V("ww", a, a + n), [[0, n]], after=[sent0])

    rq, bs = new(32, "tu"), new(24, "tu")
    rqq = new(12, "cf")
    for e in range(3):
        iota(V(rqq, 4 * e, 4 * e + 4), [[16, 4]], CAP * slot_at[e])
    dq = [new(12), new(12)]
    act(V(dq[0]), V(rqq), 1.0, column(pr_, 1.0, 4 * M - (M - 1) - BIG))
    act(V(dq[1]), V(dq[0]), 1.0, column(ph, -PS / 16.0, float(D0 - S0 - 4 * M)))
    at1 = column(ph, PS / 16.0, float(S0))

    def requests(l, after):
        w0 = 2 * NS * l
        for k in range(2):
            sca(V("ww"), V(iof, 20 * l + 10 * k, 20 * l + 10 * k + 10), V("kp", 2 * M * l + M * k, 2 * M * l + M * k + M))
        trn(V("slt", w0, w0 + 2 * NS), V("ww", w0, w0 + 2 * NS))

        def row(k, st=16):
            return V("slt", w0 + k, w0 + 2 * NS, st)
        n1, n4, n5, n6 = new(24), new(12), new(12), new(12)
        tt(V(n6), row(2, 32), row(18, 32), add)
        cp(V(bs, 12 * l, 12 * l + 12), V(n6))
        tt(V(n1), row(0), row(4), add)
        tt(V(n4), V(n1, 0, 24, 2), V(n1, 1, 24, 2), add)
        tt(V(n5), V(n4), V(dq[l]), mn_)
        if l == 1:
            ts(V(rq, 16, 28), V(n5), at1, add, M - 1 + BIG, add)
        else:
            n7, m_ = new(12, "ti"), new(12, "ti")
            ts(V(n7), V(n5), M - 1 + BIG, add)
            ts(V(m_, 0, 3), V(n5, 3, 12, 4), M - 1 + BIG, add, 1024.0, mul)
            ts(V(m_, 4, 7), V(m_, 0, 3), 63 * 1024, AND)
            ts(V(m_, 8, 11), V(m_, 0, 3), 6, SHR, 63 * 1024, AND)
            tt(V(n7, 0, 12, 4), V(n7, 0, 12, 4), V(m_, 4, 7), add)
            tt(V(n7, 1, 12, 4), V(n7, 1, 12, 4), V(m_, 8, 11), add)
            cp(V(rq, 0, 12), V(n7))
        a, k = 16 * l, 3 + l
        r = remote([([e], first[e], "ar%d" % l, V(rq, a + 4 * e, a + 4 * e + k)[0], T.rl[:, a + 4 * slot_at[e]:a + 4 * slot_at[e] + k])
                    for e in range(3)], [V(rq, a, a + 12)], after)
        landed("ar%d" % l, len(eng), [V("rl", a, a + 12)], [r])

    rs, r5k = ramp([[1, NS]]), ramp([[5, 4]])
    c_su = offsets(V(r5k), swap, 63, 4)
    for l, base in ((0, A1), (1, A2)):
        act(V("pb", NS * l, NS * l + NS), V(rs), sel[2], column(sel[3], float(base)))
    br = [new(64, "tu"), new(64, "tu")]

    def successors(l):
        if l == 1:
            for a in (0, 6):
                sca(V("ww"), V("rl", 16 + a, 22 + a), V("pb", NS + 16 * a, NS + 16 * a + 96))
        else:
            u, lo, hi, ao = new(24, "ti"), new(12, "ti"), new(8, "ti"), new(12, "tu")
            cp(V(u, 0, 12), V("rl", 0, 12))
            ts(V(lo), V(u, 0, 12), 1023, AND)
            ts(V(hi, 0, 3), V(u, 0, 12, 4), 10, SHR)
            ts(V(hi, 4, 7), V(u, 1, 12, 4), 4, SHR, 63 * 64, AND)
            tt(V(lo, 3, 12, 4), V(hi, 0, 3), V(hi, 4, 7), add)
            ts(V(ao), V(lo), at1, add)
            for a in (0, 6):
                sca(V("ww"), V(ao, a, a + 6), V("pb", 16 * a, 16 * a + 96))
        w0 = 4 * M * l
        for i in range(4):
            s0 = S0 + PS * (i // 2) + 2 * M * (i % 2) + M * l
            trn(V("sut", w0 + M * i, w0 + M * i + M), V("ww", s0, s0 + M))
        q2, q3 = new(40), new(64)
        clear(V(q3, 20, 32))
        tt(V(q2), V("sut", w0 + 2, w0 + 4 * M, 16), V("sut", w0 + 3, w0 + 4 * M, 16), add)
        tt(V(q3, 0, 20), V(q2, 0, 40, 2), V(q2, 1, 40, 2), add)
        both(q3)
        gat("v", V(br[l]), V(q3), c_su)

    def make(kq, kp_, wq_, wp_, wn, lst, lists, dq_, dp_, da, lq, lp):
        for b in range(4):
            mm(4 + b, "eq", "es", b, dq_, dp_, da, M)
            act(V("dd", M * b, M * b + M), V("ps", 512 * (4 + b), 512 * (4 + b) + M))
        for i in range(4):
            j = lists[i]
            pick(kq, kp_, M * i, wq_, wp_, wn, V(lst, 16 * j, 16 * j + 10), M)
            for b in range(4):
                mm(b, "eq", "es", 4 * (i // 2 + 1) + b, kq, kp_, M * i, M, i == 0, i == 3)
        for b in range(4):
            tt(V("xt", b, 4 * M, 4), V("ps", 512 * b, 512 * b + M), V("dd", M * b, M * b + M), add)
        layer(lq, lp)

    def pack(l, k, sq_, sp_, a, own):
        for b in range(4):
            scaled("svsv"[b], V("tp", M * b, M * b + M), V("ps", 512 * (4 + b), 512 * (4 + b) + M), 0.03125)
        for b in range(4):
            gat("svsv"[b], V("st", b, 4 * NS, 4), V("tp", M * b, M * b + M), V(bs, 12 * l, 12 * l + 12))
        quant(sq_, sp_, 0, NS, V("st"))
        send_packed(k, sq_, sp_, a)
        evac(4, "tl", 0.03125, "ssss")
        quant("bq", "bp", own, M, V("tl"))

    arrived = [V("fp", ZW + M * peers[0], ZW + M * peers[0] + M)]
    dma("y", "dv", T.vq[:].bitcast(dt.uint8), T.vc[:], arrived, [V("vq")])
    dma("y", "dv", T.vp[:], T.vs[:], arrived, [V("vp")])
    dma("y", "du", T.us[:], T.u[:], arrived, [V("us")])
    make("k1q", "k1p", "fq", "fp", ZW + 4 * M, fr[0], (0, 2, 1, 3), "pq", "pss", M, "wq", "wp")
    close(1)
    last = send_whole(1)
    requests(1, [last])
    requests(0, [last])

    quant("uq", "up", 0, 128, V("us"))

    def result(l, a):
        mm(l, "uq", "up", 0, "bq", "bp", a, M)
        act(V("ys", M * l, M * l + M), V("ps", 512 * l, 512 * l + M))

    make("k2q", "k2p", "fq", "fp", ZW + 8 * M, fr[1], (0, 2, 1, 3), "pq", "pss", 2 * M, "wq", "wp")
    close(2)
    four(0, "eq", "es", "yq", "yp", 2 * M, M)
    evac(0, "xt", 1.0)
    layer("vq", "vp")
    pack(1, 2, "scq", "scp", A2, Z2)
    result(2, Z2)

    successors(1)
    make("k3q", "k3p", "bq", "bp", Z1, br[1], (0, 1, 2, 3), "fq", "fp", ZW + 4 * M + M * rank, "vq", "vp")
    pack(0, 3, "sdq", "sdp", A1, Z1)
    result(1, Z1)
    successors(0)
    make("k4q", "k4p", "bq", "bp", Z0, br[0], (0, 1, 2, 3), "fq", "fp", ZW + M * rank, "vq", "vp")
    evac(4, "tl", 0.03125)
    quant("bq", "bp", Z0, M, V("tl"))
    result(0, Z0)

    g1, g2, pij = new(30), new(30), new(30, "tu")
    ts(V(g1), V("lvn", 0, 30), float(Z1 - M - Z0), mul, Z0 - 1024.0, add)
    tt(V(g2), V(g1), place, add)
    cp(V(pij), V(g2))
    plc = new(30, "tu")
    ts(V(plc), place, -1024.0, add)
    for i, (a, n) in enumerate(((0, 256), (256, 224))):
        pick("oq", "op", a, "bq", "bp", Z0 + M, V(pij, a // 16, (a + n) // 16), n, "v")
        dma("y", "dout", T.oc[:, 4 * a:4 * a + 4 * n], T.oq[:, a:a + n].bitcast(dt.uint8), [V("oq", a, a + n)], [])
        gat("s", V("yo", a, a + n), V("ys"), V(plc, a // 16, (a + n) // 16))
        dma("sy"[i], "dout", T.y[:, a:a + n], T.yo[:, a:a + n], [V("yo", a, a + n)], [])
    for k in range(4):
        dma("ys"[k % 2], "dout", T.osc[4 * k:4 * k + 4, :], T.op[32 * k:32 * k + 4, :], [V("op")], [])

    group = {}
    for i, o_ in enumerate(ops):
        if o_["kind"] == "d":
            group.setdefault(o_["sem"], []).append(i)
    for i, o_ in enumerate(ops):
        for j in list(o_["deps"]):
            if ops[j]["kind"] == "d" and j not in o_["soft"]:
                assert ops[j]["sem"] != o_["sem"]
                o_["deps"].update(group[ops[j]["sem"]])
    order = ORDER or list(range(len(ops)))
    assert sorted(order) == list(range(len(ops)))
    total, known, token = {}, {q: {} for q in queues}, {}
    for o_ in ops:
        if o_["kind"] != "c":
            total[o_["sem"]] = total.get(o_["sem"], 0) + o_["n"]

    def need(q, sem, cnt, snap):
        k = known[q]
        if k.get(sem, 0) >= cnt:
            return
        queues[q].wait_ge(T.sem[sem], cnt)
        k[sem] = cnt
        for s_, c_ in snap.items():
            if k.get(s_, 0) < c_:
                k[s_] = c_

    at = {i: k for k, i in enumerate(order)}
    for i in order:
        o_ = ops[i]
        q = o_["q"]
        assert all(at[j] < at[i] for j in o_["deps"])
        if o_["kind"] == "l":
            token[i] = (o_["sem"], o_["n"], {})
            continue
        for j in sorted(o_["deps"], key=lambda j: -at[j]):
            if j not in o_["soft"]:
                need(q, *token[j])
        if o_["kind"] == "c":
            sem = csem[q]
            o_["fn"]().then_inc(T.sem[sem], 1)
            total[sem] = total.get(sem, 0) + 1
            token[i] = (sem, total[sem], dict(known[q]))
        elif o_["kind"] == "d":
            o_["fn"]().then_inc(T.sem[o_["sem"]], 16)
            token[i] = (o_["sem"], total[o_["sem"]], dict(known[q]))
        else:
            o_["fn"]()
    for sem in total:
        need("g", sem, total[sem], {})
